import numpy as np, ml_dtypes
CORES = [25,29,65,69,153,157,193,197]
N = 8
BF = ml_dtypes.bfloat16
S, NM, L, RO, TAU = 1024, 2048, 256, 4, 6
ST, C0, LN = S // L, 16 - RO, NM.bit_length() - 1
def pack(nm, st, kd, ac, fu):
    return np.where(fu, 1 + 2048 * nm + 32 * st + 16 * kd + ac, 0)
def done(e, x, w, kp):
    return {"ent": np.ascontiguousarray(e.reshape(N, 128, S)).astype(np.int32), "feat": np.ascontiguousarray(x.reshape(N, 128, NM)).astype(np.float32).astype(BF),
            "wt": np.ascontiguousarray(w.reshape(N, 128, 1)).astype(np.int32), "kap": np.ascontiguousarray(kp.reshape(N, 128, 1)).astype(np.int32)}
def pooled(rng, n, other):
    pool = rng.integers(0, NM, (8, 16, n)); pool[..., 0] = rng.choice(np.array([0, NM - 1]), (8, 16))
    j = (n * rng.random((N, 8, 16, S)) ** 2).astype(np.int64)
    v = pool[np.arange(8)[:, None, None], np.arange(16)[None, :, None], j]
    return np.where(rng.random(v.shape) < other, rng.integers(0, NM, v.shape), v)
def parts(rng, n, other):
    sh = (N, 8, 16, S); nm = pooled(rng, n, other)
    st = rng.integers(0, 64, sh); kd = (rng.random(sh) < 0.45).astype(np.int64); ac = rng.integers(0, 16, sh); fu = rng.random(sh) < 0.8
    x = (64 * rng.random((N, 8, 16, NM)) ** 2).astype(np.int64)
    return nm, st, kd, ac, fu, x, rng.integers(0, 256, (N, 8, 16)), rng.integers(0, 256, (N, 8, 16))
def setup_inputs(rng):
    nm, st, kd, ac, fu, x, w, kp = parts(rng, 24, 0.3)
    return done(pack(nm, st, kd, ac, fu), x, w, kp)
def setup_inputs_spread(rng):
    sh = (N, 8, 16, S)
    nm = np.exp2(LN * rng.random(sh)).astype(np.int64) - 1; nm = np.where(rng.random((1, 8, 16, 1)) < 0.5, NM - 1 - nm, nm)
    st = np.exp2(6 * rng.random(sh)).astype(np.int64) - 1; st = np.where(rng.random(sh) < 0.5, 63 - st, st)
    kd = (rng.random(sh) < rng.choice(np.array([0.1, 0.4, 0.8]), (N, 8, 1, 1))).astype(np.int64)
    fu = rng.random(sh) < rng.random((N, 8, 1, S))
    x = (np.exp2(6 * rng.random((N, 8, 1, NM))) * rng.random((N, 8, 16, NM))).astype(np.int64)
    w = np.exp2(8 * rng.random((N, 8, 16))).astype(np.int64) - 1; kp = 256 - np.exp2(8 * rng.random((N, 8, 16))).astype(np.int64)
    return done(pack(nm, st, kd, rng.integers(0, 16, sh), fu), x, w, kp)
def at_ends(rng, hi):
    o = np.argsort(rng.random((N, 8, 16)), axis=-1)
    return np.where(o < 11, hi * rng.integers(0, 2, o.shape), rng.integers(0, hi + 1, o.shape))
def setup_inputs_ends(rng):
    sh = (N, 8, 16, S); top = 2048 * NM
    z = 32 * 63 * rng.integers(0, 2, sh) + 15 * rng.integers(0, 2, sh) + 1
    e = np.where(rng.random(sh) < 0.28, 2048 * rng.integers(0, NM, sh) + z, top * rng.integers(0, 2, sh))
    k = rng.random((N, 8, 1, S)); last = 2048 * (NM - 1) + z
    e = np.where(k < 0.41, 16 + z, e); e = np.where(k < 0.37, z, e); e = np.where(k < 0.33, last, e)
    e = np.where(k < 0.26, 0, e); e = np.where(k < 0.16, top, e)
    x = 63 * (rng.random((N, 8, 16, NM)) < 0.2).astype(np.int64); x[..., NM - 1] = 63; x[..., 0] = 0
    w = at_ends(rng, 255); kp = at_ends(rng, 255); w[0, 7] = 255; w[N - 1, 7] = 255
    for c in [0, ST] + list(range(S - ST, S)): e[:, 7, :, c] = last[:, 7, :, c]
    u = 16 * 63 * 255 & 4095
    for m in (8, 15): e[0, 7, :, ((u * u >> 5) + int(kp[N - 1, 7, m]) * u) & (S - 1)] = top
    return done(e, x, w, kp)
def setup_inputs_corners(rng):
    nm, st, kd, ac, fu, x, w, kp = parts(rng, 6, 0.1); sh = kd.shape
    o = rng.permutation(8); md = o[(np.arange(8)[None, :] + (np.arange(N)[:, None] & 1)) & 7]; m4 = md[:, :, None, None]
    kd = np.where(m4 == 0, 1, np.where(m4 == 1, 0, kd)); fu = fu | (m4 == 1)
    fu = np.where(m4 == 2, rng.random((N, 8, 1, S)) < 0.5, fu)
    ac = np.where(m4 == 3, C0 - TAU - 1 + rng.integers(0, RO + 1, sh), ac); kd = np.where(m4 == 3, (rng.random(sh) < 0.7).astype(np.int64), kd)
    st = np.where(m4 == 4, 63 * rng.integers(0, 2, sh), st); st = np.where(m4 == 7, 31, st)
    kd = np.where(m4 == 6, ((np.arange(S)[None, :] & 15) != np.arange(16)[:, None]).astype(np.int64), kd); fu = fu | (m4 == 6)
    x = np.where(m4 == 5, 63, x); m3 = md[:, :, None]
    w = np.where(m3 == 4, 0, np.where(m3 == 7, 255, w)); kp = np.where(m3 == 6, 0, np.where(m3 == 7, 255, kp))
    return done(pack(nm, st, kd, ac, fu), x, w, kp)
def setup_inputs_ties(rng):
    nm, st, kd, ac, fu, x, w, kp = parts(rng, 3, 0.02); sh = st.shape
    st = rng.integers(0, 63, (1, 8, 16, 1)) + rng.integers(0, 2, sh)
    ac = rng.choice(np.array([0, C0 - TAU - 1, C0 - TAU, C0 - TAU + 1, C0, 15]), sh); fu = rng.random(sh) < 0.9
    e = pack(nm, st, kd, ac, fu)
    w[..., 0] |= 1; kp = np.argsort(rng.random((N, 8, 256)), axis=-1)[..., :16]
    nn = rng.integers(0, NM, (N, 8, 16)); c = np.zeros((N, 8, 16), np.int64)
    for r in range(N):
        for g in range(8):
            n = int(nn[r, g, 0])
            if int(np.add.reduce(w[r, g] * x[r, g, :, n])) & 1 == 0: x[r, g, 0, n] ^= 1
            u = int(np.add.reduce(w[r, g] * x[r, g, :, n])) & 4095
            c[r, g] = ((u * u >> 5) + kp[r, g] * u) & (S - 1)
    for r in range(N):
        for g in range(8):
            q = (r + 1) % N; l = min(i for i in range(17) if not np.any(c[r - 1, g] == ST * i))
            s = rng.integers(0, 64, 16); own = pack(nn[r, g], s, (np.arange(16) > 0).astype(np.int64), rng.integers(0, 16, 16), True)
            e[r, g, :, ST * l] = own
            d = rng.integers(1, 4, 16); m = np.sort(rng.permutation(16)[:2]); d[m] = np.array([1, 0]) if (r + g) & 1 else np.array([0, 1])
            miss = np.argsort(rng.random((16, 16)), axis=0) < d[None, :]
            hit = pack(nn[r, g][:, None], s[:, None] ^ rng.integers(1, 64, (16, 16)), rng.integers(0, 2, (16, 16)), rng.integers(0, 16, (16, 16)), True)
            no = np.where(rng.random((16, 16)) < 0.5, 0, (((own - 1) >> 4) << 4)[:, None] + 1 + rng.integers(0, 16, (16, 16)))
            e[q, g][:, c[r, g]] = np.where(miss, no, hit)
    return done(e, x, w, kp)
def gone(v, c):
    return np.where((((37 * c + v) >> 3) & 7) == 0, v ^ 8, v)
def setup_inputs_crowd(rng):
    nm, st, kd, ac, fu, x, w, kp = parts(rng, 8, 0.2)
    e = np.take_along_axis(pack(nm, st, kd, ac, fu), rng.integers(0, 24, (N, 8, 1, S)), 3)
    kp[:, ::2] = kp[:, ::2, :1]
    h = int(rng.integers(0, 8)); kp[:, h] = 0; w[:, h] = 0; w[:, h, 0] = 1; w[:, h, 15] = 64
    cols = ST * np.arange(1, L); sh = (16, L - 1)
    for r in range(N):
        q = (r + 1) % N; o = rng.permutation(4096); c = (o * o >> 5) & (S - 1)
        first = np.unique(c, return_index=True)[1]; first = first[c[first] % ST != 0]
        u = o[rng.permutation(first)[:L - 1]]; p = (u * u >> 5) & (S - 1)
        names = rng.permutation(NM)[:L - 1]; x[r, h, 0, names] = u & 63; x[r, h, 15, names] = u >> 6
        it = rng.random(sh) < 0.4; it[0] = True; it[15] = True
        a = pack(np.where(it, names[None, :], rng.integers(0, NM, sh)), rng.integers(0, 64, sh), 1 - it.astype(np.int64), rng.integers(0, C0 - TAU, sh), True)
        b = pack(gone(rng.integers(0, NM, sh), p[None, :]), rng.integers(0, 64, sh), 1, rng.integers(0, C0 - TAU, sh), True)
        full = rng.random(L - 1) < 0.5; full[-1] = True
        e[r, h][:, cols] = a
        e[q, h][:, p] = np.where(full[None, :], b, a)
    e[:, h, :, 0] = pack(gone(rng.integers(0, NM, 16), 0), rng.integers(0, 64, 16), 1, rng.integers(0, C0 - TAU, 16), True)[None, :]
    return done(e, x, w, kp)
def check_inputs(d):
    bad = []
    for k, lo, hi in (("ent", 0, 2048 * NM), ("feat", 0, 63), ("wt", 0, 255), ("kap", 0, 255)):
        v = np.asarray(d[k]).astype(np.float64)
        if not (np.min(v) >= lo and np.max(v) <= hi): bad.append("range of " + k)
        elif np.any(v != np.floor(v)): bad.append("whole numbers in " + k)
    return bad
def item(a):
    return (a > 0) & ((((a - 1) >> 4) & 1) == 0)
def asleep(a, clock):
    return (a > 0) & ((((a - 1) >> 4) & 1) == 1) & (clock - ((a - 1) & 15) > TAU)
def stay(a, site, clock):
    return np.where(asleep(a, clock) & ((((37 * site + ((a - 1) >> 11)) >> 3) & 7) != 0), 0, a)
def meet(a, b, clock):
    same = (a > 0) & (b > 0) & (((a - 1) >> 11) == ((b - 1) >> 11)); big = np.maximum(a, b)
    wake = same & asleep(big, clock) & item(np.minimum(a, b))
    big = np.where(wake, (((big - 1) >> 4) << 4) + clock + 1, big)
    return np.where(same, big, np.where((a == 0) & ~asleep(b, clock), b, a)), np.where(same, big, np.where((b == 0) & ~asleep(a, clock), a, b))
def reference(ent, feat, wt, kap):
    E = ent.astype(np.int64).reshape(N, 8, 16, S); X = feat.astype(np.float32).astype(np.int64).reshape(N, 8, 16, NM)
    w = wt.astype(np.int64).reshape(N, 8, 16, 1); kp = kap.astype(np.int64).reshape(N, 8, 16, 1); A = [0] * N
    for t in range(RO):
        clock = C0 + t; lane = ST * np.arange(L) + t % ST; new = E.copy(); called = []
        for r in range(N):
            q = (r + 1 + t % (N - 1)) % N
            a = E[r][:, :, lane]
            x = np.take_along_axis(X[r], np.maximum((a - 1) >> 11, 0).reshape(8, 1, 16 * L), 2).reshape(8, 16, 16, L)
            y = np.max(np.where(item(a)[:, None], x, 0), axis=2)
            u = np.add.reduce(w[r] * y, axis=1)[:, None, :] & 4095
            e = ((u * u >> 5) + kp[r] * u + A[r]) & (S - 1)
            cand = np.take_along_axis(E[q], e.reshape(8, 1, 16 * L), 2).reshape(8, 16, 16, L) - 1
            own = a[:, :, None, :] - 1
            score = np.add.reduce((((cand >> 11) == (own >> 11)) & ((cand >> 4) != (own >> 4))).astype(np.int64), axis=1)
            p = np.take_along_axis(e, np.argmax(score, axis=1)[:, None, :], 1)
            win = np.zeros((8, L), bool)
            for g in range(8): win[g, np.unique(p[g, 0], return_index=True)[1]] = True
            b = np.take_along_axis(E[q], p, 2)
            na, nb = meet(stay(a, lane[None, None, :], clock), stay(b, p, clock), clock)
            new[r][:, :, lane] = np.where(win[:, None, :], na, a)
            called.append((q, p[:, 0], win, nb)); A[r] = int(np.count_nonzero(win)) & 31
        for q, p, win, nb in called:
            for g in range(8): new[q, g][:, p[g, win[g]]] = nb[g][:, win[g]]
        E = new
    return {"yent": E.reshape(N, 128, S).astype(np.float32)}

@@ -1,0 +1,560 @@
+from concourse.mybir import AluOpType as ALU, ActivationFunctionType as AF
+
+NR = 4
+EMP = 4096.0 * 2050
+P23, P24 = float(1 << 23), float(1 << 24)
+GS = 5
+SQ = 6
+LAT = {"a": 5.0, "u": 4.5, "c": 4.5, "n": 5.0}
+WAKE = 0.1
+SLACK = 0.03
+PIECES = 2
+
+SCRATCH = {}
+
+
+def _sb(dtype, **cols):
+    for n in cols:
+        SCRATCH[n] = ("sbuf", [128, cols[n]], dtype)
+
+
+_sb("int32", entx=1024, R=1280, wti=1, kpi=1, ci=1024, ci2=1024, pmi=16, pmj=16, xv=256, xh=256)
+_sb("bfloat16", fx=2064, one=128, blka=128, blk=128, blkb=128, zer=256, sel=2048, wsel=2048, tri=2048, dlt=256, rA=256, rK=256, sgm=512)
+_sb("float32", wtf=1, iot=1024, Ct0=1024, Ct1=1024, Ct2=1024, Ct3=1024, allf=128, pmf=16, x16=16, cmk=16, c15=1, mio=256, lio=512,
+    lbl=256, dma_=256, DM=256, KM=256, kcol=1, xs=256)
+_sb("uint16", lst=16, off=256, eu=256, e16=16, ebc=256, pos=16)
+_sb("int32", k1=256, ui=16, ub=16, uq=16, us=16, ei=256, em=256, oc=512, ky=16, kk=16, es=16, er=16, ti=1)
+_sb("float32", pr=256, acol=1, ep=256, D=4096, mx=64, m2=32, ku=16, erf=16, wacc=1, px=256, ps=256, pf=16)
+_sb("bfloat16", Yg=4096, Ys=4096, X=4096, Y=4096, NM=4096, EQ=4096)
+_sb("int32", qa=256, za=256, l5a=256, ita=256, bI=256, qb=256, zb=256, l5b=256, itb=256, hi=256)
+_sb("float32", aw=256, aP=256, zda=256, zdb=256, ca=256, bs=256, wbx=256, pb=256, rr=256, Xd=256, na1=256, nb1=256, na3=256, nbA=256,
+    a1=256, nb=256, yo=1024, xo=256)
+for _n in ("pk0", "pk1", "pu", "pc", "pm", "t1", "t2", "t3"):
+    SCRATCH[_n] = ("psum", [128, 512], "float32")
+STEP = {"a": 264, "u": 32, "c": 4, "n": 256}
+PART = {}
+MSG = {"a": (258, "int32"), "u": (32, "float32"), "c": (1, "int32"), "n": (256, "int32")}
+SEMAPHORES = ["qv", "qs", "qp", "qg", "ld0", "ld1", "ld2", "ld3", "oc0", "oc1", "oc2", "oc3", "st", "lsem"]
+for _t in range(NR):
+    for _m in MSG:
+        if _m == "c" and _t == NR - 1:
+            continue
+        for _s in "sl":
+            SCRATCH[_s + _m] = ("sbuf", [128, NR * STEP[_m]], MSG[_m][1])
+            PART["%s%s%d" % (_s, _m, _t)] = (_s + _m, _t * STEP[_m], MSG[_m][0])
+        SEMAPHORES.append("%s%d" % (_m, _t))
+for _n, _b, _c in (("v1", "t1", 0), ("v2", "t1", 256), ("v3", "t2", 0), ("v4", "t2", 256), ("v5", "t3", 0), ("v6", "t3", 256),
+                   ("cbp", "pk0", 0), ("dbp", "pk0", 256), ("dap", "pm", 256), ("nsp", "pk1", 0), ("wnp", "pk1", 256), ("bPp", "pm", 0), ("dp", "pu", 256), ("ctl", "pc", 256)):
+    PART[_n] = (_b, _c, 256)
+
+
+def bits(m):
+    return bin(m).count("1")
+
+
+def relays(topo, T, src, dst):
+    return [c for c in topo.cores_of(src) if topo.may_write(c, dst) and topo.die(c) == topo.die(src) and T.rank_of(c) is None]
+
+
+def route(topo, T, src, dst, m, t):
+    w = MSG[m][0]
+    if topo.may_write(src, dst):
+        return [(None, 0, w)]
+    rl = relays(topo, T, src, dst)
+    if w < 64:
+        return [(rl[1 if m == "u" else 0], 0, w)]
+    return [(rl[0], 0, 128), (rl[1], 128, w)]
+
+
+def target(T, rank, m, t):
+    n = len(T.cores)
+    s = 1 + t % (n - 1)
+    return (rank + s) % n if m in "au" else (rank - s) % n
+
+
+def source(T, rank, m, t):
+    n = len(T.cores)
+    s = 1 + t % (n - 1)
+    return (rank - s) % n if m in "au" else (rank + s) % n
+
+
+def hand_on(g, core, T, topo):
+    sent = 0
+    mine = [r for r, c in enumerate(T.cores) if c in topo.cores_of(core)]
+    if not mine:
+        return
+    for m, t in plan(T)[2]:
+        for r in mine:
+            src, dst = T.cores[r], T.cores[target(T, r, m, t)]
+            for rl, lo, hi in route(topo, T, src, dst, m, t):
+                if rl != core:
+                    continue
+                b, at = T["l" + m], STEP[m] * t
+                sem = T.sem["%s%d" % (m, t)]
+                g.wait_ge(sem, bits(topo.mask(src, core)))
+                rid, pid = topo.addr(dst, core)
+                mk = topo.mask(core, dst)
+                g.remote_dma(b[:, at + lo:at + hi], b[:, at + lo:at + hi], sem, T.sem.lsem, pid, rid, mk)
+                sent += bits(mk)
+    if sent:
+        g.wait_ge(T.sem.lsem, sent)
+
+
+def B(name, lo=0, hi=None, st=1):
+    if name in PART:
+        b, at, w = PART[name]
+        return (b, at + lo, at + (w if hi is None else hi), st)
+    return (name, lo, SCRATCH[name][1][1] if hi is None else hi, st)
+
+
+def width(x):
+    return (x[2] - x[1] + x[3] - 1) // x[3]
+
+
+def meets(a, b):
+    if a[2] <= b[1] or b[2] <= a[1]:
+        return False
+    return not (a[3] == b[3] and a[3] > 1 and (a[1] - b[1]) % a[3])
+
+
+def covers(a, b):
+    return a[1] <= b[1] and b[2] <= a[2] and (a[3] == 1 or (a[3] == b[3] and (a[1] - b[1]) % a[3] == 0))
+
+
+def links(ops):
+    acc, out = {}, []
+    for i, o in enumerate(ops):
+        pre = set(o["after"])
+        for wr, lst in ((False, o["r"]), (True, o["w"])):
+            for x in lst:
+                ps = SCRATCH[x[0]][0] == "psum"
+                for (y, w2, j) in acc.get(x[0], []):
+                    if j == i:
+                        continue
+                    if ps and (ops[j]["q"] != o["q"] or o["q"] == "p"):
+                        pre.add(j)
+                    elif (wr or w2) and meets(x, y):
+                        pre.add(j)
+        for x in o["w"]:
+            acc[x[0]] = [a for a in acc.get(x[0], []) if a[2] == i or not covers(x, a[0]) or (SCRATCH[x[0]][0] == "psum" and ops[a[2]]["q"] != o["q"])]
+            acc[x[0]].append((x, True, i))
+        for x in o["r"]:
+            acc.setdefault(x[0], []).append((x, False, i))
+        out.append(sorted(pre))
+    return out
+
+
+def arrange(ops, pre, wake):
+    n = len(ops)
+    suc = [[] for _ in range(n)]
+    for i in range(n):
+        for j in pre[i]:
+            suc[j].append(i)
+    prio = [0.0] * n
+    for i in range(n - 1, -1, -1):
+        prio[i] = ops[i]["dur"] + (0.0 if ops[i]["q"] == "p" else wake) + max([prio[k] for k in suc[i]] + [0.0])
+    left = [len(p) for p in pre]
+    est = [0.0] * n
+    ready = [i for i in range(n) if left[i] == 0]
+    free, seq = {}, []
+    while ready:
+        st = {i: max(free.get(ops[i]["q"], 0.0), est[i]) for i in ready}
+        first = min(ready, key=lambda i: (st[i], -prio[i]))
+        q, lim = ops[first]["q"], st[first] + SLACK
+        i = max([k for k in ready if ops[k]["q"] == q and st[k] <= lim], key=lambda k: (prio[k], -k))
+        if q is None:
+            i = first
+        ready.remove(i)
+        seq.append(i)
+        end = st[i] + ops[i]["dur"]
+        if q is not None:
+            free[q] = st[i] + 0.06 if ops[i]["kind"] == "dma" else end
+        for k in suc[i]:
+            est[k] = max(est[k], end if q == "p" and ops[k]["q"] == "p" else end + wake)
+            left[k] -= 1
+            if left[k] == 0:
+                ready.append(k)
+    return seq
+
+
+def record(T):
+    ops, where = [], {}
+    CY, G, SC = 0.001, 1.5, 3.0
+
+    def put(kind, q, fn, r, w, dur, after=(), **more):
+        d = {"kind": kind, "q": q, "fn": fn, "r": list(r), "w": list(w), "dur": dur, "after": list(after)}
+        d.update(more)
+        ops.append(d)
+
+    def ap(x):
+        name, lo, hi, st = x
+        return T[name][:, lo:hi:st] if st != 1 else T[name][:, lo:hi]
+
+    def two(*xs):
+        return 0.5 if all(SCRATCH[x[0]][2] in ("bfloat16", "uint16") for x in xs) else 1.0
+
+    def vd(n, k=1.0):
+        return max(64.0, n * k) * CY
+
+    def ts(o, a, s1, op0, s2=None, op1=None, sc=None):
+        d = vd(width(a), two(o, a))
+        r = [a] if sc is None else [a, sc]
+        if op1 is None:
+            put("run", "v", lambda e: e.tensor_scalar(ap(o), ap(a), s1 if sc is None else ap(sc), None, op0), r, [o], d)
+        else:
+            put("run", "v", lambda e: e.tensor_scalar(ap(o), ap(a), s1 if sc is None else ap(sc), s2, op0, op1), r, [o], d)
+
+    def tt(o, a, b, op):
+        k = 1.0 if "psum" in (SCRATCH[a[0]][0], SCRATCH[b[0]][0]) else 2.0
+        put("run", "v", lambda e: e.tensor_tensor(ap(o), ap(a), ap(b), op), [a, b], [o], vd(width(a), k))
+
+    def cp(o, a):
+        put("run", "v", lambda e: e.tensor_copy(ap(o), ap(a)), [a], [o], vd(width(a), two(o, a)))
+
+    def ms(o, c):
+        put("run", "v", lambda e: e.memset(ap(o), c), [], [o], vd(width(o), two(o)))
+
+    def pick(o, win, off, b=None, op=None):
+        r, d = [win, off] + ([b] if b is not None else []), 0.06 + 16 * width(off) * G * CY
+        if b is None:
+            put("run", "v", lambda e: e.tensor_copy(ap(o), ap(win).indirect(ap(off))), r, [o], d)
+        else:
+            put("run", "v", lambda e: e.tensor_tensor(ap(o), ap(win).indirect(ap(off)), ap(b), op), r, [o], d)
+
+    def scatter(win, off, a):
+        put("run", "v", lambda e: e.tensor_copy(ap(win).indirect(ap(off)), ap(a)), [a, off], [win], 0.06 + width(a) * SC * CY)
+
+    def scan(o, m, a):
+        put("run", "v", lambda e: e.tensor_tensor_scan(ap(o), ap(m), ap(a), 0.0, ALU.mult, ALU.max), [m, a], [o], vd(width(a), two(o, m, a)))
+
+    def act(o, a, f, bias=0.0, scale=1.0, accum=None, sc=None):
+        d = vd(width(a))
+        r = [a] if sc is None else [a, sc]
+        if accum is not None:
+            put("run", "s", lambda e: e.activation(ap(o), ap(a), f, bias=bias, scale=scale, accum_out=ap(accum)), r, [o, accum], d)
+        else:
+            put("run", "s", lambda e: e.activation(ap(o), ap(a), f, bias=bias, scale=scale if sc is None else ap(sc)), r, [o], d)
+
+    def apick(o, win, off):
+        put("run", "s", lambda e: e.activation(ap(o), ap(win).indirect(ap(off)), AF.Copy), [win, off], [o], 0.08 + 16 * width(off) * G * CY)
+
+    def mm(o, l, r, st, sp):
+        put("run", "p", lambda e: e.matmul(ap(o), ap(l), ap(r), st, sp), [l, r], [o], vd(width(r), 0.9))
+
+    def iota(o, pat, base, cm):
+        d = 0.16 + 2 * width(o) * CY
+        if SCRATCH[o[0]][2] != "int32":
+            put("run", "g", lambda e: e.iota(ap(o), pat, base, cm, allow_small_or_imprecise_dtypes=True), [], [o], d)
+        else:
+            put("run", "g", lambda e: e.iota(ap(o), pat, base, cm), [], [o], d)
+
+    def sift(o, a, pat, op, fill, base, cm):
+        put("run", "g", lambda e: e.affine_select(ap(o), ap(a), pat, op, fill, base, cm), [a], [o], 0.2 + 2 * width(o) * CY)
+
+    def load(q, o, a, sem, dur):
+        put("dma", q, lambda e: e.dma_start(ap(o), T[a][:]), [], [o], dur, sem=sem)
+
+    def send(m, t):
+        where[(m, t)] = len(ops)
+        put("send", "g", None, [B("s%s%d" % (m, t))], [], 0.8, msg=(m, t))
+
+    def expect(m, t):
+        put("land", None, None, [], [B("l%s%d" % (m, t))], LAT[m], [where[(m, t)]], msg=(m, t))
+
+    load("y", B("entx"), "ent", "ld0", 4.5)
+    ms(B("fx", 0, 16), 0.0)
+    load("s", B("wti"), "wt", "ld1", 2.2)
+    load("s", B("kpi"), "kap", "ld2", 2.2)
+    load("y", B("fx", 1, 2049), "feat", "ld3", 6.0)
+    ms(B("one"), 1.0)
+    sift(B("blka"), B("one"), [[-16, 8], [0, 16]], ALU.is_ge, 0.0, 0, 1)
+    sift(B("blk"), B("blka"), [[16, 8], [0, 16]], ALU.is_ge, 0.0, 15, -1)
+    iota(B("pmi"), [[0, 16]], 0, 1)
+    iota(B("lio"), [[0, 32], [1, 16]], 0, 0)
+    iota(B("x16"), [[1, 16]], 0, 0)
+    iota(B("mio"), [[1, 16], [0, 16]], 0, 0)
+    iota(B("lbl"), [[1, 256]], 1024, 0)
+    iota(B("ci"), [[37, 1024]], -1, 0)
+    iota(B("iot"), [[1, 1024]], 0, 0)
+    ms(B("wsel"), 0.0)
+    ms(B("sel"), 0.0)
+    ms(B("zer"), 0.0)
+    ms(B("allf"), 2.0 ** -28)
+    ts(B("sgm"), B("lio"), 1.0, ALU.min)
+    ts(B("pmj"), B("pmi"), 15, ALU.bitwise_and)
+    cp(B("pmf"), B("pmj"))
+    cp(B("wtf"), B("wti"))
+    for t in range(NR):
+        cp(B("sa%d" % t, 256, 257), B("kpi"))
+        cp(B("sa%d" % t, 257, 258), B("kpi"))
+    for p in range(16):
+        act(B("wsel", 129 * p, 129 * p + 113, 16), B("blk", 0, 113, 16), AF.Copy, sc=B("wtf"))
+    act(B("blkb"), B("blk"), AF.Copy, scale=P24)
+    for p in range(16):
+        act(B("sel", 129 * p, 129 * p + 113, 16), B("blk", 0, 113, 16), AF.Copy, scale=-4096.0)
+    ts(B("cmk"), B("x16"), None, ALU.is_gt, P24, ALU.mult, sc=B("pmf", 0, 1))
+    for x in range(16):
+        act(B("tri", 128 * x, 128 * x + 128), B("blk"), AF.Copy, sc=B("cmk", x, x + 1))
+    ts(B("dlt"), B("mio"), None, ALU.is_equal, sc=B("pmf", 0, 1))
+    ts(B("c15"), B("pmf", 0, 1), -256.0, ALU.mult, 3840.0, ALU.add)
+    ts(B("rA"), B("dlt"), None, ALU.mult, sc=B("c15"))
+    ts(B("dma_"), B("lio", 0, 256), None, ALU.is_equal, sc=B("pmf", 0, 1))
+    tt(B("DM"), B("dma_"), B("lbl"), ALU.mult)
+    cp(B("lst"), B("pmj"))
+    ts(B("ci2"), B("ci"), 63, ALU.bitwise_and)
+    ts(B("Ct0"), B("ci2"), 4096.0, ALU.mult, 22.0, ALU.add)
+    for t in range(1, NR):
+        act(B("Ct%d" % t), B("Ct0"), AF.Identity, bias=float(t))
+
+    def lanes(c):
+        return ("R", c, 1021 + c, 4)
+
+    def convert(c):
+        x = B("entx", c, 1021 + c, 4)
+        v, w = ("v1", "v3") if c % 2 else ("v2", "v5")
+        ts(B("xv"), x, 2047.0, ALU.add)
+        ts(B("xh"), B("xv"), -2048, ALU.bitwise_and)
+        ts(B(v), B("xh"), 3.0, ALU.mult)
+        tt(B("xs"), B(v), x, ALU.subtract)
+        ts(B(w), B("xs"), 0.0, ALU.is_equal, EMP, ALU.mult)
+        tt(lanes(c), B(w), B("xs"), ALU.max)
+
+    def own(t):
+        expect("n", t)
+        ts(B("v1"), lanes(t), 0.0, ALU.is_equal, P24, ALU.mult)
+        tt(B("v3"), B("v1"), B("ln%d" % t), ALU.min)
+        tt(lanes(t), B("v3"), lanes(t), ALU.max)
+
+    convert(0)
+    FX = B("fx", 0, 2049)
+    RT = B("R", 0, 1024)
+    for t in range(NR):
+        sa, la, su, lu = "sa%d" % t, "la%d" % t, "su%d" % t, "lu%d" % t
+        Ct = B("Ct%d" % t)
+        cp(B(sa, 0, 256), lanes(t))
+        send("a", t)
+        for h in range(2):
+            lo, hi = 128 * h, 128 * h + 128
+            x = ("R", 4 * lo + t, 4 * hi - 3 + t, 4)
+            ts(B("k1", lo, hi), x, 16, ALU.bitwise_and)
+            tt(B("pr", lo, hi), x, B("k1", lo, hi), ALU.mult)
+            ts(B("off", lo, hi), B("pr", lo, hi), 2.0 ** -16, ALU.mult)
+        for c in range(8):
+            (apick if c < GS else pick)(B("Yg", 512 * c, 512 * c + 512), FX, B("off", 32 * c, 32 * c + 32))
+        for c in range(8):
+            scan(B("Ys", 512 * c, 512 * c + 512), B("sgm"), B("Yg", 512 * c, 512 * c + 512))
+        for p in range(16):
+            mm(B("pu", 0, 16), B("wsel", 128 * p, 128 * p + 128), B("Ys", 16 * p + 15, 4096, 256), p == 0, p == 15)
+        cp(B("ui"), B("pu", 0, 16))
+        ts(B("ub"), B("ui"), 4095, ALU.bitwise_and)
+        tt(B("uq"), B("ub"), B("ub"), ALU.mult)
+        cp(B(su, 0, 16), B("ub"))
+        ts(B("us"), B("uq"), 5, ALU.arith_shift_right)
+        if t == 0:
+            cp(B(su, 16, 32), B("us"))
+        else:
+            expect("c", t - 1)
+            cp(B("acol"), B("lc%d" % (t - 1)))
+            ts(B(su, 16, 32), B("us"), None, ALU.add, sc=B("acol"))
+        send("u", t)
+        if t == 0:
+            for c in range(1, 4):
+                convert(c)
+        else:
+            own(t - 1)
+        expect("a", t)
+        A = B(la, 0, 256)
+        ts(B("oc", 0, 256), A, -16, ALU.bitwise_and)
+        put("dma", "y", lambda e: e.dma_start(T.oc[:, 256:512], T.oc[:, 0:256]), [B("oc", 0, 256)], [B("oc", 256, 512)], 2.2, sem="oc%d" % t)
+        cp(B("kcol"), B(la, 256, 257))
+        ts(B("rK"), B("dlt"), None, ALU.mult, sc=B("kcol"))
+        mm(B("pm", 0, 256), B("blk"), B("rK"), True, True)
+        act(B("KM"), B("pm", 0, 256), AF.Copy)
+        act(B("ctl"), ("Ct%d" % t, t, 1021 + t, 4), AF.Copy)
+        tt(B("qa"), B("ctl"), A, ALU.add)
+        ts(B("za"), B("qa"), 0x3801F, ALU.bitwise_and)
+        ts(B("l5a"), B("qa"), 31, ALU.bitwise_and)
+        ts(B("v5"), B("l5a"), float(5 + t), ALU.is_le, EMP, ALU.mult)
+        ts(B("v6"), B("za"), float(5 + t), ALU.is_gt, P24, ALU.mult)
+        tt(B("aw"), B("v5"), A, ALU.max)
+        tt(B("v4"), B("v6"), A, ALU.add)
+        tt(B("aP"), B("v4"), B("aw"), ALU.min)
+        tt(B("zda"), B("v6"), B("za"), ALU.subtract)
+        act(B("dap"), B("zda"), AF.Relu, bias=7.0 / 16, scale=-1.0 / 16)
+        act(B("ca"), B("aP"), AF.Identity, bias=EMP * 2048.0, scale=-2048.0)
+        ts(B("ita"), A, 16, ALU.bitwise_and)
+        expect("u", t)
+        u, s = B(lu, 0, 16), B(lu, 16, 32)
+        for h in range(PIECES):
+            lo, hi = 256 * h // PIECES, 256 * (h + 1) // PIECES
+            pick(B("ep", lo, hi), u, B("lst", lo // 16, hi // 16), B("KM", lo, hi), ALU.mult)
+            pick(B("ei", lo, hi), s, B("lst", lo // 16, hi // 16), B("ep", lo, hi), ALU.add)
+            ts(B("em", lo, hi), B("ei", lo, hi), 1023, ALU.bitwise_and)
+            cp(B("eu", lo, hi), B("em", lo, hi))
+
+        def ch(n, c):
+            return B(n, 512 * c, 512 * c + 512)
+        for c in range(8):
+            pick(ch("D", c), RT, B("eu", 32 * c, 32 * c + 32), B("oc"), ALU.subtract)
+            act(ch("X", c), ch("D", c), AF.Abs, bias=-7.5)
+            ts(ch("Y", c), ch("X", c), 3000.0, ALU.min, 262144.0 + 1016.0, ALU.add)
+            if c < SQ:
+                act(ch("NM", c), ch("Y", c), AF.Square, bias=-129.0, scale=2.0 ** -11)
+            else:
+                ts(ch("NM", c), ch("Y", c), 262144.0 + 2048.0, ALU.not_equal)
+        for c in range(4):
+            o = B("pk%d" % (c % 2), 0, 64)
+            mm(o, B("blk"), B("rA", 64 * c, 64 * c + 64), True, False)
+            mm(o, B("blk"), B("rK", 64 * c, 64 * c + 64), False, False)
+            for p in range(16):
+                mm(o, B("sel", 128 * p, 128 * p + 128), B("NM", 1024 * c + p, 1024 * c + 1024, 16), False, p == 15)
+            if c == 0:
+                cp(B("mx"), o)
+            else:
+                tt(B("mx"), o, B("mx"), ALU.max)
+        tt(B("m2"), B("mx", 0, 32), B("mx", 32, 64), ALU.max)
+        tt(B("ky"), B("m2", 0, 16), B("m2", 16, 32), ALU.max)
+        ts(B("kk"), B("ky"), 255, ALU.bitwise_and)
+        tt(B("ku"), u, B("kk"), ALU.mult)
+        tt(B("es"), s, B("ku"), ALU.add)
+        ts(B("er"), B("es"), 1023, ALU.bitwise_and)
+        cp(B("e16"), B("er"))
+        cp(B("erf"), B("er"))
+        pc = B("pc", 0, 256)
+        pick(B("ebc"), B("iot"), B("e16"))
+        mm(pc, B("zer", 0, 128), B("zer"), True, False)
+        for k in range(16):
+            ts(B("EQ", 256 * k, 240 * k + 256), B("ebc", 16 * k, 256), None, ALU.is_equal, sc=B("erf", k, k + 1))
+            if k < 15:
+                mm(B("pc", 16 * k + 16, 256), B("blkb"), B("EQ", 256 * k + 16, 240 * k + 256), False, False)
+        for x in range(16):
+            mm(B("pc", x, 241 + x, 16), B("tri", 128 * x, 128 * x + 128), B("EQ", x, 3841 + x, 256), False, x == 15)
+        act(B("wnp"), pc, AF.Relu, bias=P24, scale=-1.0, accum=B("wacc"))
+        if t < NR - 1:
+            mm(B("pu", 32, 33), B("allf"), B("wacc"), True, True)
+            cp(B("ti"), B("pu", 32, 33))
+            ts(B("sc%d" % t), B("ti"), 31, ALU.bitwise_and)
+            send("c", t)
+        pick(B("bI"), RT, B("e16"))
+        pick(B("qb"), Ct, B("e16"), B("bI"), ALU.add)
+        ts(B("zb"), B("qb"), 0x3801F, ALU.bitwise_and)
+        ts(B("l5b"), B("qb"), 31, ALU.bitwise_and)
+        ts(B("v1"), B("l5b"), float(5 + t), ALU.is_le, EMP, ALU.mult)
+        ts(B("v3"), B("zb"), float(5 + t), ALU.is_gt, P24, ALU.mult)
+        tt(B("v2"), B("v1"), B("bI"), ALU.max)
+        tt(B("bs"), B("v3"), B("bI"), ALU.add)
+        tt(B("bPp"), B("v2"), B("bs"), ALU.min)
+        tt(B("dp"), B("bPp"), B("aP"), ALU.subtract)
+        act(B("Xd"), B("dp"), AF.Abs)
+        act(B("nsp"), B("Xd"), AF.Relu, bias=-2047.5 * P24, scale=P24)
+        act(B("cbp"), B("bPp"), AF.Identity, bias=EMP * 2048.0, scale=-2048.0)
+        ts(B("itb"), B("bI"), 16, ALU.bitwise_and)
+        tt(B("zdb"), B("v3"), B("zb"), ALU.subtract)
+        act(B("dbp"), B("zdb"), AF.Relu, bias=7.0 / 16, scale=-1.0 / 16)
+        tt(B("pb"), B("dbp"), B("ita"), ALU.mult)
+        tt(B("wbx"), B("bPp"), B("pb"), ALU.subtract)
+        tt(B("v5"), B("dap"), B("itb"), ALU.mult)
+        tt(B("v4"), B("aP"), B("v5"), ALU.subtract)
+        tt(B("rr"), B("v4"), B("wbx"), ALU.min)
+        tt(B("na1"), B("v2"), B("ca"), ALU.add)
+        tt(B("nb1"), B("cbp"), B("aw"), ALU.add)
+        tt(B("a1"), B("wnp"), A, ALU.max)
+        tt(B("v6"), B("nsp"), B("rr"), ALU.add)
+        tt(B("nbA"), B("v6"), B("nb1"), ALU.min)
+        tt(B("nb"), B("bPp"), B("nbA"), ALU.min)
+        tt(B("v5"), B("v6"), B("aP"), ALU.min)
+        tt(B("na3"), B("v5"), B("na1"), ALU.min)
+        tt(B("v2"), pc, B("na3"), ALU.max)
+        tt(B("sn%d" % t), B("v2"), B("a1"), ALU.min)
+        send("n", t)
+        tt(B("px"), pc, B("DM"), ALU.min)
+        scan(B("ps"), B("sgm", 0, 256), B("px"))
+        tt(B("pf"), B("erf"), B("ps", 15, 256, 16), ALU.max)
+        cp(B("pos"), B("pf"))
+        iota(lanes(t), [[0, 256]], 0, 0)
+        scatter(B("R"), B("pos"), B("nb"))
+
+    def decode(c):
+        r = lanes(c)
+        v, w = ("v1", "v3") if c % 2 else ("v5", "v6")
+        ts(B("hi"), r, -4096, ALU.bitwise_and)
+        ts(B(w), r, EMP, ALU.is_lt)
+        ts(B(v), B("hi"), 1.5, ALU.mult)
+        tt(B("xo"), B(v), r, ALU.subtract)
+        tt(B("yo", c, 1021 + c, 4), B(w), B("xo"), ALU.mult)
+    last = (NR - 1) % 4
+    for c in range(4):
+        if c != last:
+            decode(c)
+    own(NR - 1)
+    decode(last)
+    put("dma", "y", lambda e: e.dma_start(T.yent[:], T.yo[:]), [B("yo")], [], 4.5, sem="st")
+    return ops
+
+
+ORDER = {}
+
+
+def plan(T):
+    if "o" not in ORDER:
+        ops = record(T)
+        pre = links(ops)
+        seq = arrange(ops, pre, WAKE)
+        ORDER["o"] = (pre, seq, [ops[i]["msg"] for i in seq if ops[i]["kind"] == "send"])
+    return ORDER["o"]
+
+
+def rank_program(g, core, T, topo):
+    rank = T.rank_of(core)
+    if rank is None:
+        hand_on(g, core, T, topo)
+        return
+    ops = record(T)
+    pre, seq, _ = plan(T)
+    eng = {"v": g.vector, "s": g.scalar, "p": g.tensor, "g": g, "y": g.sync}
+    cnt = {"v": 0, "s": 0, "p": 0, "g": 0}
+    known, snaps, tok, sent = {q: {} for q in eng}, {}, {}, 0
+    for i in seq:
+        o = ops[i]
+        q = o["q"]
+        if o["kind"] == "land":
+            m, t = o["msg"]
+            src = T.cores[source(T, rank, m, t)]
+            n = 0
+            for rl, lo, hi in route(topo, T, src, core, m, t):
+                n += bits(topo.mask(src if rl is None else rl, core))
+            tok[i] = ("%s%d" % (m, t), n)
+            continue
+        need = {}
+        for j in pre[i]:
+            if ops[j]["kind"] != "send" and not (q == "p" and ops[j]["q"] == "p"):
+                need[tok[j][0]] = max(need.get(tok[j][0], 0), tok[j][1])
+        for s in sorted(need):
+            if known[q].get(s, 0) < need[s]:
+                eng[q].wait_ge(T.sem[s], need[s])
+                known[q][s] = need[s]
+                for s2, v2 in snaps.get((s, need[s]), {}).items():
+                    known[q][s2] = max(known[q].get(s2, 0), v2)
+        if o["kind"] == "run":
+            cnt[q] += 1
+            tok[i] = ("q" + q, cnt[q])
+            o["fn"](eng[q]).then_inc(T.sem["q" + q], 1)
+        elif o["kind"] == "dma":
+            tok[i] = (o["sem"], 16)
+            o["fn"](eng[q]).then_inc(T.sem[o["sem"]], 16)
+        else:
+            m, t = o["msg"]
+            dst = T.cores[target(T, rank, m, t)]
+            s, l, at = T["s" + m], T["l" + m], STEP[m] * t
+            for rl, lo, hi in route(topo, T, core, dst, m, t):
+                to = dst if rl is None else rl
+                rid, pid = topo.addr(to, core)
+                mk = topo.mask(core, to)
+                g.remote_dma(l[:, at + lo:at + hi], s[:, at + lo:at + hi], T.sem["%s%d" % (m, t)], T.sem.lsem, pid, rid, mk)
+                sent += bits(mk)
+            continue
+        snaps[tok[i]] = dict(known[q])
+    g.wait_ge(T.sem.st, 16)
+    g.wait_ge(T.sem.lsem, sent)
+    for q in "vspg":
+        g.wait_ge(T.sem["q" + q], cnt[q])

@@ -1,110 +1,150 @@
 from concourse.mybir import AluOpType as ALU, ActivationFunctionType as AF
 
 NR = 4
-EMP = 4096.0 * 2050
-P23, P24 = float(1 << 23), float(1 << 24)
-GS = 5
-SQ = 6
-LAT = {"a": 5.0, "u": 4.5, "c": 4.5, "n": 5.0}
+BIG = float(1 << 24)
+C16, C4096, C1 = 1.5 * (1 << 27), 1.5 * (1 << 35), 1.5 * (1 << 23)
+FV = (1, 3, 5)
+PARTS = ((0, 8, "SSVV"), (8, 16, "SSVV"))
+AHEAD = (2.0, 3.0, 4.0, 2.5)
+HP = 1.5 * (1 << 22)
+SHIFT = {"S": 0.0, "M": 131072.0, "V": -131072.0}
+LAT = {"A": 8.0, "U": 5.0, "T": 14.0, "f": 14.0, "b": 6.0, "a": 6.0, "c": 5.0}
 WAKE = 0.1
-SLACK = 0.03
-PIECES = 2
+FIX, FIXS = 0.005, 0.05
+FIXP, SAME = 0.0, 0.25
+WIDE = 2
+PASSES = 6
 
-SCRATCH = {}
+SCRATCH, PART = {}, {}
 
 
 def _sb(dtype, **cols):
+    b = "all" + dtype
     for n in cols:
-        SCRATCH[n] = ("sbuf", [128, cols[n]], dtype)
+        at = SCRATCH[b][1][1] if b in SCRATCH else 0
+        SCRATCH[b] = ("sbuf", [128, at + (cols[n] + 15) // 16 * 16], dtype)
+        PART[n] = (b, at, cols[n], n)
 
 
-_sb("int32", entx=1024, R=1280, wti=1, kpi=1, ci=1024, ci2=1024, pmi=16, pmj=16, xv=256, xh=256)
-_sb("bfloat16", fx=2064, one=128, blka=128, blk=128, blkb=128, zer=256, sel=2048, wsel=2048, tri=2048, dlt=256, rA=256, rK=256, sgm=512)
-_sb("float32", wtf=1, iot=1024, Ct0=1024, Ct1=1024, Ct2=1024, Ct3=1024, allf=128, pmf=16, x16=16, cmk=16, c15=1, mio=256, lio=512,
-    lbl=256, dma_=256, DM=256, KM=256, kcol=1, xs=256)
-_sb("uint16", lst=16, off=256, eu=256, e16=16, ebc=256, pos=16)
-_sb("int32", k1=256, ui=16, ub=16, uq=16, us=16, ei=256, em=256, oc=512, ky=16, kk=16, es=16, er=16, ti=1)
-_sb("float32", pr=256, acol=1, ep=256, D=4096, mx=64, m2=32, ku=16, erf=16, wacc=1, px=256, ps=256, pf=16)
-_sb("bfloat16", Yg=4096, Ys=4096, X=4096, Y=4096, NM=4096, EQ=4096)
-_sb("int32", qa=256, za=256, l5a=256, ita=256, bI=256, qb=256, zb=256, l5b=256, itb=256, hi=256)
-_sb("float32", aw=256, aP=256, zda=256, zdb=256, ca=256, bs=256, wbx=256, pb=256, rr=256, Xd=256, na1=256, nb1=256, na3=256, nbA=256,
-    a1=256, nb=256, yo=1024, xo=256)
-for _n in ("pk0", "pk1", "pu", "pc", "pm", "t1", "t2", "t3"):
-    SCRATCH[_n] = ("psum", [128, 512], "float32")
-STEP = {"a": 264, "u": 32, "c": 4, "n": 256}
-PART = {}
-MSG = {"a": (258, "int32"), "u": (32, "float32"), "c": (1, "int32"), "n": (256, "int32")}
-SEMAPHORES = ["qv", "qs", "qp", "qg", "ld0", "ld1", "ld2", "ld3", "oc0", "oc1", "oc2", "oc3", "st", "lsem"]
+def _ps(bank, **views):
+    SCRATCH[bank] = ("psum", [128, 512], "float32")
+    for n in views:
+        PART[n] = (bank, views[n][0], views[n][1], bank)
+
+
+_sb("int32", entx=1024, wti=1, kpi=1, ci=1024, pmi=16, pmj=16, lpi=16, n1=512, q=256, k1=256, za=256, l5a=256, ui=16, ub=16, uq=16,
+    ei=256, em=256, ky=16, er=16, ti=1, ta=1, qb=256, zb=256, l5b=256, bk=256, bkc=256)
+_sb("bfloat16", fx0=2064, fx2=2064, fx3=2064, one=128, blka=128, blk=128, idb=128, hid=128, zer=256, zz=720, tri=2048, dlt=16, rA=256, rK=16,
+    sgm=512, fl=256, sgs=256, sgk=256, Yg=4096, Ys=4096, Xb=4096, NM=4096, NM2=4096, EQ=4096)
+_sb("uint16", lstP=16, lstI=16, off=256, eu=256, e16=16, ebc=256, pos=16, pos2=16, sel=16)
+_sb("float32", TB0=1280, TB1=1280, TB2=1280, TB3=1280, TB4=1024, LB=1280, yo=1280, Ct=1024, iot=1024, D=4096, idf=128, allf=128, pmf=16,
+    x16=16, cmk=16, lI=16, lbl=16, lbl8=16, mio=256, wk=2, pr=256, x1=256, oc=256, oT=1536, aw=256, aP=256, akc=256, ca=256, sU=48, lU=48, uk=48,
+    sA=256, lA=256, iap=256, ef=256, mxa=128, mxb=128, m2=64, m3=32, erf=16, wacc=2, pm=16, sl=16, bF=256, dp=256, wbx=256, r1=256, rr=256, tb=256, xb=256, xa=256,
+    W=512, nb=256, na=256, d1=256, d2=256)
 for _t in range(NR):
-    for _m in MSG:
-        if _m == "c" and _t == NR - 1:
-            continue
-        for _s in "sl":
-            SCRATCH[_s + _m] = ("sbuf", [128, NR * STEP[_m]], MSG[_m][1])
-            PART["%s%s%d" % (_s, _m, _t)] = (_s + _m, _t * STEP[_m], MSG[_m][0])
-        SEMAPHORES.append("%s%d" % (_m, _t))
-for _n, _b, _c in (("v1", "t1", 0), ("v2", "t1", 256), ("v3", "t2", 0), ("v4", "t2", 256), ("v5", "t3", 0), ("v6", "t3", 256),
-                   ("cbp", "pk0", 0), ("dbp", "pk0", 256), ("dap", "pm", 256), ("nsp", "pk1", 0), ("wnp", "pk1", 256), ("bPp", "pm", 0), ("dp", "pu", 256), ("ctl", "pc", 256)):
-    PART[_n] = (_b, _c, 256)
+    _sb("float32", **{"sb%d" % _t: 272, "lb%d" % _t: 272, "sa%d" % _t: 256, "la%d" % _t: 256, "sc%d" % _t: 1, "lc%d" % _t: 1})
+_ps("pu", up=(0, 16), cnt=(32, 1), c2=(64, 16), kmp=(256, 16))
+_ps("pk0", key0=(0, 512))
+_ps("pk1", key1=(0, 512))
+_ps("pc", pcp=(0, 256), ctp=(256, 256))
+_ps("pa", Ap=(0, 256), Ia=(256, 256))
+_ps("pn", ns=(0, 256), cb=(256, 256))
+_ps("t0", u0=(0, 512), w0=(0, 256), w1=(256, 256))
+_ps("t1", u1=(0, 512), w2=(0, 256), w3=(256, 256))
+for _i, _n in enumerate(("zS", "zM", "zP", "z1", "zw")):
+    PART[_n] = (PART["zz"][0], PART["zz"][1] + 144 * _i, 144, "zz")
+
+
+def messages(n):
+    x = [-1]
+    for t in range(NR):
+        x.append(x[-1] + 1 + t % (n - 1))
+    hold = x[1:] + [0]
+    out = {}
+
+    def piece(m, src, dst, lo, hi, by, kind):
+        for name in (src, dst):
+            PART[name + m] = (PART[name][0], PART[name][1] + lo, hi - lo, name)
+        out[m] = (src + m, dst + m, hi - lo, by, kind)
+    piece("U", "sU", "lU", 0, 48, -x[0], "c")
+    for h in range(2):
+        piece("A%d" % h, "sA", "lA", 128 * h, 128 * h + 128, -x[0], "ba"[h])
+    for t in range(NR):
+        piece("T%d" % (t + 1), "TB%d" % t, "TB%d" % (t + 1), 0, 1024, hold[t] - hold[t + 1], "T")
+        if t > 1:
+            piece("f%d" % t, "fx0", "fx%d" % t, 0, 2064, -x[t], "f")
+        if t + 1 < NR:
+            piece("c%d" % t, "sc%d" % t, "lc%d" % t, 0, 1, x[t] - x[t + 1], "c")
+        for h in range(2):
+            piece("b%d%d" % (t, h), "sb%d" % t, "lb%d" % t, 128 * h, 128 + 144 * h, hold[t] - hold[t + 1], "b")
+            piece("a%d%d" % (t, h), "sa%d" % t, "la%d" % t, 128 * h, 128 * h + 128, x[t] - hold[t + 1], "a")
+    return out
+
+
+MSG = messages(8)
+SEMAPHORES = ["qv", "qs", "qp", "qg", "ld0", "ld4", "ld5", "ld6", "st", "lsem"] + ["oc%d" % _i for _i in range(2 * NR)] + sorted(MSG)
 
 
 def bits(m):
     return bin(m).count("1")
 
 
-def relays(topo, T, src, dst):
-    return [c for c in topo.cores_of(src) if topo.may_write(c, dst) and topo.die(c) == topo.die(src) and T.rank_of(c) is None]
+def route(topo, T, src, dst, m):
+    if (src, dst, m) not in WAYS:
+        here = topo.cores_of(src)
+        alone = all(T.cores[(r + MSG[m][3]) % len(T.cores)] in here for r, c in enumerate(T.cores) if c in here and c != src)
+        WAYS[(src, dst, m)] = ways(topo, T, src, dst, MSG[m][2], MSG[m][4], alone)
+    return WAYS[(src, dst, m)]
 
 
-def route(topo, T, src, dst, m, t):
-    w = MSG[m][0]
-    if topo.may_write(src, dst):
-        return [(None, 0, w)]
-    rl = relays(topo, T, src, dst)
-    if w < 64:
-        return [(rl[1 if m == "u" else 0], 0, w)]
-    return [(rl[0], 0, 128), (rl[1], 128, w)]
+WAYS = {}
 
 
-def target(T, rank, m, t):
-    n = len(T.cores)
-    s = 1 + t % (n - 1)
-    return (rank + s) % n if m in "au" else (rank - s) % n
+def ways(topo, T, src, dst, w, kind, alone):
+    if dst in topo.cores_of(src):
+        return [((), 0, w)]
+    free = [c for c in topo.cores_of(src) if T.rank_of(c) is None]
+    mine = [c for c in free if topo.die(c) == topo.die(src)]
+    near = [c for c in mine if topo.may_write(c, dst)]
+    if kind in "abc":
+        return [(() if topo.may_write(src, dst) else (near[0 if kind == "b" else 1],), 0, w)]
+    if alone:
+        chains = [(c,) for c in free if topo.may_write(c, dst) and c not in mine] + [(c,) for c in near]
+    else:
+        far = [c for c in range(256) if topo.mates(c, dst) and topo.may_write(c, dst) and topo.die(c) == topo.die(src)]
+        chains = [(c, far[0]) for c in mine if c not in near] + [(c,) for c in near]
+    cut = [(w * j // len(chains) + 15) // 16 * 16 for j in range(len(chains))] + [w]
+    return [(chains[j], cut[j], cut[j + 1]) for j in range(len(chains))]
 
 
-def source(T, rank, m, t):
-    n = len(T.cores)
-    s = 1 + t % (n - 1)
-    return (rank - s) % n if m in "au" else (rank + s) % n
+def view(T, name, lo, hi):
+    b, at = PART[name][:2]
+    return T[b][:, at + lo:at + hi]
 
 
 def hand_on(g, core, T, topo):
-    sent = 0
-    mine = [r for r, c in enumerate(T.cores) if c in topo.cores_of(core)]
-    if not mine:
-        return
-    for m, t in plan(T)[2]:
-        for r in mine:
-            src, dst = T.cores[r], T.cores[target(T, r, m, t)]
-            for rl, lo, hi in route(topo, T, src, dst, m, t):
-                if rl != core:
+    sent, n = 0, len(T.cores)
+    for m in plan(T)[2]:
+        for r in range(n):
+            src, dst = T.cores[r], T.cores[(r + MSG[m][3]) % n]
+            for chain, lo, hi in route(topo, T, src, dst, m):
+                if core not in chain:
                     continue
-                b, at = T["l" + m], STEP[m] * t
-                sem = T.sem["%s%d" % (m, t)]
-                g.wait_ge(sem, bits(topo.mask(src, core)))
-                rid, pid = topo.addr(dst, core)
-                mk = topo.mask(core, dst)
-                g.remote_dma(b[:, at + lo:at + hi], b[:, at + lo:at + hi], sem, T.sem.lsem, pid, rid, mk)
+                way = (src,) + chain + (dst,)
+                before, to = way[way.index(core) - 1], way[way.index(core) + 1]
+                b = view(T, MSG[m][1], lo, hi)
+                g.wait_ge(T.sem[m], bits(topo.mask(before, core)))
+                rid, pid = topo.addr(to, core)
+                mk = topo.mask(core, to)
+                g.remote_dma(b, b, T.sem[m], T.sem.lsem, pid, rid, mk)
                 sent += bits(mk)
     if sent:
         g.wait_ge(T.sem.lsem, sent)
 
 
 def B(name, lo=0, hi=None, st=1):
-    if name in PART:
-        b, at, w = PART[name]
-        return (b, at + lo, at + (w if hi is None else hi), st)
-    return (name, lo, SCRATCH[name][1][1] if hi is None else hi, st)
+    b, at, w, key = PART[name]
+    return (b, at + lo, at + (w if hi is None else hi), st, key)
 
 
 def width(x):
@@ -122,87 +162,130 @@ def covers(a, b):
 
 
 def links(ops):
-    acc, out = {}, []
+    acc, out, group = {}, [], {}
     for i, o in enumerate(ops):
         pre = set(o["after"])
+        o["banks"] = sorted(set(x[0] for x in o["r"] + o["w"] if SCRATCH[x[0]][0] == "psum"))
+        if o["q"] == "p":
+            if o["banks"][0] in group:
+                pre.add(group[o["banks"][0]])
+            group[o["banks"][0]] = i
         for wr, lst in ((False, o["r"]), (True, o["w"])):
             for x in lst:
-                ps = SCRATCH[x[0]][0] == "psum"
-                for (y, w2, j) in acc.get(x[0], []):
-                    if j == i:
-                        continue
-                    if ps and (ops[j]["q"] != o["q"] or o["q"] == "p"):
-                        pre.add(j)
-                    elif (wr or w2) and meets(x, y):
+                for (y, w2, j) in acc.get(x[4], []):
+                    if j != i and (wr or w2) and meets(x, y):
                         pre.add(j)
         for x in o["w"]:
-            acc[x[0]] = [a for a in acc.get(x[0], []) if a[2] == i or not covers(x, a[0]) or (SCRATCH[x[0]][0] == "psum" and ops[a[2]]["q"] != o["q"])]
-            acc[x[0]].append((x, True, i))
+            acc[x[4]] = [a for a in acc.get(x[4], []) if a[2] == i or not covers(x, a[0])]
+            acc[x[4]].append((x, True, i))
         for x in o["r"]:
-            acc.setdefault(x[0], []).append((x, False, i))
+            acc.setdefault(x[4], []).append((x, False, i))
         out.append(sorted(pre))
     return out
 
 
 def arrange(ops, pre, wake):
     n = len(ops)
-    suc = [[] for _ in range(n)]
+    dur = [o["dur"] for o in ops]
+    fwd, bwd = [[] for _ in ops], [[] for _ in ops]
     for i in range(n):
-        for j in pre[i]:
-            suc[j].append(i)
-    prio = [0.0] * n
+        for j, lag in [(j, dur[j] + (wake if ops[i]["q"] != ops[j]["q"] else 0.0 if ops[i]["q"] == "p" else SAME)) for j in pre[i]] + ops[i]["behind"]:
+            fwd[j].append((i, lag))
+            bwd[i].append((j, lag + dur[i] - dur[j]))
+
+    def after(line, t):
+        lo, hi = 0, len(line)
+        while lo < hi:
+            mid = (lo + hi) // 2
+            if line[mid][1] <= t + 1e-9:
+                lo = mid + 1
+            else:
+                hi = mid
+        return lo
+
+    def place(edges, back, key):
+        left, est, start, busy = [len(b) for b in back], [0.0] * n, [0.0] * n, {}
+        ready = [i for i in range(n) if not left[i]]
+        while ready:
+            i = min(ready, key=key)
+            ready.remove(i)
+            t = est[i]
+            if ops[i]["kind"] in ("run", "send"):
+                q = ops[i]["q"]
+                lines = [(q, 0.0)] + [(b + r, wake) for b in ops[i]["banks"] for r in "vsp" if r != q]
+                moved = True
+                while moved:
+                    moved = False
+                    for name, pad in lines:
+                        line = busy.get(name, [])
+                        lo = after(line, t - pad)
+                        while lo < len(line) and line[lo][0] < t + dur[i] + pad:
+                            t, moved = line[lo][1] + pad, True
+                            lo += 1
+                for name in [q] + [b + q for b in ops[i]["banks"]]:
+                    line = busy.setdefault(name, [])
+                    line.insert(after(line, t), (t, t + dur[i]))
+            start[i] = t
+            for k, lag in edges[i]:
+                est[k] = max(est[k], t + lag)
+                left[k] -= 1
+                if not left[k]:
+                    ready.append(k)
+        return start
+
+    late = [0.0] * n
     for i in range(n - 1, -1, -1):
-        prio[i] = ops[i]["dur"] + (0.0 if ops[i]["q"] == "p" else wake) + max([prio[k] for k in suc[i]] + [0.0])
-    left = [len(p) for p in pre]
-    est = [0.0] * n
-    ready = [i for i in range(n) if left[i] == 0]
-    free, seq = {}, []
-    while ready:
-        st = {i: max(free.get(ops[i]["q"], 0.0), est[i]) for i in ready}
-        first = min(ready, key=lambda i: (st[i], -prio[i]))
-        q, lim = ops[first]["q"], st[first] + SLACK
-        i = max([k for k in ready if ops[k]["q"] == q and st[k] <= lim], key=lambda k: (prio[k], -k))
-        if q is None:
-            i = first
-        ready.remove(i)
-        seq.append(i)
-        end = st[i] + ops[i]["dur"]
-        if q is not None:
-            free[q] = st[i] + 0.06 if ops[i]["kind"] == "dma" else end
-        for k in suc[i]:
-            est[k] = max(est[k], end if q == "p" and ops[k]["q"] == "p" else end + wake)
-            left[k] -= 1
-            if left[k] == 0:
-                ready.append(k)
+        for j, lag in bwd[i]:
+            late[j] = max(late[j], late[i] + lag)
+    best = None
+    for _ in range(PASSES):
+        start = place(fwd, bwd, lambda i: (-late[i] - dur[i], i))
+        end = max(start[i] + dur[i] for i in range(n))
+        if best is None or end < best[0]:
+            best = (end, start)
+        late = place(bwd, fwd, lambda i: (-start[i] - dur[i], -i))
+    ORDER["end"] = best[0]
+    seq, seen = sorted(range(n), key=lambda i: (best[1][i], i)), {}
+    for i in seq:
+        for b in ops[i]["banks"]:
+            pre[i] = pre[i] + [seen[b + r] for r in "vsp" if r != ops[i]["q"] and b + r in seen]
+            seen[b + ops[i]["q"]] = i
     return seq
 
 
 def record(T):
     ops, where = [], {}
-    CY, G, SC = 0.001, 1.5, 3.0
+    CY, G, SC = 0.00085, 1.55, 3.8
 
     def put(kind, q, fn, r, w, dur, after=(), **more):
-        d = {"kind": kind, "q": q, "fn": fn, "r": list(r), "w": list(w), "dur": dur, "after": list(after)}
+        d = {"kind": kind, "q": q, "fn": fn, "r": list(r), "w": list(w), "dur": dur, "after": list(after), "behind": []}
         d.update(more)
         ops.append(d)
 
+    def mark(name):
+        where[name] = len(ops) - 1
+
+    def behind(name, lag=0.0):
+        ops[-1]["behind"].append((where[name], lag))
+
     def ap(x):
-        name, lo, hi, st = x
+        name, lo, hi, st = x[:4]
         return T[name][:, lo:hi:st] if st != 1 else T[name][:, lo:hi]
+
+    def val(s):
+        return ap(s) if isinstance(s, tuple) else s
 
     def two(*xs):
         return 0.5 if all(SCRATCH[x[0]][2] in ("bfloat16", "uint16") for x in xs) else 1.0
 
     def vd(n, k=1.0):
-        return max(64.0, n * k) * CY
+        return max(64.0, n * k) * CY + FIX
 
-    def ts(o, a, s1, op0, s2=None, op1=None, sc=None):
-        d = vd(width(a), two(o, a))
-        r = [a] if sc is None else [a, sc]
-        if op1 is None:
-            put("run", "v", lambda e: e.tensor_scalar(ap(o), ap(a), s1 if sc is None else ap(sc), None, op0), r, [o], d)
-        else:
-            put("run", "v", lambda e: e.tensor_scalar(ap(o), ap(a), s1 if sc is None else ap(sc), s2, op0, op1), r, [o], d)
+    def ts(o, a, s1, op0, s2=None, op1=None, by=None):
+        r = [x for x in (a, s1, s2, by) if isinstance(x, tuple)]
+        d = vd(width(a), two(o, a)) if by is None else 0.05 + width(o) * G * CY
+        tail = (op0,) if op1 is None else (op0, op1)
+        put("run", "v", lambda e: e.tensor_scalar(ap(o), ap(a) if by is None else ap(a).indirect(ap(by)), val(s1), val(s2), *tail), r, [o], d)
 
     def tt(o, a, b, op):
         k = 1.0 if "psum" in (SCRATCH[a[0]][0], SCRATCH[b[0]][0]) else 2.0
@@ -215,280 +298,376 @@ def record(T):
         put("run", "v", lambda e: e.memset(ap(o), c), [], [o], vd(width(o), two(o)))
 
     def pick(o, win, off, b=None, op=None):
-        r, d = [win, off] + ([b] if b is not None else []), 0.06 + 16 * width(off) * G * CY
+        r, d = [win, off] + ([b] if b is not None else []), 0.05 + width(o) * G * CY
         if b is None:
             put("run", "v", lambda e: e.tensor_copy(ap(o), ap(win).indirect(ap(off))), r, [o], d)
         else:
             put("run", "v", lambda e: e.tensor_tensor(ap(o), ap(win).indirect(ap(off)), ap(b), op), r, [o], d)
 
     def scatter(win, off, a):
-        put("run", "v", lambda e: e.tensor_copy(ap(win).indirect(ap(off)), ap(a)), [a, off], [win], 0.06 + width(a) * SC * CY)
+        put("run", "v", lambda e: e.tensor_copy(ap(win).indirect(ap(off)), ap(a)), [a, off], [win], 0.05 + width(a) * SC * CY)
 
     def scan(o, m, a):
         put("run", "v", lambda e: e.tensor_tensor_scan(ap(o), ap(m), ap(a), 0.0, ALU.mult, ALU.max), [m, a], [o], vd(width(a), two(o, m, a)))
 
-    def act(o, a, f, bias=0.0, scale=1.0, accum=None, sc=None):
-        d = vd(width(a))
-        r = [a] if sc is None else [a, sc]
+    def act(o, a, f, bias=0.0, scale=1.0, accum=None, by=None):
+        r = [x for x in (a, scale, bias, by) if isinstance(x, tuple)]
+        d = vd(width(a)) + FIXS if by is None else 0.065 + width(o) * G * CY
         if accum is not None:
-            put("run", "s", lambda e: e.activation(ap(o), ap(a), f, bias=bias, scale=scale, accum_out=ap(accum)), r, [o, accum], d)
+            put("run", "s", lambda e: e.activation(ap(o), ap(a), f, bias=bias, scale=scale, accum_out=ap(accum)), r, [o, accum], d + 0.02)
         else:
-            put("run", "s", lambda e: e.activation(ap(o), ap(a), f, bias=bias, scale=scale if sc is None else ap(sc)), r, [o], d)
-
-    def apick(o, win, off):
-        put("run", "s", lambda e: e.activation(ap(o), ap(win).indirect(ap(off)), AF.Copy), [win, off], [o], 0.08 + 16 * width(off) * G * CY)
+            put("run", "s", lambda e: e.activation(ap(o), ap(a) if by is None else ap(a).indirect(ap(by)), f, bias=val(bias), scale=val(scale)), r, [o], d)
 
     def mm(o, l, r, st, sp):
-        put("run", "p", lambda e: e.matmul(ap(o), ap(l), ap(r), st, sp), [l, r], [o], vd(width(r), 0.9))
+        if st:
+            where[o[0]] = o
+        put("run", "p", lambda e: e.matmul(ap(o), ap(l), ap(r), st, sp), [l, r], [where[o[0]] if sp else o], (vd(width(r)) - FIX) * (4 if SCRATCH[l[0]][2] == "float32" else 1) + FIXP)
 
     def iota(o, pat, base, cm):
-        d = 0.16 + 2 * width(o) * CY
+        d = 0.13 + 2 * width(o) * CY
         if SCRATCH[o[0]][2] != "int32":
             put("run", "g", lambda e: e.iota(ap(o), pat, base, cm, allow_small_or_imprecise_dtypes=True), [], [o], d)
         else:
             put("run", "g", lambda e: e.iota(ap(o), pat, base, cm), [], [o], d)
 
     def sift(o, a, pat, op, fill, base, cm):
-        put("run", "g", lambda e: e.affine_select(ap(o), ap(a), pat, op, fill, base, cm), [a], [o], 0.2 + 2 * width(o) * CY)
+        put("run", "g", lambda e: e.affine_select(ap(o), ap(a), pat, op, fill, base, cm), [a], [o], 0.17 + 2 * width(o) * CY)
 
-    def load(q, o, a, sem, dur):
-        put("dma", q, lambda e: e.dma_start(ap(o), T[a][:]), [], [o], dur, sem=sem)
+    def gcp(o, a):
+        sift(o, a, [[0, width(o)]], ALU.is_ge, 0.0, 0, 0)
 
-    def send(m, t):
-        where[(m, t)] = len(ops)
-        put("send", "g", None, [B("s%s%d" % (m, t))], [], 0.8, msg=(m, t))
+    def load(q, o, a, sem, dur, lo=0, hi=None):
+        put("dma", q, lambda e: e.dma_start(ap(o), T[a][:] if hi is None else T[a][:, lo:hi]), [], [o], dur, sem=sem, inc=16)
 
-    def expect(m, t):
-        put("land", None, None, [], [B("l%s%d" % (m, t))], LAT[m], [where[(m, t)]], msg=(m, t))
+    def send(m, after=()):
+        where[m] = len(ops)
+        put("send", "g", None, [B(MSG[m][0], 0, MSG[m][2])] + list(after), [], 2.1 if m[0] in "Tf" else 0.7, msg=m)
+
+    def expect(m):
+        put("land", None, None, [], [B(MSG[m][1], 0, MSG[m][2])], LAT[m[0]], [where[m]], msg=m)
+
+    def cls(name, c):
+        return B(name, c, 1021 + c, 4)
+
+    def slide(name, p):
+        return B(name, 15 - p, 143 - p)
 
     load("y", B("entx"), "ent", "ld0", 4.5)
-    ms(B("fx", 0, 16), 0.0)
-    load("s", B("wti"), "wt", "ld1", 2.2)
-    load("s", B("kpi"), "kap", "ld2", 2.2)
-    load("y", B("fx", 1, 2049), "feat", "ld3", 6.0)
+    mark("load")
+    ms(B("fx0", 0, 16), 0.0)
+    ms(B("fx0", 2048, 2064), 0.0)
+    load("s", B("wti"), "wt", "ld4", 2.2)
+    load("s", B("kpi"), "kap", "ld5", 2.2)
+    load("y", B("fx0", 1, 2049), "feat", "ld6", 6.5)
+    behind("load")
+    cp(B("fx0", 2056, 2057), B("wti"))
+    cp(B("fx0", 2057, 2058), B("kpi"))
     ms(B("one"), 1.0)
+    iota(B("ci"), [[37, 1024]], 0, 0)
+    iota(B("lpi"), [[1, 16]], 0, 16)
+    iota(B("pmi"), [[0, 16]], 0, 1)
+    iota(B("x16"), [[1, 16]], 0, 0)
+    for k0, k1, path in PARTS:
+        iota(B("mio", 16 * k0, 16 * k1), [[1, 16], [0, k1 - k0]], 0, 0)
     sift(B("blka"), B("one"), [[-16, 8], [0, 16]], ALU.is_ge, 0.0, 0, 1)
     sift(B("blk"), B("blka"), [[16, 8], [0, 16]], ALU.is_ge, 0.0, 15, -1)
-    iota(B("pmi"), [[0, 16]], 0, 1)
-    iota(B("lio"), [[0, 32], [1, 16]], 0, 0)
-    iota(B("x16"), [[1, 16]], 0, 0)
-    iota(B("mio"), [[1, 16], [0, 16]], 0, 0)
-    iota(B("lbl"), [[1, 256]], 1024, 0)
-    iota(B("ci"), [[37, 1024]], -1, 0)
-    iota(B("iot"), [[1, 1024]], 0, 0)
-    ms(B("wsel"), 0.0)
-    ms(B("sel"), 0.0)
+    sift(B("idb"), B("one"), [[-1, 128]], ALU.is_equal, 0.0, 0, 1)
+    ms(B("zz"), 0.0)
     ms(B("zer"), 0.0)
-    ms(B("allf"), 2.0 ** -28)
-    ts(B("sgm"), B("lio"), 1.0, ALU.min)
+    ms(B("allf"), -1.0 / 16)
+    ms(B("sgm"), 1.0)
+    cp(B("sgm", 0, 497, 16), B("zer", 0, 32))
+    ts(B("ci"), B("ci"), 63, ALU.bitwise_and)
+    ts(B("Ct"), B("ci"), 4096.0, ALU.mult, 262144.0 - 2048.0, ALU.add)
+    ts(B("lpi"), B("lpi"), 255, ALU.bitwise_and)
+    cp(B("lstP"), B("lpi"))
     ts(B("pmj"), B("pmi"), 15, ALU.bitwise_and)
     cp(B("pmf"), B("pmj"))
-    cp(B("wtf"), B("wti"))
-    for t in range(NR):
-        cp(B("sa%d" % t, 256, 257), B("kpi"))
-        cp(B("sa%d" % t, 257, 258), B("kpi"))
-    for p in range(16):
-        act(B("wsel", 129 * p, 129 * p + 113, 16), B("blk", 0, 113, 16), AF.Copy, sc=B("wtf"))
-    act(B("blkb"), B("blk"), AF.Copy, scale=P24)
-    for p in range(16):
-        act(B("sel", 129 * p, 129 * p + 113, 16), B("blk", 0, 113, 16), AF.Copy, scale=-4096.0)
-    ts(B("cmk"), B("x16"), None, ALU.is_gt, P24, ALU.mult, sc=B("pmf", 0, 1))
+    pm = B("pmf", 0, 1)
+    ts(B("lI"), B("x16"), 16.0, ALU.mult, pm, ALU.add)
+    cp(B("lstI"), B("lI"))
+    ts(B("lbl"), B("lI"), 1024.0, ALU.add)
+    for k0, k1, path in PARTS:
+        ts(B("lbl8", k0, k1), B("lI", k0, k1), 16.0, ALU.mult, -256.0 * k0, ALU.add)
+    ts(B("dlt"), B("x16"), pm, ALU.is_equal)
+    for k0, k1, path in PARTS:
+        n = 16 * (k1 - k0) // len(path)
+        for c in range(len(path)):
+            at = 16 * k0 + n * c
+            act(B("rA", at, at + n), B("mio", at, at + n), AF.Identity, bias=15360.0 + SHIFT[path[c]], scale=-1024.0)
+    act(B("idf"), B("idb"), AF.Copy)
+    act(B("hid"), B("idb"), AF.Copy, scale=HP)
+    for n, s in (("zS", -8192.0), ("zM", -16384.0), ("zP", 16384.0), ("z1", 128.0)):
+        act(B(n, 15, 128, 16), B("blk", 0, 113, 16), AF.Copy, scale=s)
+    ts(B("cmk"), B("x16"), pm, ALU.is_gt)
     for x in range(16):
-        act(B("tri", 128 * x, 128 * x + 128), B("blk"), AF.Copy, sc=B("cmk", x, x + 1))
-    ts(B("dlt"), B("mio"), None, ALU.is_equal, sc=B("pmf", 0, 1))
-    ts(B("c15"), B("pmf", 0, 1), -256.0, ALU.mult, 3840.0, ALU.add)
-    ts(B("rA"), B("dlt"), None, ALU.mult, sc=B("c15"))
-    ts(B("dma_"), B("lio", 0, 256), None, ALU.is_equal, sc=B("pmf", 0, 1))
-    tt(B("DM"), B("dma_"), B("lbl"), ALU.mult)
-    cp(B("lst"), B("pmj"))
-    ts(B("ci2"), B("ci"), 63, ALU.bitwise_and)
-    ts(B("Ct0"), B("ci2"), 4096.0, ALU.mult, 22.0, ALU.add)
-    for t in range(1, NR):
-        act(B("Ct%d" % t), B("Ct0"), AF.Identity, bias=float(t))
+        act(B("tri", 128 * x, 128 * x + 128), B("blk"), AF.Copy, scale=B("cmk", x, x + 1))
 
-    def lanes(c):
-        return ("R", c, 1021 + c, 4)
+    def convert(o, x, w):
+        n1, w = B("n1", 0, width(x)), B(w, 0, width(x))
+        ts(n1, x, 2.0 ** -11, ALU.mult, 0.5 - 2.0 ** -12, ALU.add)
+        ts(w, n1, 2048.0, ALU.mult, 15.0, ALU.add)
+        tt(o, w, x, ALU.add)
+    convert(B("sA"), cls("entx", 0), "u0")
+    for h in range(2):
+        send("A%d" % h)
+    iota(B("iot"), [[1, 1024]], 0, 0)
+    behind("A1")
 
-    def convert(c):
-        x = B("entx", c, 1021 + c, 4)
-        v, w = ("v1", "v3") if c % 2 else ("v2", "v5")
-        ts(B("xv"), x, 2047.0, ALU.add)
-        ts(B("xh"), B("xv"), -2048, ALU.bitwise_and)
-        ts(B(v), B("xh"), 3.0, ALU.mult)
-        tt(B("xs"), B(v), x, ALU.subtract)
-        ts(B(w), B("xs"), 0.0, ALU.is_equal, EMP, ALU.mult)
-        tt(lanes(c), B(w), B("xs"), ALU.max)
+    def decode(o, a, w, k):
+        d1, d2 = B("d1", k, k + width(a)), B("d2", k, k + width(a))
+        act(d1, a, AF.Identity, bias=C1, scale=2.0 ** -12)
+        act(w, d1, AF.Identity, bias=2048.0 * C1, scale=-2048.0)
+        tt(d2, w, a, ALU.add)
+        act(o, d2, AF.Relu, bias=-15.0)
 
-    def own(t):
-        expect("n", t)
-        ts(B("v1"), lanes(t), 0.0, ALU.is_equal, P24, ALU.mult)
-        tt(B("v3"), B("v1"), B("ln%d" % t), ALU.min)
-        tt(lanes(t), B("v3"), lanes(t), ALU.max)
+    def complete(t, name):
+        for h, (k0, k1, path) in enumerate(PARTS):
+            expect("a%d%d" % (t - 1, h))
+            o, a = B(name, 64 * k0 + t - 1, 64 * k1 + t - 4, 4), B("la%d" % (t - 1), 16 * k0, 16 * k1)
+            if t < NR:
+                gcp(o, a)
+            else:
+                act(o, a, AF.Copy)
+            expect("b%d%d" % (t - 1, h))
+        cp(B("pos2"), B("lb%d" % (t - 1), 256, 272))
+        scatter(B(name), B("pos2"), B("lb%d" % (t - 1), 0, 256))
 
-    convert(0)
-    FX = B("fx", 0, 2049)
-    RT = B("R", 0, 1024)
+    ID = B("lstI")
+    act(B("ctp"), cls("Ct", 0), AF.Copy)
     for t in range(NR):
-        sa, la, su, lu = "sa%d" % t, "la%d" % t, "su%d" % t, "lu%d" % t
-        Ct = B("Ct%d" % t)
-        cp(B(sa, 0, 256), lanes(t))
-        send("a", t)
-        for h in range(2):
-            lo, hi = 128 * h, 128 * h + 128
-            x = ("R", 4 * lo + t, 4 * hi - 3 + t, 4)
-            ts(B("k1", lo, hi), x, 16, ALU.bitwise_and)
-            tt(B("pr", lo, hi), x, B("k1", lo, hi), ALU.mult)
-            ts(B("off", lo, hi), B("pr", lo, hi), 2.0 ** -16, ALU.mult)
+        last = t == NR - 1
+        A, fx, TB, U = cls("LB", t) if t else B("sA"), "fx%d" % (t if t > 1 else 0), "TB%d" % t, "uk" if t else "sU"
+        tau, clock = 5.0 + t, 12.0 + t
+        if t > 1:
+            expect("f%d" % t)
+        if t != 1:
+            cp(B("wk"), B(fx, 2056, 2058))
+            if t:
+                behind("scatter")
+            ts(B("zw", 15, 128, 16), B("blk", 0, 113, 16), B("wk", 0, 1), ALU.mult)
+            ts(B("rK"), B("dlt"), B("wk", 1, 2), ALU.mult)
+            mm(B("kmp"), B("blk"), B("rK"), True, True)
+        cp(B(U, 32, 48), B("kmp"))
+        tt(B("q"), B("ctp"), A, ALU.add)
+        act(B("Ap"), A, AF.Copy)
+        ts(B("k1"), B("q"), 16, ALU.bitwise_and)
+        tt(B("pr"), B("Ap"), B("k1"), ALU.mult)
+        for lo, hi in ((0, 4), (4, 16)):
+            ts(B("off", 16 * lo, 16 * hi), B("pr"), 2.0 ** -16, ALU.mult, 127.0 / 256, ALU.add, by=B("lstP", lo, hi))
         for c in range(8):
-            (apick if c < GS else pick)(B("Yg", 512 * c, 512 * c + 512), FX, B("off", 32 * c, 32 * c + 32))
-        for c in range(8):
-            scan(B("Ys", 512 * c, 512 * c + 512), B("sgm"), B("Yg", 512 * c, 512 * c + 512))
-        for p in range(16):
-            mm(B("pu", 0, 16), B("wsel", 128 * p, 128 * p + 128), B("Ys", 16 * p + 15, 4096, 256), p == 0, p == 15)
-        cp(B("ui"), B("pu", 0, 16))
+            o, l = B("Yg", 512 * c, 512 * c + 512), B("off", 32 * c, 32 * c + 32)
+            if c in FV:
+                pick(o, B(fx, 0, 2049), l)
+            else:
+                act(o, B(fx, 0, 2049), AF.Copy, by=l)
+            scan(B("Ys", 512 * c, 512 * c + 512), B("sgm"), o)
+            for p in (2 * c, 2 * c + 1):
+                mm(B("up"), slide("zw", p), B("Ys", 256 * p + 15, 256 * p + 256, 16), p == 0, p == 15)
+        cp(B("ui"), B("up"))
         ts(B("ub"), B("ui"), 4095, ALU.bitwise_and)
         tt(B("uq"), B("ub"), B("ub"), ALU.mult)
-        cp(B(su, 0, 16), B("ub"))
-        ts(B("us"), B("uq"), 5, ALU.arith_shift_right)
-        if t == 0:
-            cp(B(su, 16, 32), B("us"))
+        if t:
+            expect("c%d" % (t - 1))
+        cp(B(U, 0, 16), B("ub"))
+        ts(B(U, 16, 32), B("uq"), 2.0 ** -5, ALU.mult, B("lc%d" % (t - 1)) if t else -13.0 / 32, ALU.add)
+        if not t:
+            send("U")
+            for h in range(2):
+                expect("A%d" % h)
+            A, U = B("lA"), "lU"
+            tt(B("q"), B("ctp"), A, ALU.add)
+        act(B("x1"), A, AF.Identity, bias=-7.5)
+        ts(B("oc"), B("x1"), C16, ALU.add, C16, ALU.subtract)
+        for h, (k0, k1, path) in enumerate(PARTS):
+            n, reps = 16 * (k1 - k0), 16 // len(path)
+            first = 1 if t else reps
+            for j in range(first):
+                act(B("oT", 768 * h + n * j, 768 * h + n * j + n), B("oc", 16 * k0, 16 * k1), AF.Identity, bias=7.5)
+            n, reps = n * first, reps // first
+            for j in range(1, reps):
+                o, a = B("oT", 768 * h + n * j, 768 * h + n * j + n), B("oT", 768 * h, 768 * h + n)
+                put("dma", "y", lambda e, o=o, a=a: e.dma_start(ap(o), ap(a)), [a], [o], 2.2, sem="oc%d" % (2 * t + h), inc=16 * (reps - 1))
+        ts(B("za"), B("q"), 0x3801F, ALU.bitwise_and)
+        ts(B("l5a"), B("q"), 31, ALU.bitwise_and)
+        act(B("sgs"), B("l5a"), AF.Sign, bias=-tau - 0.5, by=ID)
+        act(B("sgk"), B("za"), AF.Sign, bias=tau + 0.5, scale=-1.0, by=ID)
+        for o, x, signs in (("w0", A, ("sgs",)), ("w2", B("oc"), ("sgk",)), ("w1", A, ("sgs", "sgk"))):
+            mm(B(o), B("idf"), x, True, False)
+            for s in signs:
+                mm(B(o), B("hid"), B(s), False, s == signs[-1])
+        act(B("aw"), B("w0"), AF.Relu, bias=-HP)
+        act(B("akc"), B("w2"), AF.Identity, bias=clock - HP)
+        act(B("aP"), B("w1"), AF.Copy)
+        act(B("ca"), B("w1"), AF.Relu, bias=-15.5 * 16384, scale=16384.0)
+        mark("lanes")
+        act(B("iap"), B("l5a"), AF.Relu, bias=31 * BIG, scale=-2 * BIG, by=ID)
+        act(B("Ia"), B("iap"), AF.Identity, bias=clock, scale=-1.0)
+        if last:
+            decode(B("x1"), A, B("Ap"), 0)
+            A = B("x1")
+        for h in range(2):
+            gcp(B("W", 256 * h + 128, 256 * h + 256), (A[0], A[1] + 128 * h * A[3], A[1] + (128 * h + 127) * A[3] + 1) + A[3:])
+        if t:
+            expect("T%d" % t)
+            complete(t, TB)
         else:
-            expect("c", t - 1)
-            cp(B("acol"), B("lc%d" % (t - 1)))
-            ts(B(su, 16, 32), B("us"), None, ALU.add, sc=B("acol"))
-        send("u", t)
-        if t == 0:
-            for c in range(1, 4):
-                convert(c)
-        else:
-            own(t - 1)
-        expect("a", t)
-        A = B(la, 0, 256)
-        ts(B("oc", 0, 256), A, -16, ALU.bitwise_and)
-        put("dma", "y", lambda e: e.dma_start(T.oc[:, 256:512], T.oc[:, 0:256]), [B("oc", 0, 256)], [B("oc", 256, 512)], 2.2, sem="oc%d" % t)
-        cp(B("kcol"), B(la, 256, 257))
-        ts(B("rK"), B("dlt"), None, ALU.mult, sc=B("kcol"))
-        mm(B("pm", 0, 256), B("blk"), B("rK"), True, True)
-        act(B("KM"), B("pm", 0, 256), AF.Copy)
-        act(B("ctl"), ("Ct%d" % t, t, 1021 + t, 4), AF.Copy)
-        tt(B("qa"), B("ctl"), A, ALU.add)
-        ts(B("za"), B("qa"), 0x3801F, ALU.bitwise_and)
-        ts(B("l5a"), B("qa"), 31, ALU.bitwise_and)
-        ts(B("v5"), B("l5a"), float(5 + t), ALU.is_le, EMP, ALU.mult)
-        ts(B("v6"), B("za"), float(5 + t), ALU.is_gt, P24, ALU.mult)
-        tt(B("aw"), B("v5"), A, ALU.max)
-        tt(B("v4"), B("v6"), A, ALU.add)
-        tt(B("aP"), B("v4"), B("aw"), ALU.min)
-        tt(B("zda"), B("v6"), B("za"), ALU.subtract)
-        act(B("dap"), B("zda"), AF.Relu, bias=7.0 / 16, scale=-1.0 / 16)
-        act(B("ca"), B("aP"), AF.Identity, bias=EMP * 2048.0, scale=-2048.0)
-        ts(B("ita"), A, 16, ALU.bitwise_and)
-        expect("u", t)
-        u, s = B(lu, 0, 16), B(lu, 16, 32)
-        for h in range(PIECES):
-            lo, hi = 256 * h // PIECES, 256 * (h + 1) // PIECES
-            pick(B("ep", lo, hi), u, B("lst", lo // 16, hi // 16), B("KM", lo, hi), ALU.mult)
-            pick(B("ei", lo, hi), s, B("lst", lo // 16, hi // 16), B("ep", lo, hi), ALU.add)
-            ts(B("em", lo, hi), B("ei", lo, hi), 1023, ALU.bitwise_and)
-            cp(B("eu", lo, hi), B("em", lo, hi))
+            for j in range(2):
+                convert(B(TB, 512 * j, 512 * j + 512), B("entx", 512 * j, 512 * j + 512), "key%d" % j)
+            expect("U")
+        send("T%d" % (t + 1), [] if t else [B("lU")])
+        if t + 2 < NR:
+            send("f%d" % (t + 2))
+            behind("T%d" % (t + 1))
+        if not last:
+            gcp(cls("LB", t + 1), cls(TB, t + 1))
+        RT = B(TB, 0, 1024)
 
-        def ch(n, c):
-            return B(n, 512 * c, 512 * c + 512)
-        for c in range(8):
-            pick(ch("D", c), RT, B("eu", 32 * c, 32 * c + 32), B("oc"), ALU.subtract)
-            act(ch("X", c), ch("D", c), AF.Abs, bias=-7.5)
-            ts(ch("Y", c), ch("X", c), 3000.0, ALU.min, 262144.0 + 1016.0, ALU.add)
-            if c < SQ:
-                act(ch("NM", c), ch("Y", c), AF.Square, bias=-129.0, scale=2.0 ** -11)
-            else:
-                ts(ch("NM", c), ch("Y", c), 262144.0 + 2048.0, ALU.not_equal)
-        for c in range(4):
-            o = B("pk%d" % (c % 2), 0, 64)
-            mm(o, B("blk"), B("rA", 64 * c, 64 * c + 64), True, False)
-            mm(o, B("blk"), B("rK", 64 * c, 64 * c + 64), False, False)
+        for h, (k0, k1, path) in enumerate(PARTS):
+            lo, hi, nk = 16 * k0, 16 * k1, k1 - k0
+            cw = 16 * nk // len(path)
+
+            def H(n):
+                return B(n, lo, hi)
+
+            def ch(n, c, more=1):
+                return B(n, 16 * (lo + cw * c), 16 * (lo + cw * (c + more)))
+            for k in range(k0, k1):
+                ts(B("ei", lo + k - k0, hi, nk), B(U, 32, 48), B(U, k, k + 1), ALU.mult, B(U, 16 + k, 17 + k), ALU.add)
+            ts(H("em"), H("ei"), 1023, ALU.bitwise_and)
+            cp(H("eu"), H("em"))
+            act(H("ef"), H("em"), AF.Copy, by=B("lstI", 0, nk))
+            own = B("oT", 768 * h, 768 * h + 16 * cw)
+            for c in range(len(path)):
+                l = B("eu", lo + cw * c, lo + cw * c + cw)
+                pick(ch("Xb" if path[c] == "V" else "D", c), RT, l, own, ALU.subtract)
+                if h or c:
+                    behind("pick")
+                mark("pick")
+                pair = WIDE and path[c] == path[c ^ 1] and (h or c > 1 or WIDE > 1)
+                if pair and c % 2 == 0:
+                    continue
+                c0, n = (c - 1, 2) if pair else (c, 1)
+                if path[c] != "V":
+                    act(ch("D" if path[c] == "S" else "Xb", c0, n), ch("D", c0, n), AF.Abs)
+                    if h or c0:
+                        behind("sign")
+                if path[c] == "S":
+                    act(ch("D", c0, n), ch("D", c0, n), AF.Abs, bias=-1032.25)
+                    act(ch("NM", c0, n), ch("D", c0, n), AF.Sign, bias=-1024.0)
+                    mark("sign")
+                elif path[c] == "M":
+                    mark("sign")
+                    ts(ch("Xb", c0, n), ch("Xb", c0, n), 3000.0, ALU.min, 262144.0 + 1016.0, ALU.add)
+                    act(ch("NM", c0, n), ch("Xb", c0, n), AF.Square, bias=-129.0, scale=2.0 ** -11)
+                else:
+                    ts(ch("NM", c0, n), ch("Xb", c0, n), C16, ALU.add, C16, ALU.is_equal)
+                    ts(ch("NM2", c0, n), ch("Xb", c0, n), C4096, ALU.add, C4096, ALU.is_equal)
+            key = "key%d" % h
+            mm(B(key, 0, 16 * nk), B("idb"), H("rA"), True, False)
+            mm(B(key, 0, 16 * nk), B("idf"), H("ef"), False, False)
+            runs = []
+            for c in range(len(path)):
+                if runs and path[runs[-1][0]] == path[c] and cw * (runs[-1][1] + 1) <= 64:
+                    runs[-1][1] += 1
+                else:
+                    runs.append([c, 1])
+            todo = []
+            for c, n in runs:
+                for z, src in {"S": [("zS", "NM")], "M": [("zM", "NM")], "V": [("zM", "NM"), ("zP", "NM2")]}[path[c]]:
+                    for p in range(16):
+                        todo.append((B(key, cw * c, cw * (c + n)), slide(z, p), B(src, 16 * (lo + cw * c) + p, 16 * (lo + cw * (c + n)), 16)))
+            for i, (o, l, r) in enumerate(todo):
+                mm(o, l, r, False, i == len(todo) - 1)
+            cp(B("mxa", 0, 8 * nk), B(key, 0, 8 * nk))
+            behind("keys" if h else "lanes", AHEAD[0 if h else 2])
+            mark("keys")
+            tt(B("mxb", 0, 8 * nk), B(key, 8 * nk, 16 * nk), B("mxa", 0, 8 * nk), ALU.max)
+            tt(B("m2", 0, 4 * nk), B("mxb", 0, 4 * nk), B("mxb", 4 * nk, 8 * nk), ALU.max)
+            tt(B("m3", 0, 2 * nk), B("m2", 0, 2 * nk), B("m2", 2 * nk, 4 * nk), ALU.max)
+            tt(B("ky", k0, k1), B("m3", 0, nk), B("m3", nk, 2 * nk), ALU.max)
+            ts(B("er", k0, k1), B("ky", k0, k1), 1023, ALU.bitwise_and)
+            cp(B("e16", k0, k1), B("er", k0, k1))
+            cp(B("erf", k0, k1), B("er", k0, k1))
+            e = B("e16", k0, k1)
+            pick(H("ebc"), B("iot"), e)
+            mm(H("pcp"), B("zer", 0, 128), H("zer"), True, False)
+            for k in range(k1):
+                a = max(16 * k, lo)
+                ts(B("EQ", 240 * k + a, 240 * k + hi), B("ebc", a, hi), B("erf", k, k + 1), ALU.is_equal)
+                a = max(16 * k + 16, lo)
+                if a < hi:
+                    mm(B("pcp", a, hi), B("blk"), B("EQ", 240 * k + a, 240 * k + hi), False, False)
+            for x in range(16):
+                mm(B("pcp", lo + x, hi - 15 + x, 16), B("tri", 128 * x, 128 * x + 128), B("EQ", 256 * k0 + x, 256 * k1 - 255 + x, 256), False, x == 15)
+            act(H("fl"), H("pcp"), AF.Sign, accum=B("wacc", h, h + 1))
+            c2, pos, sel = B("c2", k0, k1), B("sb%d" % t, 256 + k0, 256 + k1), B("sel", k0, k1)
             for p in range(16):
-                mm(o, B("sel", 128 * p, 128 * p + 128), B("NM", 1024 * c + p, 1024 * c + 1024, 16), False, p == 15)
-            if c == 0:
-                cp(B("mx"), o)
-            else:
-                tt(B("mx"), o, B("mx"), ALU.max)
-        tt(B("m2"), B("mx", 0, 32), B("mx", 32, 64), ALU.max)
-        tt(B("ky"), B("m2", 0, 16), B("m2", 16, 32), ALU.max)
-        ts(B("kk"), B("ky"), 255, ALU.bitwise_and)
-        tt(B("ku"), u, B("kk"), ALU.mult)
-        tt(B("es"), s, B("ku"), ALU.add)
-        ts(B("er"), B("es"), 1023, ALU.bitwise_and)
-        cp(B("e16"), B("er"))
-        cp(B("erf"), B("er"))
-        pc = B("pc", 0, 256)
-        pick(B("ebc"), B("iot"), B("e16"))
-        mm(pc, B("zer", 0, 128), B("zer"), True, False)
-        for k in range(16):
-            ts(B("EQ", 256 * k, 240 * k + 256), B("ebc", 16 * k, 256), None, ALU.is_equal, sc=B("erf", k, k + 1))
-            if k < 15:
-                mm(B("pc", 16 * k + 16, 256), B("blkb"), B("EQ", 256 * k + 16, 240 * k + 256), False, False)
-        for x in range(16):
-            mm(B("pc", x, 241 + x, 16), B("tri", 128 * x, 128 * x + 128), B("EQ", x, 3841 + x, 256), False, x == 15)
-        act(B("wnp"), pc, AF.Relu, bias=P24, scale=-1.0, accum=B("wacc"))
-        if t < NR - 1:
-            mm(B("pu", 32, 33), B("allf"), B("wacc"), True, True)
-            cp(B("ti"), B("pu", 32, 33))
-            ts(B("sc%d" % t), B("ti"), 31, ALU.bitwise_and)
-            send("c", t)
-        pick(B("bI"), RT, B("e16"))
-        pick(B("qb"), Ct, B("e16"), B("bI"), ALU.add)
-        ts(B("zb"), B("qb"), 0x3801F, ALU.bitwise_and)
-        ts(B("l5b"), B("qb"), 31, ALU.bitwise_and)
-        ts(B("v1"), B("l5b"), float(5 + t), ALU.is_le, EMP, ALU.mult)
-        ts(B("v3"), B("zb"), float(5 + t), ALU.is_gt, P24, ALU.mult)
-        tt(B("v2"), B("v1"), B("bI"), ALU.max)
-        tt(B("bs"), B("v3"), B("bI"), ALU.add)
-        tt(B("bPp"), B("v2"), B("bs"), ALU.min)
-        tt(B("dp"), B("bPp"), B("aP"), ALU.subtract)
-        act(B("Xd"), B("dp"), AF.Abs)
-        act(B("nsp"), B("Xd"), AF.Relu, bias=-2047.5 * P24, scale=P24)
-        act(B("cbp"), B("bPp"), AF.Identity, bias=EMP * 2048.0, scale=-2048.0)
-        ts(B("itb"), B("bI"), 16, ALU.bitwise_and)
-        tt(B("zdb"), B("v3"), B("zb"), ALU.subtract)
-        act(B("dbp"), B("zdb"), AF.Relu, bias=7.0 / 16, scale=-1.0 / 16)
-        tt(B("pb"), B("dbp"), B("ita"), ALU.mult)
-        tt(B("wbx"), B("bPp"), B("pb"), ALU.subtract)
-        tt(B("v5"), B("dap"), B("itb"), ALU.mult)
-        tt(B("v4"), B("aP"), B("v5"), ALU.subtract)
-        tt(B("rr"), B("v4"), B("wbx"), ALU.min)
-        tt(B("na1"), B("v2"), B("ca"), ALU.add)
-        tt(B("nb1"), B("cbp"), B("aw"), ALU.add)
-        tt(B("a1"), B("wnp"), A, ALU.max)
-        tt(B("v6"), B("nsp"), B("rr"), ALU.add)
-        tt(B("nbA"), B("v6"), B("nb1"), ALU.min)
-        tt(B("nb"), B("bPp"), B("nbA"), ALU.min)
-        tt(B("v5"), B("v6"), B("aP"), ALU.min)
-        tt(B("na3"), B("v5"), B("na1"), ALU.min)
-        tt(B("v2"), pc, B("na3"), ALU.max)
-        tt(B("sn%d" % t), B("v2"), B("a1"), ALU.min)
-        send("n", t)
-        tt(B("px"), pc, B("DM"), ALU.min)
-        scan(B("ps"), B("sgm", 0, 256), B("px"))
-        tt(B("pf"), B("erf"), B("ps", 15, 256, 16), ALU.max)
-        cp(B("pos"), B("pf"))
-        iota(lanes(t), [[0, 256]], 0, 0)
-        scatter(B("R"), B("pos"), B("nb"))
+                mm(c2, slide("z1", p), B("fl", lo + p, hi - 15 + p, 16), p == 0, p == 15)
+            tt(B("pm", k0, k1), c2, B("lbl", k0, k1), ALU.min)
+            tt(pos, B("pm", k0, k1), B("erf", k0, k1), ALU.max)
+            tt(B("sl", k0, k1), c2, B("lbl8", k0, k1), ALU.add)
+            ts(sel, B("sl", k0, k1), 0.0625, ALU.mult)
+            w0, w1, w2, w3, ns, cb = [H(n) for n in ("w0", "w1", "w2", "w3", "ns", "cb")]
+            act(H("bF"), RT, AF.Copy, by=e)
+            pick(H("qb"), B("Ct"), e, H("bF"), ALU.add)
+            ts(H("zb"), H("qb"), 0x3801F, ALU.bitwise_and)
+            ts(H("l5b"), H("qb"), 31, ALU.bitwise_and)
+            ts(w1, H("zb"), tau, ALU.is_le)
+            ts(w0, H("l5b"), tau, ALU.is_gt)
+            tt(H("bk"), w1, H("bF"), ALU.mult)
+            tt(w0, w0, H("bF"), ALU.mult)
+            tt(w3, w0, H("bk"), ALU.max)
+            tt(H("dp"), w3, H("aP"), ALU.subtract)
+            act(cb, w3, AF.Relu, bias=-15.5 * 16384, scale=16384.0)
+            act(H("dp"), H("dp"), AF.Abs)
+            act(ns, H("dp"), AF.Relu, bias=-2047.5 * BIG, scale=BIG)
+            ts(H("bkc"), H("bk"), -16, ALU.bitwise_and)
+            tt(H("wbx"), H("Ia"), H("bkc"), ALU.add)
+            ts(w2, H("l5b"), 16.0, ALU.is_lt, -BIG, ALU.mult)
+            tt(w2, w2, H("akc"), ALU.add)
+            tt(w2, w2, H("wbx"), ALU.max)
+            tt(H("r1"), w2, H("aP"), ALU.max)
+            tt(H("rr"), w3, H("r1"), ALU.max)
+            tt(H("tb"), H("aw"), cb, ALU.subtract)
+            tt(H("xb"), w3, H("tb"), ALU.max)
+            tt(w1, H("rr"), ns, ALU.subtract)
+            tt(H("nb") if last else H("sb%d" % t), w1, H("xb"), ALU.max)
+            tt(w0, w0, H("ca"), ALU.subtract)
+            tt(H("xa"), w0, H("aP"), ALU.max)
+            Wn = B("W", 256 * h, 256 * h + 128)
+            tt(H("na") if last else Wn, w1, H("xa"), ALU.max)
+            if h:
+                behind("met", AHEAD[1])
+            mark("met")
+            if last:
+                decode(H("sb%d" % t), H("nb"), ns, lo)
+                decode(Wn, H("na"), cb, lo)
+            act(H("sa%d" % t), B("W", 256 * h, 256 * h + 256), AF.Copy, by=sel)
+            for m in "ab":
+                send("%s%d%d" % (m, t, h))
+                if h:
+                    behind("%s%d0" % (m, t), AHEAD[3])
+            if not last:
+                cp(B("pos", k0, k1), pos)
+                scatter(B("LB"), B("pos", k0, k1), H("sb%d" % t))
+                if h:
+                    behind("scatter", AHEAD[3])
+                mark("scatter")
+        if not last:
+            for h in range(2):
+                mm(B("cnt"), B("allf"), B("wacc", h, h + 1), h == 0, h == 1)
+            cp(B("ti"), B("cnt"))
+            ts(B("ta"), B("ti"), 31, ALU.bitwise_and)
+            ts(B("sc%d" % t), B("ta"), -13.0 / 32, ALU.add)
+            send("c%d" % t)
+            act(B("ctp"), cls("Ct", t + 1), AF.Copy)
 
-    def decode(c):
-        r = lanes(c)
-        v, w = ("v1", "v3") if c % 2 else ("v5", "v6")
-        ts(B("hi"), r, -4096, ALU.bitwise_and)
-        ts(B(w), r, EMP, ALU.is_lt)
-        ts(B(v), B("hi"), 1.5, ALU.mult)
-        tt(B("xo"), B(v), r, ALU.subtract)
-        tt(B("yo", c, 1021 + c, 4), B(w), B("xo"), ALU.mult)
-    last = (NR - 1) % 4
+    expect("T%d" % NR)
     for c in range(4):
-        if c != last:
-            decode(c)
-    own(NR - 1)
-    decode(last)
-    put("dma", "y", lambda e: e.dma_start(T.yent[:], T.yo[:]), [B("yo")], [], 4.5, sem="st")
+        decode(B("yo", 256 * c, 256 * c + 256), B("TB4", 256 * c, 256 * c + 256), B("Ap" if c % 2 else "ctp"), 0)
+    complete(NR, "yo")
+    put("dma", "y", lambda e: e.dma_start(T.yent[:], ap(B("yo", 0, 1024))), [B("yo")], [], 4.5, sem="st", inc=16)
     return ops
 
 
@@ -509,6 +688,7 @@ def rank_program(g, core, T, topo):
     if rank is None:
         hand_on(g, core, T, topo)
         return
+    n = len(T.cores)
     ops = record(T)
     pre, seq, _ = plan(T)
     eng = {"v": g.vector, "s": g.scalar, "p": g.tensor, "g": g, "y": g.sync}
@@ -518,12 +698,9 @@ def rank_program(g, core, T, topo):
         o = ops[i]
         q = o["q"]
         if o["kind"] == "land":
-            m, t = o["msg"]
-            src = T.cores[source(T, rank, m, t)]
-            n = 0
-            for rl, lo, hi in route(topo, T, src, core, m, t):
-                n += bits(topo.mask(src if rl is None else rl, core))
-            tok[i] = ("%s%d" % (m, t), n)
+            m = o["msg"]
+            src = T.cores[(rank - MSG[m][3]) % n]
+            tok[i] = (m, sum(bits(topo.mask(((src,) + chain)[-1], core)) for chain, lo, hi in route(topo, T, src, core, m)))
             continue
         need = {}
         for j in pre[i]:
@@ -540,17 +717,16 @@ def rank_program(g, core, T, topo):
             tok[i] = ("q" + q, cnt[q])
             o["fn"](eng[q]).then_inc(T.sem["q" + q], 1)
         elif o["kind"] == "dma":
-            tok[i] = (o["sem"], 16)
+            tok[i] = (o["sem"], o["inc"])
             o["fn"](eng[q]).then_inc(T.sem[o["sem"]], 16)
         else:
-            m, t = o["msg"]
-            dst = T.cores[target(T, rank, m, t)]
-            s, l, at = T["s" + m], T["l" + m], STEP[m] * t
-            for rl, lo, hi in route(topo, T, core, dst, m, t):
-                to = dst if rl is None else rl
+            m = o["msg"]
+            dst = T.cores[(rank + MSG[m][3]) % n]
+            for chain, lo, hi in route(topo, T, core, dst, m):
+                to = (chain + (dst,))[0]
                 rid, pid = topo.addr(to, core)
                 mk = topo.mask(core, to)
-                g.remote_dma(l[:, at + lo:at + hi], s[:, at + lo:at + hi], T.sem["%s%d" % (m, t)], T.sem.lsem, pid, rid, mk)
+                g.remote_dma(view(T, MSG[m][1], lo, hi), view(T, MSG[m][0], lo, hi), T.sem[m], T.sem.lsem, pid, rid, mk)
                 sent += bits(mk)
             continue
         snaps[tok[i]] = dict(known[q])

@@ -1,17 +1,24 @@
-from concourse.mybir import AluOpType as ALU, ActivationFunctionType as AF
+from concourse.mybir import AluOpType as ALU, ActivationFunctionType as AF, AxisListType
 
 NR = 4
 BIG = float(1 << 24)
 C16, C4096, C1 = 1.5 * (1 << 27), 1.5 * (1 << 35), 1.5 * (1 << 23)
 FV = (1, 3, 5)
 PARTS = ((0, 8, "SSVV"), (8, 16, "SSVV"))
-AHEAD = (2.0, 3.0, 4.0, 2.5)
+AHEAD = (2.5, 2.5, 0.0, 1.5, 2.0)
 HP = 1.5 * (1 << 22)
 SHIFT = {"S": 0.0, "M": 131072.0, "V": -131072.0}
-LAT = {"A": 8.0, "U": 5.0, "T": 14.0, "f": 14.0, "b": 6.0, "a": 6.0, "c": 5.0}
-WAKE = 0.1
-FIX, FIXS = 0.005, 0.05
+LAT = {"A": 6.0, "U": 4.2, "T": 14.0, "f": 14.0, "b": 5.5, "a": 5.5, "c": 4.7}
+WAKE = 0.2
+FIX, FIXS = 0.0, 0.0
 FIXP, SAME = 0.0, 0.25
+CY, G, SC, CALL = 0.00083, 1.3, 3.8, 0.7
+VFIRST = 2
+GCP = False
+SAMEV = (0, 1)
+TWICE = True
+PICKS = None
+JOG, TRIES = 0.5, 250
 WIDE = 2
 PASSES = 6
 
@@ -32,18 +39,18 @@ def _ps(bank, **views):
         PART[n] = (bank, views[n][0], views[n][1], bank)
 
 
-_sb("int32", entx=1024, wti=1, kpi=1, ci=1024, pmi=16, pmj=16, lpi=16, n1=512, q=256, k1=256, za=256, l5a=256, ui=16, ub=16, uq=16,
-    ei=256, em=256, ky=16, er=16, ti=1, ta=1, qb=256, zb=256, l5b=256, bk=256, bkc=256)
+_sb("int32", entx=1024, wti=1, kpi=1, ci=1024, pmi=16, pmj=16, n1=512, q=256, k1=256, za=256, l5a=256, ui=16, ub=16, uq=16,
+    ei=256, em=256, ky=16, er=16, qb=256, zb=256, l5b=256, bk=256, bkc=256)
 _sb("bfloat16", fx0=2064, fx2=2064, fx3=2064, one=128, blka=128, blk=128, idb=128, hid=128, zer=256, zz=720, tri=2048, dlt=16, rA=256, rK=16,
     sgm=512, fl=256, sgs=256, sgk=256, Yg=4096, Ys=4096, Xb=4096, NM=4096, NM2=4096, EQ=4096)
-_sb("uint16", lstP=16, lstI=16, off=256, eu=256, e16=16, ebc=256, pos=16, pos2=16, sel=16)
+_sb("uint16", lstP=8, lstI=16, off=256, eu=256, e16=16, ebc=256, pos=16, pos2=16, sel=16)
 _sb("float32", TB0=1280, TB1=1280, TB2=1280, TB3=1280, TB4=1024, LB=1280, yo=1280, Ct=1024, iot=1024, D=4096, idf=128, allf=128, pmf=16,
-    x16=16, cmk=16, lI=16, lbl=16, lbl8=16, mio=256, wk=2, pr=256, x1=256, oc=256, oT=1536, aw=256, aP=256, akc=256, ca=256, sU=48, lU=48, uk=48,
-    sA=256, lA=256, iap=256, ef=256, mxa=128, mxb=128, m2=64, m3=32, erf=16, wacc=2, pm=16, sl=16, bF=256, dp=256, wbx=256, r1=256, rr=256, tb=256, xb=256, xa=256,
-    W=512, nb=256, na=256, d1=256, d2=256)
+    x16=16, cmk=16, lI=16, lbl=16, lbl8=16, mio=256, wk=2, pr=256, x1=256, oc=256, oT=1536, aw=256, aP=256, gk=256, gs=256, ibp=256, kyf=16, ca=256, sU=48, lU=48, uk=48,
+    sA=256, lA=256, iap=256, ef=256, mxa=128, mxb=128, m2=64, m3=32, erf=16, wacc=3, ta=1, pm=16, sl=16, bF=256, dp=256, wbx=256, r1=256, rr=256, tb=256, xb=256, xa=256,
+    W=512, nb=256, na=256, d1=512, d2=512, ep=256, lpf=2)
 for _t in range(NR):
     _sb("float32", **{"sb%d" % _t: 272, "lb%d" % _t: 272, "sa%d" % _t: 256, "la%d" % _t: 256, "sc%d" % _t: 1, "lc%d" % _t: 1})
-_ps("pu", up=(0, 16), cnt=(32, 1), c2=(64, 16), kmp=(256, 16))
+_ps("pu", up=(0, 16), cnt=(32, 1), c2=(64, 16), kmp=(128, 16), spare=(256, 256))
 _ps("pk0", key0=(0, 512))
 _ps("pk1", key1=(0, 512))
 _ps("pc", pcp=(0, 256), ctp=(256, 256))
@@ -66,8 +73,8 @@ def messages(n):
         for name in (src, dst):
             PART[name + m] = (PART[name][0], PART[name][1] + lo, hi - lo, name)
         out[m] = (src + m, dst + m, hi - lo, by, kind)
-    piece("U", "sU", "lU", 0, 48, -x[0], "c")
     for h in range(2):
+        piece("U%d" % h, "sU", "lU", 32 * h, 32 + 16 * h, -x[0], "cb"[h])
         piece("A%d" % h, "sA", "lA", 128 * h, 128 * h + 128, -x[0], "ba"[h])
     for t in range(NR):
         piece("T%d" % (t + 1), "TB%d" % t, "TB%d" % (t + 1), 0, 1024, hold[t] - hold[t + 1], "T")
@@ -205,9 +212,10 @@ def arrange(ops, pre, wake):
 
     def place(edges, back, key):
         left, est, start, busy = [len(b) for b in back], [0.0] * n, [0.0] * n, {}
+        rank = {i: r for r, i in enumerate(sorted(range(n), key=key))}
         ready = [i for i in range(n) if not left[i]]
         while ready:
-            i = min(ready, key=key)
+            i = min(ready, key=rank.get)
             ready.remove(i)
             t = est[i]
             if ops[i]["kind"] in ("run", "send"):
@@ -237,13 +245,23 @@ def arrange(ops, pre, wake):
     for i in range(n - 1, -1, -1):
         for j, lag in bwd[i]:
             late[j] = max(late[j], late[i] + lag)
-    best = None
-    for _ in range(PASSES):
+    best, seed = None, 1
+    for turn in range(PASSES + TRIES):
+        bias = {}
+        if turn >= PASSES:
+            late = best[2]
+            for i in range(n):
+                if ops[i]["role"] not in bias:
+                    seed = (seed * 1103515245 + 12345) % 2147483648
+                    bias[ops[i]["role"]] = JOG * (seed % 2001 - 1000) / 1000 if seed >> 16 & 7 == 0 else 0.0
+            start = place(fwd, bwd, lambda i: (bias[ops[i]["role"]] - late[i] - dur[i], i))
+            late = place(bwd, fwd, lambda i: (-start[i] - dur[i], -i))
         start = place(fwd, bwd, lambda i: (-late[i] - dur[i], i))
         end = max(start[i] + dur[i] for i in range(n))
         if best is None or end < best[0]:
-            best = (end, start)
-        late = place(bwd, fwd, lambda i: (-start[i] - dur[i], -i))
+            best = (end, start, late)
+        if turn < PASSES:
+            late = place(bwd, fwd, lambda i: (-start[i] - dur[i], -i))
     ORDER["end"] = best[0]
     seq, seen = sorted(range(n), key=lambda i: (best[1][i], i)), {}
     for i in seq:
@@ -254,12 +272,14 @@ def arrange(ops, pre, wake):
 
 
 def record(T):
-    ops, where = [], {}
-    CY, G, SC = 0.00085, 1.55, 3.8
+    ops, where, seen = [], {}, {}
 
     def put(kind, q, fn, r, w, dur, after=(), **more):
         d = {"kind": kind, "q": q, "fn": fn, "r": list(r), "w": list(w), "dur": dur, "after": list(after), "behind": []}
         d.update(more)
+        key = (q,) + tuple((w or r or [(kind, 0, 0, 0, kind)])[0][1:3]) + ((w or r or [(kind, 0, 0, 0, kind)])[0][4].rstrip("0123"),)
+        seen[key] = seen.get(key, 0) + 1
+        d["role"] = key + (seen[key],)
         ops.append(d)
 
     def mark(name):
@@ -293,6 +313,9 @@ def record(T):
 
     def cp(o, a):
         put("run", "v", lambda e: e.tensor_copy(ap(o), ap(a)), [a], [o], vd(width(a), two(o, a)))
+
+    def most(o, a):
+        put("run", "v", lambda e: e.tensor_reduce(ap(o), ap(a), AxisListType.X, ALU.max), [a], [o], vd(width(a)))
 
     def ms(o, c):
         put("run", "v", lambda e: e.memset(ap(o), c), [], [o], vd(width(o), two(o)))
@@ -341,13 +364,16 @@ def record(T):
 
     def send(m, after=()):
         where[m] = len(ops)
-        put("send", "g", None, [B(MSG[m][0], 0, MSG[m][2])] + list(after), [], 2.1 if m[0] in "Tf" else 0.7, msg=m)
+        put("send", "g", None, [B(MSG[m][0], 0, MSG[m][2])] + list(after), [], 3 * CALL if m[0] in "Tf" else CALL, msg=m)
 
     def expect(m):
         put("land", None, None, [], [B(MSG[m][1], 0, MSG[m][2])], LAT[m[0]], [where[m]], msg=m)
 
     def cls(name, c):
         return B(name, c, 1021 + c, 4)
+
+    def half(x, h):
+        return (x[0], x[1] + 128 * h * x[3], x[1] + (128 * h + 127) * x[3] + 1) + x[3:]
 
     def slide(name, p):
         return B(name, 15 - p, 143 - p)
@@ -364,7 +390,6 @@ def record(T):
     cp(B("fx0", 2057, 2058), B("kpi"))
     ms(B("one"), 1.0)
     iota(B("ci"), [[37, 1024]], 0, 0)
-    iota(B("lpi"), [[1, 16]], 0, 16)
     iota(B("pmi"), [[0, 16]], 0, 1)
     iota(B("x16"), [[1, 16]], 0, 0)
     for k0, k1, path in PARTS:
@@ -375,15 +400,17 @@ def record(T):
     ms(B("zz"), 0.0)
     ms(B("zer"), 0.0)
     ms(B("allf"), -1.0 / 16)
+    ms(B("wacc", 2, 3), 15.5 / 8)
     ms(B("sgm"), 1.0)
     cp(B("sgm", 0, 497, 16), B("zer", 0, 32))
     ts(B("ci"), B("ci"), 63, ALU.bitwise_and)
     ts(B("Ct"), B("ci"), 4096.0, ALU.mult, 262144.0 - 2048.0, ALU.add)
-    ts(B("lpi"), B("lpi"), 255, ALU.bitwise_and)
-    cp(B("lstP"), B("lpi"))
     ts(B("pmj"), B("pmi"), 15, ALU.bitwise_and)
     cp(B("pmf"), B("pmj"))
     pm = B("pmf", 0, 1)
+    ts(B("lpf", 0, 1), pm, 7.5, ALU.is_gt, -127.0, ALU.mult)
+    ts(B("lpf", 1, 2), pm, 16.0, ALU.mult, B("lpf", 0, 1), ALU.add)
+    ts(B("lstP"), B("x16", 0, 8), 2.0, ALU.mult, B("lpf", 1, 2), ALU.add)
     ts(B("lI"), B("x16"), 16.0, ALU.mult, pm, ALU.add)
     cp(B("lstI"), B("lI"))
     ts(B("lbl"), B("lI"), 1024.0, ALU.add)
@@ -408,7 +435,10 @@ def record(T):
         ts(n1, x, 2.0 ** -11, ALU.mult, 0.5 - 2.0 ** -12, ALU.add)
         ts(w, n1, 2048.0, ALU.mult, 15.0, ALU.add)
         tt(o, w, x, ALU.add)
+    ts(B("q"), cls("entx", 0), 15.0, ALU.add)
     convert(B("sA"), cls("entx", 0), "u0")
+    ts(B("k1"), B("q"), 16, ALU.bitwise_and)
+    tt(B("pr"), B("n1", 0, 256), B("k1"), ALU.mult)
     for h in range(2):
         send("A%d" % h)
     iota(B("iot"), [[1, 1024]], 0, 0)
@@ -425,7 +455,7 @@ def record(T):
         for h, (k0, k1, path) in enumerate(PARTS):
             expect("a%d%d" % (t - 1, h))
             o, a = B(name, 64 * k0 + t - 1, 64 * k1 + t - 4, 4), B("la%d" % (t - 1), 16 * k0, 16 * k1)
-            if t < NR:
+            if t < NR and (h == 0 or GCP):
                 gcp(o, a)
             else:
                 act(o, a, AF.Copy)
@@ -437,48 +467,56 @@ def record(T):
     act(B("ctp"), cls("Ct", 0), AF.Copy)
     for t in range(NR):
         last = t == NR - 1
+        seen.clear()
         A, fx, TB, U = cls("LB", t) if t else B("sA"), "fx%d" % (t if t > 1 else 0), "TB%d" % t, "uk" if t else "sU"
         tau, clock = 5.0 + t, 12.0 + t
         if t > 1:
             expect("f%d" % t)
         if t != 1:
-            cp(B("wk"), B(fx, 2056, 2058))
+            act(B("wk"), B(fx, 2056, 2058), AF.Copy)
             if t:
                 behind("scatter")
-            ts(B("zw", 15, 128, 16), B("blk", 0, 113, 16), B("wk", 0, 1), ALU.mult)
-            ts(B("rK"), B("dlt"), B("wk", 1, 2), ALU.mult)
+            act(B("zw", 15, 128, 16), B("blk", 0, 113, 16), AF.Copy, scale=B("wk", 0, 1))
+            act(B("rK"), B("dlt"), AF.Copy, scale=B("wk", 1, 2))
             mm(B("kmp"), B("blk"), B("rK"), True, True)
-        cp(B(U, 32, 48), B("kmp"))
-        tt(B("q"), B("ctp"), A, ALU.add)
-        act(B("Ap"), A, AF.Copy)
-        ts(B("k1"), B("q"), 16, ALU.bitwise_and)
-        tt(B("pr"), B("Ap"), B("k1"), ALU.mult)
-        for lo, hi in ((0, 4), (4, 16)):
-            ts(B("off", 16 * lo, 16 * hi), B("pr"), 2.0 ** -16, ALU.mult, 127.0 / 256, ALU.add, by=B("lstP", lo, hi))
-        for c in range(8):
-            o, l = B("Yg", 512 * c, 512 * c + 512), B("off", 32 * c, 32 * c + 32)
-            if c in FV:
-                pick(o, B(fx, 0, 2049), l)
-            else:
-                act(o, B(fx, 0, 2049), AF.Copy, by=l)
-            scan(B("Ys", 512 * c, 512 * c + 512), B("sgm"), o)
-            for p in (2 * c, 2 * c + 1):
-                mm(B("up"), slide("zw", p), B("Ys", 256 * p + 15, 256 * p + 256, 16), p == 0, p == 15)
-        cp(B("ui"), B("up"))
-        ts(B("ub"), B("ui"), 4095, ALU.bitwise_and)
-        tt(B("uq"), B("ub"), B("ub"), ALU.mult)
+        act(B(U, 16, 32), B("kmp"), AF.Copy)
         if t:
             expect("c%d" % (t - 1))
-        cp(B(U, 0, 16), B("ub"))
-        ts(B(U, 16, 32), B("uq"), 2.0 ** -5, ALU.mult, B("lc%d" % (t - 1)) if t else -13.0 / 32, ALU.add)
+        for h in range(2):
+            lo, hi, k0, k1 = 128 * h, 128 * h + 128, 8 * h, 8 * h + 8
+            if t:
+                tt(B("q", lo, hi), B("ctp", lo, hi), half(A, h), ALU.add)
+                act(B("Ap", lo, hi), half(A, h), AF.Copy)
+                ts(B("k1", lo, hi), B("q", lo, hi), 16, ALU.bitwise_and)
+                tt(B("pr", lo, hi), B("Ap", lo, hi), B("k1", lo, hi), ALU.mult)
+            ts(B("off", lo, hi), B("pr", lo, hi), 2.0 ** (-16 if t else -4), ALU.mult, 127.0 / 256 if t else 0.0, ALU.add, by=B("lstP"))
+            for c in range(4 * h, 4 * h + 4):
+                o, l = B("Yg", 512 * c, 512 * c + 512), B("off", 32 * c, 32 * c + 32)
+                if c in FV:
+                    pick(o, B(fx, 0, 2049), l)
+                else:
+                    act(o, B(fx, 0, 2049), AF.Copy, by=l)
+                scan(B("Ys", 512 * c, 512 * c + 512), B("sgm"), o)
+                for p in range(4 * (c % 4), 4 * (c % 4) + 4):
+                    mm(B("up", k0, k1), slide("zw", p), B("Ys", 16 * lo + 128 * p + 15, 16 * lo + 128 * p + 128, 16), p == 0, p == 15)
+            cp(B("ui", k0, k1), B("up", k0, k1))
+            if h:
+                behind("sum", AHEAD[4])
+            mark("sum")
+            ts(B("ub", k0, k1), B("ui", k0, k1), 4095, ALU.bitwise_and)
+            tt(B("uq", k0, k1), B("ub", k0, k1), B("ub", k0, k1), ALU.mult)
+            cp(B(U, 32 * h, 32 * h + 8), B("ub", k0, k1))
+            ts(B(U, 32 * h + 8, 32 * h + 16), B("uq", k0, k1), 2.0 ** -5, ALU.mult, (15.5 if t else 0.0) - 13.0 / 32, ALU.add)
+            if not t:
+                send("U%d" % h)
         if not t:
-            send("U")
             for h in range(2):
                 expect("A%d" % h)
             A, U = B("lA"), "lU"
             tt(B("q"), B("ctp"), A, ALU.add)
         act(B("x1"), A, AF.Identity, bias=-7.5)
-        ts(B("oc"), B("x1"), C16, ALU.add, C16, ALU.subtract)
+        act(B("x1"), B("x1"), AF.Identity, bias=C16)
+        act(B("oc"), B("x1"), AF.Identity, bias=-C16)
         for h, (k0, k1, path) in enumerate(PARTS):
             n, reps = 16 * (k1 - k0), 16 // len(path)
             first = 1 if t else reps
@@ -497,24 +535,25 @@ def record(T):
             for s in signs:
                 mm(B(o), B("hid"), B(s), False, s == signs[-1])
         act(B("aw"), B("w0"), AF.Relu, bias=-HP)
-        act(B("akc"), B("w2"), AF.Identity, bias=clock - HP)
-        act(B("aP"), B("w1"), AF.Copy)
+        act(B("Ap"), B("w2"), AF.Identity, bias=clock - HP)
+        act(B("aP"), B("w1"), AF.Relu)
         act(B("ca"), B("w1"), AF.Relu, bias=-15.5 * 16384, scale=16384.0)
         mark("lanes")
         act(B("iap"), B("l5a"), AF.Relu, bias=31 * BIG, scale=-2 * BIG, by=ID)
         act(B("Ia"), B("iap"), AF.Identity, bias=clock, scale=-1.0)
         if last:
-            decode(B("x1"), A, B("Ap"), 0)
+            decode(B("x1"), A, B("ctp"), 0)
             A = B("x1")
         for h in range(2):
-            gcp(B("W", 256 * h + 128, 256 * h + 256), (A[0], A[1] + 128 * h * A[3], A[1] + (128 * h + 127) * A[3] + 1) + A[3:])
+            gcp(B("W", 256 * h + 128, 256 * h + 256), half(A, h))
         if t:
             expect("T%d" % t)
             complete(t, TB)
         else:
             for j in range(2):
                 convert(B(TB, 512 * j, 512 * j + 512), B("entx", 512 * j, 512 * j + 512), "key%d" % j)
-            expect("U")
+            for h in range(2):
+                expect("U%d" % h)
         send("T%d" % (t + 1), [] if t else [B("lU")])
         if t + 2 < NR:
             send("f%d" % (t + 2))
@@ -533,7 +572,9 @@ def record(T):
             def ch(n, c, more=1):
                 return B(n, 16 * (lo + cw * c), 16 * (lo + cw * (c + more)))
             for k in range(k0, k1):
-                ts(B("ei", lo + k - k0, hi, nk), B(U, 32, 48), B(U, k, k + 1), ALU.mult, B(U, 16 + k, 17 + k), ALU.add)
+                u, s = B(U, 24 * h + k, 24 * h + k + 1), B(U, 24 * h + 8 + k, 24 * h + 9 + k)
+                act(B("ep", lo + k - k0, hi, nk), B(U, 16, 32), AF.Identity, bias=s, scale=u)
+            ts(H("ei"), H("ep"), B("lc%d" % (t - 1)) if t else 0.0, ALU.add)
             ts(H("em"), H("ei"), 1023, ALU.bitwise_and)
             cp(H("eu"), H("em"))
             act(H("ef"), H("em"), AF.Copy, by=B("lstI", 0, nk))
@@ -541,9 +582,15 @@ def record(T):
             for c in range(len(path)):
                 l = B("eu", lo + cw * c, lo + cw * c + cw)
                 pick(ch("Xb" if path[c] == "V" else "D", c), RT, l, own, ALU.subtract)
-                if h or c:
-                    behind("pick")
-                mark("pick")
+                if PICKS is None:
+                    if h or c:
+                        behind("pick")
+                    mark("pick")
+                else:
+                    mark("pick%d" % (4 * h + c))
+                    if 4 * h + c == 7:
+                        for i, j in zip(PICKS, PICKS[1:]):
+                            ops[where["pick%d" % j]]["behind"].append((where["pick%d" % i], 0.0))
                 pair = WIDE and path[c] == path[c ^ 1] and (h or c > 1 or WIDE > 1)
                 if pair and c % 2 == 0:
                     continue
@@ -563,6 +610,8 @@ def record(T):
                 else:
                     ts(ch("NM", c0, n), ch("Xb", c0, n), C16, ALU.add, C16, ALU.is_equal)
                     ts(ch("NM2", c0, n), ch("Xb", c0, n), C4096, ALU.add, C4096, ALU.is_equal)
+                    if VFIRST > 1:
+                        mark("pick")
             key = "key%d" % h
             mm(B(key, 0, 16 * nk), B("idb"), H("rA"), True, False)
             mm(B(key, 0, 16 * nk), B("idf"), H("ef"), False, False)
@@ -573,19 +622,17 @@ def record(T):
                 else:
                     runs.append([c, 1])
             todo = []
-            for c, n in runs:
+            for c, n in sorted(runs, key=lambda r: VFIRST and path[r[0]] != "V"):
                 for z, src in {"S": [("zS", "NM")], "M": [("zM", "NM")], "V": [("zM", "NM"), ("zP", "NM2")]}[path[c]]:
                     for p in range(16):
                         todo.append((B(key, cw * c, cw * (c + n)), slide(z, p), B(src, 16 * (lo + cw * c) + p, 16 * (lo + cw * (c + n)), 16)))
             for i, (o, l, r) in enumerate(todo):
                 mm(o, l, r, False, i == len(todo) - 1)
-            cp(B("mxa", 0, 8 * nk), B(key, 0, 8 * nk))
+            for k in range(k0, k1):
+                most(B("kyf", k, k + 1), B(key, k - k0, 16 * nk, nk))
             behind("keys" if h else "lanes", AHEAD[0 if h else 2])
             mark("keys")
-            tt(B("mxb", 0, 8 * nk), B(key, 8 * nk, 16 * nk), B("mxa", 0, 8 * nk), ALU.max)
-            tt(B("m2", 0, 4 * nk), B("mxb", 0, 4 * nk), B("mxb", 4 * nk, 8 * nk), ALU.max)
-            tt(B("m3", 0, 2 * nk), B("m2", 0, 2 * nk), B("m2", 2 * nk, 4 * nk), ALU.max)
-            tt(B("ky", k0, k1), B("m3", 0, nk), B("m3", nk, 2 * nk), ALU.max)
+            cp(B("ky", k0, k1), B("kyf", k0, k1))
             ts(B("er", k0, k1), B("ky", k0, k1), 1023, ALU.bitwise_and)
             cp(B("e16", k0, k1), B("er", k0, k1))
             cp(B("erf", k0, k1), B("er", k0, k1))
@@ -613,25 +660,30 @@ def record(T):
             pick(H("qb"), B("Ct"), e, H("bF"), ALU.add)
             ts(H("zb"), H("qb"), 0x3801F, ALU.bitwise_and)
             ts(H("l5b"), H("qb"), 31, ALU.bitwise_and)
-            ts(w1, H("zb"), tau, ALU.is_le)
-            ts(w0, H("l5b"), tau, ALU.is_gt)
-            tt(H("bk"), w1, H("bF"), ALU.mult)
-            tt(w0, w0, H("bF"), ALU.mult)
+            each = B("lstI", 0, nk)
+            act(w1, H("bF"), AF.Copy)
+            act(H("gk"), H("zb"), AF.Sign, bias=tau + 0.5, scale=-1.0, by=each)
+            act(H("gs"), H("l5b"), AF.Sign, bias=-tau - 0.5, by=each)
+            act(H("ibp"), H("l5b"), AF.Relu, bias=31 * BIG, scale=-2 * BIG, by=each)
+            tt(H("bk"), w1, H("gk"), ALU.mult)
+            tt(w0, w1, H("gs"), ALU.mult)
             tt(w3, w0, H("bk"), ALU.max)
             tt(H("dp"), w3, H("aP"), ALU.subtract)
             act(cb, w3, AF.Relu, bias=-15.5 * 16384, scale=16384.0)
-            act(H("dp"), H("dp"), AF.Abs)
-            act(ns, H("dp"), AF.Relu, bias=-2047.5 * BIG, scale=BIG)
+            if h in SAMEV:
+                ts(ns, H("dp"), C4096, ALU.add, C4096, ALU.is_equal)
+            else:
+                act(H("dp"), H("dp"), AF.Abs)
+                act(ns, H("dp"), AF.Relu, bias=-2047.5 * BIG, scale=BIG)
             ts(H("bkc"), H("bk"), -16, ALU.bitwise_and)
             tt(H("wbx"), H("Ia"), H("bkc"), ALU.add)
-            ts(w2, H("l5b"), 16.0, ALU.is_lt, -BIG, ALU.mult)
-            tt(w2, w2, H("akc"), ALU.add)
-            tt(w2, w2, H("wbx"), ALU.max)
+            tt(w2, H("Ap"), H("ibp"), ALU.subtract)
             tt(H("r1"), w2, H("aP"), ALU.max)
-            tt(H("rr"), w3, H("r1"), ALU.max)
+            tt(w2, w3, H("r1"), ALU.max)
+            tt(H("rr"), w2, H("wbx"), ALU.max)
             tt(H("tb"), H("aw"), cb, ALU.subtract)
             tt(H("xb"), w3, H("tb"), ALU.max)
-            tt(w1, H("rr"), ns, ALU.subtract)
+            tt(w1, H("rr"), ns, ALU.mult if h in SAMEV else ALU.subtract)
             tt(H("nb") if last else H("sb%d" % t), w1, H("xb"), ALU.max)
             tt(w0, w0, H("ca"), ALU.subtract)
             tt(H("xa"), w0, H("aP"), ALU.max)
@@ -648,24 +700,27 @@ def record(T):
                 send("%s%d%d" % (m, t, h))
                 if h:
                     behind("%s%d0" % (m, t), AHEAD[3])
-            if not last:
+            if not last and TWICE:
                 cp(B("pos", k0, k1), pos)
                 scatter(B("LB"), B("pos", k0, k1), H("sb%d" % t))
                 if h:
                     behind("scatter", AHEAD[3])
                 mark("scatter")
+            elif not last and h:
+                cp(B("pos"), B("sb%d" % t, 256, 272))
+                scatter(B("LB"), B("pos"), B("sb%d" % t, 0, 256))
+                mark("scatter")
         if not last:
-            for h in range(2):
-                mm(B("cnt"), B("allf"), B("wacc", h, h + 1), h == 0, h == 1)
-            cp(B("ti"), B("cnt"))
-            ts(B("ta"), B("ti"), 31, ALU.bitwise_and)
-            ts(B("sc%d" % t), B("ta"), -13.0 / 32, ALU.add)
+            for h in (2, 0, 1):
+                mm(B("cnt"), B("allf"), B("wacc", h, h + 1), h == 2, h == 1)
+            ts(B("ta"), B("cnt"), 2 * C16, ALU.add, 2 * C16, ALU.subtract)
+            tt(B("sc%d" % t), B("cnt"), B("ta"), ALU.subtract)
             send("c%d" % t)
             act(B("ctp"), cls("Ct", t + 1), AF.Copy)
 
     expect("T%d" % NR)
     for c in range(4):
-        decode(B("yo", 256 * c, 256 * c + 256), B("TB4", 256 * c, 256 * c + 256), B("Ap" if c % 2 else "ctp"), 0)
+        decode(B("yo", 256 * c, 256 * c + 256), B("TB4", 256 * c, 256 * c + 256), B("spare"), 256)
     complete(NR, "yo")
     put("dma", "y", lambda e: e.dma_start(T.yent[:], ap(B("yo", 0, 1024))), [B("yo")], [], 4.5, sem="st", inc=16)
     return ops

@@ -1,3 +1,5 @@
+import math
+from concourse.bass import DstId, RemoteDMATransfer
 from concourse.mybir import AluOpType as ALU, ActivationFunctionType as AF, AxisListType
 
 NR = 4
@@ -6,7 +8,7 @@ C16, C4096, C1 = 1.5 * (1 << 27), 1.5 * (1 << 35), 1.5 * (1 << 23)
 FV = (1, 3, 5)
 PARTS = ((0, 8, "SSVV"), (8, 16, "SSVV"))
 AHEAD = (2.5, 2.5, 0.0, 1.5, 2.0)
-HP = 1.5 * (1 << 22)
+PEN = 2 * BIG
 SHIFT = {"S": 0.0, "M": 131072.0, "V": -131072.0}
 LAT = {"A": 6.0, "U": 4.2, "T": 14.0, "f": 14.0, "b": 5.5, "a": 5.5, "c": 4.7}
 WAKE = 0.2
@@ -14,12 +16,13 @@ FIX, FIXS = 0.0, 0.0
 FIXP, SAME = 0.0, 0.25
 CY, G, SC, CALL = 0.00083, 1.3, 3.8, 0.7
 VFIRST = 2
-GCP = False
-SAMEV = (0, 1)
-TWICE = True
+SAMEV = (1,)
+EH, ROWS, GK = True, True, (0, 1)
+US, ES, JOINT = True, True, True
 PICKS = None
-JOG, TRIES = 0.5, 250
+JOG, TRIES = 0.5, 60
 WIDE = 2
+SWAPS, SLACK = 40000, 0.02
 PASSES = 6
 
 SCRATCH, PART = {}, {}
@@ -39,26 +42,38 @@ def _ps(bank, **views):
         PART[n] = (bank, views[n][0], views[n][1], bank)
 
 
-_sb("int32", entx=1024, wti=1, kpi=1, ci=1024, pmi=16, pmj=16, n1=512, q=256, k1=256, za=256, l5a=256, ui=16, ub=16, uq=16,
-    ei=256, em=256, ky=16, er=16, qb=256, zb=256, l5b=256, bk=256, bkc=256)
-_sb("bfloat16", fx0=2064, fx2=2064, fx3=2064, one=128, blka=128, blk=128, idb=128, hid=128, zer=256, zz=720, tri=2048, dlt=16, rA=256, rK=16,
-    sgm=512, fl=256, sgs=256, sgk=256, Yg=4096, Ys=4096, Xb=4096, NM=4096, NM2=4096, EQ=4096)
-_sb("uint16", lstP=8, lstI=16, off=256, eu=256, e16=16, ebc=256, pos=16, pos2=16, sel=16)
-_sb("float32", TB0=1280, TB1=1280, TB2=1280, TB3=1280, TB4=1024, LB=1280, yo=1280, Ct=1024, iot=1024, D=4096, idf=128, allf=128, pmf=16,
-    x16=16, cmk=16, lI=16, lbl=16, lbl8=16, mio=256, wk=2, pr=256, x1=256, oc=256, oT=1536, aw=256, aP=256, gk=256, gs=256, ibp=256, kyf=16, ca=256, sU=48, lU=48, uk=48,
-    sA=256, lA=256, iap=256, ef=256, mxa=128, mxb=128, m2=64, m3=32, erf=16, wacc=3, ta=1, pm=16, sl=16, bF=256, dp=256, wbx=256, r1=256, rr=256, tb=256, xb=256, xa=256,
-    W=512, nb=256, na=256, d1=512, d2=512, ep=256, lpf=2)
+_sb("int32", entx=1024, wti=1, kpi=1, ci=1024, pmi=16, pmj=16, n1=512, q=256, k1=256, za=256, l5a=256, ui=32, ub=32,
+    ei=256, em=256, ky=32, er=32, qb=256, zb=256, l5b=256, jd=16)
+_sb("bfloat16", fx0=2064, fx2=2064, fx3=2064, one=128, blka=128, blk=128, idb=128, idn=128, idk=128, idw=128, zer=32, zz=576, dlt=16,
+    rA=256, rK=16, sgm=512, fl=16, spa=256, kpa=256, k1a=256, iap=256, ca=256, da=256, spb=256, kpb=256, k1b=256, ibp=256, dl=512,
+    blw=128, blx=128, thr=192, lab=256, Yg=4096, Ys=4096, Xb=4096, NM=4096, NM2=4096)
+SCRATCH["EQ"] = ("sbuf", [128, 16, 256], "bfloat16")
+_sb("float16", eh=256, idh=128)
+_sb("uint16", lstP=16, lstI=16, lst8=4, off=256, eu=256, e16=16, ebc=256, pos=16, pos2=16, sel=16)
+_sb("float32", old0=288, Ct=1024, la0=288, old1=288, iot=1024, la1=288, old2=288, TB0=1024, la2=288, old3=288, TB4=1024, la3=288, TB1=1320,
+    TB2=1320, TB3=1320, aw=256, sv=256, cap=16, pw=16, x128=192, t128=192, LB0=1320, LB1=1320, yo=1320, D=4096, idf=128, allf=128, pmf=16,
+    x16=16, cmk=16, lI=16, mio=256, wk=2, pr=256, x1=256, oc=256, oT=1536, kyf=16, sU=80, lU=80, uk=80, uq=32,
+    sA=256, lA=256, ef=256, erf=32, wacc=3, ta=1, bF=256, dp=256, tb=256, bt=256, X=256, fa=256, fb=256, fy=256, ft=256,
+    d1=1024, d2=1024, ep=256, lpf=16, YP=8 * 288)
 for _t in range(NR):
-    _sb("float32", **{"sb%d" % _t: 272, "lb%d" % _t: 272, "sa%d" % _t: 256, "la%d" % _t: 256, "sc%d" % _t: 1, "lc%d" % _t: 1})
-_ps("pu", up=(0, 16), cnt=(32, 1), c2=(64, 16), kmp=(128, 16), spare=(256, 256))
-_ps("pk0", key0=(0, 512))
-_ps("pk1", key1=(0, 512))
+    _sb("float32", **{"xb%d" % _t: 288, "lb%d" % _t: 288, "ta%d" % _t: 288, "sc%d" % _t: 1, "lc%d" % _t: 1})
+    PART["Y%d" % _t] = (PART["YP"][0], PART["YP"][1] + 576 * _t, 288, "Y%d" % _t)
+    PART["aP%d" % _t] = (PART["YP"][0], PART["YP"][1] + 576 * _t + 288, 288, "aP%d" % _t)
+    PART["win%d" % _t] = PART["old%d" % _t][:2] + (1600, "win")
+GAP, FAR = ("Ct", "iot", "TB0", "TB4"), 1312.0
+_ps("pu", up=(0, 16), cnt=(32, 1), kmp=(128, 16), spare=(256, 256))
 _ps("pc", pcp=(0, 256), ctp=(256, 256))
-_ps("pa", Ap=(0, 256), Ia=(256, 256))
-_ps("pn", ns=(0, 256), cb=(256, 256))
-_ps("t0", u0=(0, 512), w0=(0, 256), w1=(256, 256))
-_ps("t1", u1=(0, 512), w2=(0, 256), w3=(256, 256))
-for _i, _n in enumerate(("zS", "zM", "zP", "z1", "zw")):
+_ps("pa", a75=(0, 256), w1=(256, 256))
+_ps("tk", tbp=(0, 256), sp2=(256, 256))
+for _h, (_k0, _k1, _) in enumerate(PARTS):
+    _n, _h = 16 * (_k1 - _k0), str(_h)
+    _ps("pk" + _h, **{"big" + _h: (0, 512), "key" + _h: (0, _n), "dq" + _h: (512 - 2 * _n, 2 * _n)})
+    _ps("m" + _h, **{"u" + _h: (0, 512), "w3" + _h: (0, _n), "p2" + _h: (_n, _n)})
+    if _n <= 128:
+        _ps("m" + _h, **{"ns" + _h: (2 * _n, _n), "wx" + _h: (3 * _n, _n)})
+    else:
+        _ps("tk", **{"ns" + _h: (0, _n), "wx" + _h: (256, _n)})
+for _i, _n in enumerate(("zS", "zM", "zP", "zw")):
     PART[_n] = (PART["zz"][0], PART["zz"][1] + 144 * _i, 144, "zz")
 
 
@@ -70,26 +85,28 @@ def messages(n):
     out = {}
 
     def piece(m, src, dst, lo, hi, by, kind):
-        for name in (src, dst):
+        src = src if isinstance(src, tuple) else (src,)
+        for name in src + (dst,):
             PART[name + m] = (PART[name][0], PART[name][1] + lo, hi - lo, name)
-        out[m] = (src + m, dst + m, hi - lo, by, kind)
-    for h in range(2):
-        piece("U%d" % h, "sU", "lU", 32 * h, 32 + 16 * h, -x[0], "cb"[h])
-        piece("A%d" % h, "sA", "lA", 128 * h, 128 * h + 128, -x[0], "ba"[h])
+        out[m] = (tuple(s + m for s in src), dst + m, hi - lo, by, kind)
+    for h, (k0, k1, path) in enumerate(PARTS):
+        piece("U%d" % h, "sU", "lU", 48 * h, 32 + 32 * h + k1 - k0, -x[0], "cb"[h])
+        piece("A%d" % h, "sA", "lA", 16 * k0, 16 * k1, -x[0], "ba"[h])
     for t in range(NR):
         piece("T%d" % (t + 1), "TB%d" % t, "TB%d" % (t + 1), 0, 1024, hold[t] - hold[t + 1], "T")
         if t > 1:
             piece("f%d" % t, "fx0", "fx%d" % t, 0, 2064, -x[t], "f")
         if t + 1 < NR:
             piece("c%d" % t, "sc%d" % t, "lc%d" % t, 0, 1, x[t] - x[t + 1], "c")
-        for h in range(2):
-            piece("b%d%d" % (t, h), "sb%d" % t, "lb%d" % t, 128 * h, 128 + 144 * h, hold[t] - hold[t + 1], "b")
-            piece("a%d%d" % (t, h), "sa%d" % t, "la%d" % t, 128 * h, 128 * h + 128, x[t] - hold[t + 1], "a")
+        for h, (k0, k1, path) in enumerate(PARTS):
+            lo, hi = (16 * k0 + 16, 272 + k1 - k0) if h else (16 - k1, 16 * k1 + 16)
+            piece("b%d%d" % (t, h), ("xb%d" % t, "Y%d" % t), "lb%d" % t, lo, hi, hold[t] - hold[t + 1], "b")
+            piece("a%d%d" % (t, h), ("ta%d" % t, "Y%d" % t, "aP%d" % t), "la%d" % t, lo, hi, x[t] - hold[t + 1], "a")
     return out
 
 
 MSG = messages(8)
-SEMAPHORES = ["qv", "qs", "qp", "qg", "ld0", "ld4", "ld5", "ld6", "st", "lsem"] + ["oc%d" % _i for _i in range(2 * NR)] + sorted(MSG)
+SEMAPHORES = ["qv", "qs", "qp", "qg", "ld0", "ld1", "ld4", "ld5", "ld6", "st", "lsem"] + ["oc%d" % _i for _i in range(2 * NR)] + sorted(MSG)
 
 
 def bits(m):
@@ -124,6 +141,20 @@ def ways(topo, T, src, dst, w, kind, alone):
     return [(chains[j], cut[j], cut[j + 1]) for j in range(len(chains))]
 
 
+def share(topo, T, core, to, m):
+    rank = T.rank_of(core)
+    if rank is None or m[0] not in "ab":
+        return topo.mask(core, to)
+    other = "ba"["ab".index(m[0])] + m[1:]
+    dst = T.cores[(rank + MSG[other][3]) % len(T.cores)]
+    mine, its = topo.engines(core, to), topo.engines(core, (route(topo, T, core, dst, other)[0][0] + (dst,))[0])
+    if len(mine) > len(its):
+        mine = [e for e in mine if e not in its]
+    elif len(mine) == len(its):
+        mine = mine[:len(mine) // 2] if m[0] == "a" else mine[len(mine) // 2:]
+    return sum(1 << e for e in mine)
+
+
 def view(T, name, lo, hi):
     b, at = PART[name][:2]
     return T[b][:, at + lo:at + hi]
@@ -140,7 +171,7 @@ def hand_on(g, core, T, topo):
                 way = (src,) + chain + (dst,)
                 before, to = way[way.index(core) - 1], way[way.index(core) + 1]
                 b = view(T, MSG[m][1], lo, hi)
-                g.wait_ge(T.sem[m], bits(topo.mask(before, core)))
+                g.wait_ge(T.sem[m], bits(share(topo, T, before, core, m)))
                 rid, pid = topo.addr(to, core)
                 mk = topo.mask(core, to)
                 g.remote_dma(b, b, T.sem[m], T.sem.lsem, pid, rid, mk)
@@ -154,7 +185,13 @@ def B(name, lo=0, hi=None, st=1):
     return (b, at + lo, at + (w if hi is None else hi), st, key)
 
 
+def rows(k0, k1, lo, hi):
+    return ("EQ", 256 * k0 + lo, 256 * (k1 - 1) + hi, 1, "EQ", (k0, k1, lo, hi))
+
+
 def width(x):
+    if len(x) > 5:
+        return (x[5][1] - x[5][0]) * (x[5][3] - x[5][2])
     return (x[2] - x[1] + x[3] - 1) // x[3]
 
 
@@ -189,6 +226,101 @@ def links(ops):
             acc.setdefault(x[4], []).append((x, False, i))
         out.append(sorted(pre))
     return out
+
+
+def polish(ops, pre, seq, wake):
+    n = len(ops)
+    dur = [o["dur"] for o in ops]
+    hold = [o["dur"] if o["kind"] in ("run", "send") else 0.05 for o in ops]
+    q = [o["q"] if o["kind"] != "land" else None for o in ops]
+    dep = [[(j, dur[j] + (0.0 if ops[j]["kind"] == "send" else wake if q[i] != q[j] else SAME)) for j in pre[i]
+            if not (q[i] == "p" and q[j] == "p") and (ops[j]["kind"] != "send" or q[i] is None)] for i in range(n)]
+    banks = [[([b + r for r in "vsp" if r != q[i]], b + q[i]) for b in ops[i]["banks"]] for i in range(n)]
+    needs = [set(pre[i]) | set(j for j, lag in ops[i]["behind"] if ops[i]["kind"] != "run") for i in range(n)]
+
+    def run(seq, at, was):
+        at -= at % 64
+        st, by, marks = (list(was[2]), list(was[3]), was[4][:at // 64]) if at else ([0.0] * n, [-1] * n, [])
+        last, end, who = (dict(was[4][at // 64]) if at else {}), 0.0, -1
+        for x in range(at, n):
+            if not x % 64:
+                marks.append(dict(last))
+            i = seq[x]
+            t, w, k = 0.0, -1, q[i]
+            if k:
+                j = last.get(k, -1)
+                if j >= 0:
+                    t, w = st[j] + hold[j], -2 - j
+                last[k] = i
+            for j, lag in dep[i]:
+                if st[j] + lag > t:
+                    t, w = st[j] + lag, j
+            for others, me in banks[i]:
+                for r in others:
+                    j = last.get(r, -1)
+                    if j >= 0 and st[j] + dur[j] + wake > t:
+                        t, w = st[j] + dur[j] + wake, j if j in needs[i] else -2 - j
+                last[me] = i
+            st[i], by[i] = t, w
+            if t + dur[i] > end:
+                end, who = t + dur[i], i
+        return end, who, st, by, marks
+
+    def swap(seq, pa, pb, forth):
+        mid = seq[pa:pb + 1]
+        if forth:
+            move = {mid[-1]}
+            for i in mid[::-1]:
+                if i in move:
+                    move |= needs[i]
+            if mid[0] in move:
+                return None
+            return seq[:pa] + [i for i in mid if i in move] + [i for i in mid if i not in move] + seq[pb + 1:]
+        move = {mid[0]}
+        for i in mid:
+            if needs[i] & move:
+                move.add(i)
+        if mid[-1] in move:
+            return None
+        return seq[:pa] + [i for i in mid if i not in move] + [i for i in mid if i in move] + seq[pb + 1:]
+
+    seed = [7]
+
+    def draw(k):
+        seed[0] = (seed[0] * 1103515245 + 12345) % 2147483648
+        return (seed[0] >> 8) % k
+    cur, left = run(seq, 0, None), SWAPS
+    best = (cur[0], seq)
+    while left > 0:
+        place = {i: x for x, i in enumerate(seq)}
+        seq = sorted(seq, key=lambda i: (cur[2][i], place[i]))
+        cur = run(seq, 0, None)
+        for _ in range(40):
+            place, pairs, i = {i: x for x, i in enumerate(seq)}, [], cur[1]
+            while cur[3][i] != -1:
+                j = cur[3][i]
+                if j < -1:
+                    j = -2 - j
+                    pairs.append((j, i))
+                i = j
+            while left > 0:
+                left -= 1
+                k, hop, forth = draw(len(pairs)), (0, 0, 1, 2, 4)[draw(5)], draw(2)
+                a, b = pairs[k]
+                while hop and forth and k + 1 < len(pairs) and pairs[k + 1][1] == a:
+                    k, a, hop = k + 1, pairs[k + 1][0], hop - 1
+                while hop and not forth and k and pairs[k - 1][0] == b:
+                    k, b, hop = k - 1, pairs[k - 1][1], hop - 1
+                other = swap(seq, place[a], place[b], forth)
+                if other:
+                    new = run(other, place[a], cur)
+                    if new[0] < cur[0] - SLACK * math.log((draw(1000) + 1) / 1001):
+                        seq, cur = other, new
+                        break
+            if cur[0] < best[0]:
+                best = (cur[0], seq)
+    ORDER["end"] = best[0]
+    return best[1]
 
 
 def arrange(ops, pre, wake):
@@ -263,7 +395,7 @@ def arrange(ops, pre, wake):
         if turn < PASSES:
             late = place(bwd, fwd, lambda i: (-start[i] - dur[i], -i))
     ORDER["end"] = best[0]
-    seq, seen = sorted(range(n), key=lambda i: (best[1][i], i)), {}
+    seq, seen = polish(ops, pre, sorted(range(n), key=lambda i: (best[1][i], i)), wake), {}
     for i in seq:
         for b in ops[i]["banks"]:
             pre[i] = pre[i] + [seen[b + r] for r in "vsp" if r != ops[i]["q"] and b + r in seen]
@@ -290,13 +422,16 @@ def record(T):
 
     def ap(x):
         name, lo, hi, st = x[:4]
+        if len(x) > 5:
+            k0, k1, lo, hi = x[5]
+            return T[name][:, k0, lo:hi] if k1 == k0 + 1 else T[name][:, k0:k1, lo:hi]
         return T[name][:, lo:hi:st] if st != 1 else T[name][:, lo:hi]
 
     def val(s):
         return ap(s) if isinstance(s, tuple) else s
 
     def two(*xs):
-        return 0.5 if all(SCRATCH[x[0]][2] in ("bfloat16", "uint16") for x in xs) else 1.0
+        return 0.5 if all(SCRATCH[x[0]][2] in ("bfloat16", "uint16", "float16") for x in xs) else 1.0
 
     def vd(n, k=1.0):
         return max(64.0, n * k) * CY + FIX
@@ -327,14 +462,18 @@ def record(T):
         else:
             put("run", "v", lambda e: e.tensor_tensor(ap(o), ap(win).indirect(ap(off)), ap(b), op), r, [o], d)
 
-    def scatter(win, off, a):
-        put("run", "v", lambda e: e.tensor_copy(ap(win).indirect(ap(off)), ap(a)), [a, off], [win], 0.05 + width(a) * SC * CY)
+    def scatter(win, off, a, b=None):
+        d = 0.05 + width(a) * SC * CY
+        if b is None:
+            put("run", "v", lambda e: e.tensor_copy(ap(win).indirect(ap(off)), ap(a)), [a, off], [win], d)
+        else:
+            put("run", "v", lambda e: e.tensor_tensor(ap(win).indirect(ap(off)), ap(a), ap(b), ALU.max), [a, b, off], [win], d)
 
-    def scan(o, m, a):
-        put("run", "v", lambda e: e.tensor_tensor_scan(ap(o), ap(m), ap(a), 0.0, ALU.mult, ALU.max), [m, a], [o], vd(width(a), two(o, m, a)))
+    def scan(o, m, a, first=0.0, op=ALU.mult):
+        put("run", "v", lambda e: e.tensor_tensor_scan(ap(o), ap(m), ap(a), first, op, ALU.max), [m, a], [o], vd(width(a), two(o, m, a)))
 
-    def act(o, a, f, bias=0.0, scale=1.0, accum=None, by=None):
-        r = [x for x in (a, scale, bias, by) if isinstance(x, tuple)]
+    def act(o, a, f, bias=0.0, scale=1.0, accum=None, by=None, also=()):
+        r = [x for x in (a, scale, bias, by) if isinstance(x, tuple)] + list(also)
         d = vd(width(a)) + FIXS if by is None else 0.065 + width(o) * G * CY
         if accum is not None:
             put("run", "s", lambda e: e.activation(ap(o), ap(a), f, bias=bias, scale=scale, accum_out=ap(accum)), r, [o, accum], d + 0.02)
@@ -362,9 +501,11 @@ def record(T):
     def load(q, o, a, sem, dur, lo=0, hi=None):
         put("dma", q, lambda e: e.dma_start(ap(o), T[a][:] if hi is None else T[a][:, lo:hi]), [], [o], dur, sem=sem, inc=16)
 
-    def send(m, after=()):
-        where[m] = len(ops)
-        put("send", "g", None, [B(MSG[m][0], 0, MSG[m][2])] + list(after), [], 3 * CALL if m[0] in "Tf" else CALL, msg=m)
+    def send(m, after=(), also=None):
+        ms = [m, also] if also else [m]
+        for x in ms:
+            where[x] = len(ops)
+        put("send", "g", None, [B(s, 0, MSG[x][2]) for x in ms for s in MSG[x][0]] + list(after), [], 3 * CALL if m[0] in "Tf" else CALL, msg=ms)
 
     def expect(m):
         put("land", None, None, [], [B(MSG[m][1], 0, MSG[m][2])], LAT[m[0]], [where[m]], msg=m)
@@ -373,18 +514,26 @@ def record(T):
         return B(name, c, 1021 + c, 4)
 
     def half(x, h):
-        return (x[0], x[1] + 128 * h * x[3], x[1] + (128 * h + 127) * x[3] + 1) + x[3:]
+        return (x[0], x[1] + 16 * PARTS[h][0] * x[3], x[1] + (16 * PARTS[h][1] - 1) * x[3] + 1) + x[3:]
+
+    def vals(name, h):
+        k0, k1 = PARTS[h][:2]
+        return B(name, 16 * k0 + 16, 16 * k1 + 16), B(name, 272, 272 + k1 - k0) if h else B(name, 16 - k1, 16)
 
     def slide(name, p):
         return B(name, 15 - p, 143 - p)
 
-    load("y", B("entx"), "ent", "ld0", 4.5)
+    cut = 64 * PARTS[0][1]
+    load("y", B("entx", 0, cut), "ent", "ld0", 3.4, 0, cut)
     mark("load")
     ms(B("fx0", 0, 16), 0.0)
     ms(B("fx0", 2048, 2064), 0.0)
     load("s", B("wti"), "wt", "ld4", 2.2)
     load("s", B("kpi"), "kap", "ld5", 2.2)
-    load("y", B("fx0", 1, 2049), "feat", "ld6", 6.5)
+    load("y", B("fx0", 1, 2049), "feat", "ld6", 5.4)
+    behind("load")
+    mark("load")
+    load("y", B("entx", cut), "ent", "ld1", 6.4, cut, 1024)
     behind("load")
     cp(B("fx0", 2056, 2057), B("wti"))
     cp(B("fx0", 2057, 2058), B("kpi"))
@@ -399,8 +548,8 @@ def record(T):
     sift(B("idb"), B("one"), [[-1, 128]], ALU.is_equal, 0.0, 0, 1)
     ms(B("zz"), 0.0)
     ms(B("zer"), 0.0)
-    ms(B("allf"), -1.0 / 16)
-    ms(B("wacc", 2, 3), 15.5 / 8)
+    ms(B("allf"), -0.5)
+    ms(B("wacc", 2, 3), 16.0 + 31.0 / 128)
     ms(B("sgm"), 1.0)
     cp(B("sgm", 0, 497, 16), B("zer", 0, 32))
     ts(B("ci"), B("ci"), 63, ALU.bitwise_and)
@@ -408,38 +557,57 @@ def record(T):
     ts(B("pmj"), B("pmi"), 15, ALU.bitwise_and)
     cp(B("pmf"), B("pmj"))
     pm = B("pmf", 0, 1)
-    ts(B("lpf", 0, 1), pm, 7.5, ALU.is_gt, -127.0, ALU.mult)
-    ts(B("lpf", 1, 2), pm, 16.0, ALU.mult, B("lpf", 0, 1), ALU.add)
-    ts(B("lstP"), B("x16", 0, 8), 2.0, ALU.mult, B("lpf", 1, 2), ALU.add)
     ts(B("lI"), B("x16"), 16.0, ALU.mult, pm, ALU.add)
     cp(B("lstI"), B("lI"))
-    ts(B("lbl"), B("lI"), 1024.0, ALU.add)
-    for k0, k1, path in PARTS:
-        ts(B("lbl8", k0, k1), B("lI", k0, k1), 16.0, ALU.mult, -256.0 * k0, ALU.add)
+    for h, (k0, k1, path) in enumerate(PARTS):
+        nk = k1 - k0
+        ts(B("jd", k0, k1), B("lI", 0, nk), (1 - nk) / 2, ALU.add, 1 / nk, ALU.mult)
+        ts(B("lpf", k0, k1), B("jd", k0, k1), (1 - 16 * nk) / 16, ALU.mult)
+        tt(B("lpf", k0, k1), B("lpf", k0, k1), B("lI", 0, nk), ALU.add)
+        ts(B("lstP", k0, k1), B("lpf", k0, k1), 16.0, ALU.mult)
+        ts(B("lst8", 2 * h, 2 * h + 1), pm, nk - 1.0, ALU.min)
+    ts(B("cap"), B("lI"), -1.0, ALU.mult, FAR, ALU.add)
+    ms(B("lab"), 4 * BIG)
+    ts(B("lab", 0, 241, 16), B("lI"), -1.0, ALU.mult)
     ts(B("dlt"), B("x16"), pm, ALU.is_equal)
+    for t in range(NR):
+        ms(B("old%d" % t, 272, 288), 0.0)
+        ms(B("la%d" % t, 0, 16 - PARTS[0][1]), 0.0)
+    for h, (k0, k1, path) in enumerate(PARTS):
+        for j in range(272, 272 + k1 - k0) if h else range(16 - k1, 16):
+            act(B("YP", j, 8 * 288, 288), B("one", 0, 8), AF.Copy, scale=-4096.0)
+            ops[-1]["w"] = [B(n + str(t), j, j + 1) for n in ("Y", "aP") for t in range(NR)]
     for k0, k1, path in PARTS:
         n = 16 * (k1 - k0) // len(path)
         for c in range(len(path)):
             at = 16 * k0 + n * c
             act(B("rA", at, at + n), B("mio", at, at + n), AF.Identity, bias=15360.0 + SHIFT[path[c]], scale=-1024.0)
     act(B("idf"), B("idb"), AF.Copy)
-    act(B("hid"), B("idb"), AF.Copy, scale=HP)
-    for n, s in (("zS", -8192.0), ("zM", -16384.0), ("zP", 16384.0), ("z1", 128.0)):
+    for n, s in (("idn", -1.0), ("idk", 1 / PEN), ("idw", 6.5)):
+        act(B(n), B("idb"), AF.Copy, scale=s)
+    for n, s in (("zS", -8192.0), ("zM", -16384.0), ("zP", 16384.0)):
         act(B(n, 15, 128, 16), B("blk", 0, 113, 16), AF.Copy, scale=s)
-    ts(B("cmk"), B("x16"), pm, ALU.is_gt)
-    for x in range(16):
-        act(B("tri", 128 * x, 128 * x + 128), B("blk"), AF.Copy, scale=B("cmk", x, x + 1))
+    cp(B("idh"), B("idb"))
+    ts(B("cmk"), B("x16"), pm, ALU.is_gt, 1.0, ALU.add)
+    scan(B("pw"), B("cmk"), B("zer", 0, 16), 2048.0)
+    act(B("blw"), B("blk"), AF.Copy, scale=B("pw", 15, 16))
+    act(B("blx"), B("blk"), AF.Copy, scale=8 * BIG)
+    iota(B("x128"), [[0, 12], [1, 16]], 0, 0)
+    ts(B("x128"), B("x128"), pm, ALU.is_equal)
+    ts(B("t128"), B("x128"), B("pw", 15, 16), ALU.mult, -2.0, ALU.mult)
+    ts(B("x128"), B("x128"), -1.0, ALU.add, BIG * 8192, ALU.mult)
+    tt(B("thr"), B("x128"), B("t128"), ALU.add)
 
-    def convert(o, x, w):
-        n1, w = B("n1", 0, width(x)), B(w, 0, width(x))
+    def convert(o, x, w, at=0):
+        n1, w = B("n1", at, at + width(x)), B(w, 0, width(x))
         ts(n1, x, 2.0 ** -11, ALU.mult, 0.5 - 2.0 ** -12, ALU.add)
         ts(w, n1, 2048.0, ALU.mult, 15.0, ALU.add)
         tt(o, w, x, ALU.add)
-    ts(B("q"), cls("entx", 0), 15.0, ALU.add)
-    convert(B("sA"), cls("entx", 0), "u0")
-    ts(B("k1"), B("q"), 16, ALU.bitwise_and)
-    tt(B("pr"), B("n1", 0, 256), B("k1"), ALU.mult)
     for h in range(2):
+        ts(half(B("q"), h), half(cls("entx", 0), h), 15.0, ALU.add)
+        convert(half(B("sA"), h), half(cls("entx", 0), h), "u%d" % h, 16 * PARTS[h][0])
+        ts(half(B("k1"), h), half(B("q"), h), 16, ALU.bitwise_and)
+        tt(half(B("pr"), h), half(B("n1"), h), half(B("k1"), h), ALU.mult)
         send("A%d" % h)
     iota(B("iot"), [[1, 1024]], 0, 0)
     behind("A1")
@@ -452,23 +620,27 @@ def record(T):
         act(o, d2, AF.Relu, bias=-15.0)
 
     def complete(t, name):
+        la, lb, old, c = "la%d" % (t - 1), "lb%d" % (t - 1), "old%d" % (t - 1), t - 1
+        for h in range(2):
+            gcp(vals(old, h)[0], half(cls(name, c), h))
         for h, (k0, k1, path) in enumerate(PARTS):
-            expect("a%d%d" % (t - 1, h))
-            o, a = B(name, 64 * k0 + t - 1, 64 * k1 + t - 4, 4), B("la%d" % (t - 1), 16 * k0, 16 * k1)
-            if t < NR and (h == 0 or GCP):
-                gcp(o, a)
-            else:
-                act(o, a, AF.Copy)
-            expect("b%d%d" % (t - 1, h))
-        cp(B("pos2"), B("lb%d" % (t - 1), 256, 272))
-        scatter(B(name), B("pos2"), B("lb%d" % (t - 1), 0, 256))
+            lo, hi = 16, 16 * k1 + 16
+            expect("a%d%d" % (c, h))
+            ts(B("sel", k0, k1), vals(la, h)[1], -1.0, ALU.mult, FAR, ALU.add)
+            act(half(cls(name, c), h), B("win%d" % c, lo, hi + int(FAR)), AF.Copy, by=B("sel", k0, k1),
+                also=[B(la, 0, hi), B(GAP[c]), B(old, lo)])
+        for h, (k0, k1, path) in enumerate(PARTS):
+            expect("b%d%d" % (c, h))
+            cp(B("pos2", k0, k1), vals(lb, h)[1])
+        scatter(B(name), B("pos2"), B(lb, 16, 272))
 
     ID = B("lstI")
     act(B("ctp"), cls("Ct", 0), AF.Copy)
     for t in range(NR):
         last = t == NR - 1
         seen.clear()
-        A, fx, TB, U = cls("LB", t) if t else B("sA"), "fx%d" % (t if t > 1 else 0), "TB%d" % t, "uk" if t else "sU"
+        LB = "LB%d" % ((t + 1) % 2)
+        A, fx, TB, U = cls("LB%d" % (t % 2), t) if t else B("sA"), "fx%d" % (t if t > 1 else 0), "TB%d" % t, "uk" if t else "sU"
         tau, clock = 5.0 + t, 12.0 + t
         if t > 1:
             expect("f%d" % t)
@@ -479,34 +651,36 @@ def record(T):
             act(B("zw", 15, 128, 16), B("blk", 0, 113, 16), AF.Copy, scale=B("wk", 0, 1))
             act(B("rK"), B("dlt"), AF.Copy, scale=B("wk", 1, 2))
             mm(B("kmp"), B("blk"), B("rK"), True, True)
-        act(B(U, 16, 32), B("kmp"), AF.Copy)
+        act(B(U, 0, 16), B("kmp"), AF.Copy)
         if t:
             expect("c%d" % (t - 1))
-        for h in range(2):
-            lo, hi, k0, k1 = 128 * h, 128 * h + 128, 8 * h, 8 * h + 8
+        for h, (k0, k1, path) in enumerate(PARTS):
+            lo, hi, nk = 16 * k0, 16 * k1, k1 - k0
             if t:
                 tt(B("q", lo, hi), B("ctp", lo, hi), half(A, h), ALU.add)
-                act(B("Ap", lo, hi), half(A, h), AF.Copy)
+                act(B("a75", lo, hi), half(A, h), AF.Identity, bias=-7.5)
                 ts(B("k1", lo, hi), B("q", lo, hi), 16, ALU.bitwise_and)
-                tt(B("pr", lo, hi), B("Ap", lo, hi), B("k1", lo, hi), ALU.mult)
-            ts(B("off", lo, hi), B("pr", lo, hi), 2.0 ** (-16 if t else -4), ALU.mult, 127.0 / 256 if t else 0.0, ALU.add, by=B("lstP"))
-            for c in range(4 * h, 4 * h + 4):
+                tt(B("pr", lo, hi), B("a75", lo, hi), B("k1", lo, hi), ALU.mult)
+            ts(B("off", lo, hi), B("pr", lo, hi), 2.0 ** (-16 if t else -4), ALU.mult, 127.0 / 256 if t else 0.0, ALU.add, by=B("lstP", k0, k1))
+            for c in range(k0 // 2, k1 // 2):
                 o, l = B("Yg", 512 * c, 512 * c + 512), B("off", 32 * c, 32 * c + 32)
                 if c in FV:
                     pick(o, B(fx, 0, 2049), l)
                 else:
                     act(o, B(fx, 0, 2049), AF.Copy, by=l)
                 scan(B("Ys", 512 * c, 512 * c + 512), B("sgm"), o)
-                for p in range(4 * (c % 4), 4 * (c % 4) + 4):
-                    mm(B("up", k0, k1), slide("zw", p), B("Ys", 16 * lo + 128 * p + 15, 16 * lo + 128 * p + 128, 16), p == 0, p == 15)
-            cp(B("ui", k0, k1), B("up", k0, k1))
+                for p in range(32 * (c - k0 // 2) // nk, 32 * (c + 1 - k0 // 2) // nk):
+                    mm(B("up", k0, k1), slide("zw", p), B("Ys", 16 * (lo + nk * p) + 15, 16 * (lo + nk * p + nk), 16), p == 0, p == 15)
+            ui, ub, uq, few = B("ui", 16 * h, 16 * h + nk), B("ub", 16 * h, 16 * h + nk), B("uq", 16 * h, 16 * h + nk), B("lst8", 2 * h, 2 * h + 1)
+            cp(ui, B("up", k0, k1))
             if h:
                 behind("sum", AHEAD[4])
             mark("sum")
-            ts(B("ub", k0, k1), B("ui", k0, k1), 4095, ALU.bitwise_and)
-            tt(B("uq", k0, k1), B("ub", k0, k1), B("ub", k0, k1), ALU.mult)
-            cp(B(U, 32 * h, 32 * h + 8), B("ub", k0, k1))
-            ts(B(U, 32 * h + 8, 32 * h + 16), B("uq", k0, k1), 2.0 ** -5, ALU.mult, (15.5 if t else 0.0) - 13.0 / 32, ALU.add)
+            ts(ub, ui, 4095, ALU.bitwise_and)
+            at = 16 + 32 * h
+            act(B(U, at, at + 16), ub, AF.Copy, by=few)
+            act(B("uq", 16 * h, 16 * h + 16), ub, AF.Square, by=few)
+            act(B(U, at + 16, at + 16 + nk), uq, AF.Identity, scale=2.0 ** -5, bias=(15.5 if t else 0.0) - 13.0 / 32)
             if not t:
                 send("U%d" % h)
         if not t:
@@ -514,8 +688,8 @@ def record(T):
                 expect("A%d" % h)
             A, U = B("lA"), "lU"
             tt(B("q"), B("ctp"), A, ALU.add)
-        act(B("x1"), A, AF.Identity, bias=-7.5)
-        act(B("x1"), B("x1"), AF.Identity, bias=C16)
+            act(B("a75"), A, AF.Identity, bias=-7.5)
+        act(B("x1"), B("a75"), AF.Identity, bias=C16)
         act(B("oc"), B("x1"), AF.Identity, bias=-C16)
         for h, (k0, k1, path) in enumerate(PARTS):
             n, reps = 16 * (k1 - k0), 16 // len(path)
@@ -528,30 +702,37 @@ def record(T):
                 put("dma", "y", lambda e, o=o, a=a: e.dma_start(ap(o), ap(a)), [a], [o], 2.2, sem="oc%d" % (2 * t + h), inc=16 * (reps - 1))
         ts(B("za"), B("q"), 0x3801F, ALU.bitwise_and)
         ts(B("l5a"), B("q"), 31, ALU.bitwise_and)
-        act(B("sgs"), B("l5a"), AF.Sign, bias=-tau - 0.5, by=ID)
-        act(B("sgk"), B("za"), AF.Sign, bias=tau + 0.5, scale=-1.0, by=ID)
-        for o, x, signs in (("w0", A, ("sgs",)), ("w2", B("oc"), ("sgk",)), ("w1", A, ("sgs", "sgk"))):
-            mm(B(o), B("idf"), x, True, False)
-            for s in signs:
-                mm(B(o), B("hid"), B(s), False, s == signs[-1])
-        act(B("aw"), B("w0"), AF.Relu, bias=-HP)
-        act(B("Ap"), B("w2"), AF.Identity, bias=clock - HP)
-        act(B("aP"), B("w1"), AF.Relu)
+        act(B("spa"), B("l5a"), AF.Relu, bias=(tau + 0.5) * PEN, scale=-PEN, by=ID)
+        act(B("kpa"), B("za"), AF.Relu, bias=(tau + 0.5) * PEN, scale=-PEN, by=ID)
+        act(B("k1a"), B("kpa"), AF.Sign)
+
+        def total(o, *terms):
+            for j, (l, r) in enumerate(terms):
+                mm(o, B(l), r, j == 0, j == len(terms) - 1)
+        total(B("w1"), ("idb", B("kpa")), ("idn", B("spa")), ("idf", A))
+        total(B("sp2"), ("idf", A), ("idn", B("spa")))
+        act(B("aw"), B("sp2"), AF.Relu)
+        if last:
+            decode(B("fy"), B("aw"), B("sp2"), 256)
+        total(B("tbp"), ("idk", B("kpa")), ("idw", B("k1a")))
+        act(B("da"), B("tbp"), AF.Copy)
+
+        def out(name, h):
+            return vals(name + str(t), h)[0]
+        aP = [half(B("fa"), h) if last else out("aP", h) for h in range(2)]
+        for h in range(2):
+            act(aP[h], half(B("w1"), h), AF.Relu)
+            if last:
+                decode(out("aP", h), aP[h], half(B("ctp"), h), 16 * PARTS[h][0])
         act(B("ca"), B("w1"), AF.Relu, bias=-15.5 * 16384, scale=16384.0)
         mark("lanes")
         act(B("iap"), B("l5a"), AF.Relu, bias=31 * BIG, scale=-2 * BIG, by=ID)
-        act(B("Ia"), B("iap"), AF.Identity, bias=clock, scale=-1.0)
-        if last:
-            decode(B("x1"), A, B("ctp"), 0)
-            A = B("x1")
-        for h in range(2):
-            gcp(B("W", 256 * h + 128, 256 * h + 256), half(A, h))
         if t:
             expect("T%d" % t)
             complete(t, TB)
         else:
             for j in range(2):
-                convert(B(TB, 512 * j, 512 * j + 512), B("entx", 512 * j, 512 * j + 512), "key%d" % j)
+                convert(B(TB, 512 * j, 512 * j + 512), B("entx", 512 * j, 512 * j + 512), "big%d" % j)
             for h in range(2):
                 expect("U%d" % h)
         send("T%d" % (t + 1), [] if t else [B("lU")])
@@ -559,7 +740,7 @@ def record(T):
             send("f%d" % (t + 2))
             behind("T%d" % (t + 1))
         if not last:
-            gcp(cls("LB", t + 1), cls(TB, t + 1))
+            gcp(cls(LB, t + 1), cls(TB, t + 1))
         RT = B(TB, 0, 1024)
 
         for h, (k0, k1, path) in enumerate(PARTS):
@@ -572,12 +753,15 @@ def record(T):
             def ch(n, c, more=1):
                 return B(n, 16 * (lo + cw * c), 16 * (lo + cw * (c + more)))
             for k in range(k0, k1):
-                u, s = B(U, 24 * h + k, 24 * h + k + 1), B(U, 24 * h + 8 + k, 24 * h + 9 + k)
-                act(B("ep", lo + k - k0, hi, nk), B(U, 16, 32), AF.Identity, bias=s, scale=u)
+                at = 16 + 32 * h + k - k0
+                act(B("ep", lo + k - k0, hi, nk), B(U, 0, 16), AF.Identity, bias=B(U, at + 16, at + 17), scale=B(U, at, at + 1))
             ts(H("ei"), H("ep"), B("lc%d" % (t - 1)) if t else 0.0, ALU.add)
             ts(H("em"), H("ei"), 1023, ALU.bitwise_and)
             cp(H("eu"), H("em"))
-            act(H("ef"), H("em"), AF.Copy, by=B("lstI", 0, nk))
+            if EH:
+                cp(H("eh"), H("eu"))
+            else:
+                act(H("ef"), H("em"), AF.Copy, by=B("lstI", 0, nk))
             own = B("oT", 768 * h, 768 * h + 16 * cw)
             for c in range(len(path)):
                 l = B("eu", lo + cw * c, lo + cw * c + cw)
@@ -614,10 +798,10 @@ def record(T):
                         mark("pick")
             key = "key%d" % h
             mm(B(key, 0, 16 * nk), B("idb"), H("rA"), True, False)
-            mm(B(key, 0, 16 * nk), B("idf"), H("ef"), False, False)
+            mm(B(key, 0, 16 * nk), B("idh" if EH else "idf"), H("eh" if EH else "ef"), False, False)
             runs = []
             for c in range(len(path)):
-                if runs and path[runs[-1][0]] == path[c] and cw * (runs[-1][1] + 1) <= 64:
+                if runs and path[runs[-1][0]] == path[c] and cw * runs[-1][1] < 64:
                     runs[-1][1] += 1
                 else:
                     runs.append([c, 1])
@@ -632,83 +816,91 @@ def record(T):
                 most(B("kyf", k, k + 1), B(key, k - k0, 16 * nk, nk))
             behind("keys" if h else "lanes", AHEAD[0 if h else 2])
             mark("keys")
-            cp(B("ky", k0, k1), B("kyf", k0, k1))
-            ts(B("er", k0, k1), B("ky", k0, k1), 1023, ALU.bitwise_and)
-            cp(B("e16", k0, k1), B("er", k0, k1))
-            cp(B("erf", k0, k1), B("er", k0, k1))
+            ky, er, erf = [B(n, 16 * h, 16 * h + nk) for n in ("ky", "er", "erf")]
+            cp(ky, B("kyf", k0, k1))
+            ts(er, ky, 1023, ALU.bitwise_and)
+            cp(B("e16", k0, k1), er)
+            if ES:
+                act(B("erf", 16 * h, 16 * h + 16), er, AF.Copy, by=B("lst8", 2 * h, 2 * h + 1))
+            else:
+                cp(erf, er)
             e = B("e16", k0, k1)
             pick(H("ebc"), B("iot"), e)
-            mm(H("pcp"), B("zer", 0, 128), H("zer"), True, False)
+            mm(H("pcp"), B("idb"), B("thr", 0, hi - lo), True, False)
             for k in range(k1):
-                a = max(16 * k, lo)
-                ts(B("EQ", 240 * k + a, 240 * k + hi), B("ebc", a, hi), B("erf", k, k + 1), ALU.is_equal)
+                a, at = max(16 * k, lo), 16 * k if k >= k0 else 0
+                j = k if k < PARTS[0][1] else 16 + k - k0
+                ts(rows(k, k + 1, a - at, hi - at), B("ebc", a, hi), B("erf", j, j + 1), ALU.is_equal)
                 a = max(16 * k + 16, lo)
                 if a < hi:
-                    mm(B("pcp", a, hi), B("blk"), B("EQ", 240 * k + a, 240 * k + hi), False, False)
-            for x in range(16):
-                mm(B("pcp", lo + x, hi - 15 + x, 16), B("tri", 128 * x, 128 * x + 128), B("EQ", 256 * k0 + x, 256 * k1 - 255 + x, 256), False, x == 15)
-            act(H("fl"), H("pcp"), AF.Sign, accum=B("wacc", h, h + 1))
-            c2, pos, sel = B("c2", k0, k1), B("sb%d" % t, 256 + k0, 256 + k1), B("sel", k0, k1)
-            for p in range(16):
-                mm(c2, slide("z1", p), B("fl", lo + p, hi - 15 + p, 16), p == 0, p == 15)
-            tt(B("pm", k0, k1), c2, B("lbl", k0, k1), ALU.min)
-            tt(pos, B("pm", k0, k1), B("erf", k0, k1), ALU.max)
-            tt(B("sl", k0, k1), c2, B("lbl8", k0, k1), ALU.add)
-            ts(sel, B("sl", k0, k1), 0.0625, ALU.mult)
-            w0, w1, w2, w3, ns, cb = [H(n) for n in ("w0", "w1", "w2", "w3", "ns", "cb")]
+                    mm(B("pcp", a, hi), B("blx"), rows(k, k + 1, a - at, hi - at), False, False)
+                if not ROWS and k >= k0:
+                    mm(B("pcp", 16 * k, 16 * k + 16), B("blw"), rows(k, k + 1, 0, 16), False, k == k1 - 1)
+            if ROWS:
+                mm(H("pcp"), B("blw"), rows(k0, k1, 0, 16), False, True)
+            scan(H("sv"), H("lab"), H("pcp"), 0.0, ALU.min)
+            sv = B("sv", lo + 15, hi, 16)
+            z, pos = [vals(n + str(t), h)[1] for n in ("ta", "xb")]
+            act(B("fl", k0, k1), sv, AF.Sign, bias=-600.0, accum=B("wacc", h, h + 1))
+            tt(z, sv, B("cap", k0, k1), ALU.min)
+            tt(pos, z, erf, ALU.max)
+            w3, p2, ns, wx, dq = [B(n + str(h)) for n in ("w3", "p2", "ns", "wx", "dq")]
             act(H("bF"), RT, AF.Copy, by=e)
             pick(H("qb"), B("Ct"), e, H("bF"), ALU.add)
             ts(H("zb"), H("qb"), 0x3801F, ALU.bitwise_and)
             ts(H("l5b"), H("qb"), 31, ALU.bitwise_and)
             each = B("lstI", 0, nk)
-            act(w1, H("bF"), AF.Copy)
-            act(H("gk"), H("zb"), AF.Sign, bias=tau + 0.5, scale=-1.0, by=each)
-            act(H("gs"), H("l5b"), AF.Sign, bias=-tau - 0.5, by=each)
+            act(H("kpb"), H("zb"), AF.Relu, bias=(tau + 0.5) * PEN, scale=-PEN, by=each)
+            act(H("spb"), H("l5b"), AF.Relu, bias=(tau + 0.5) * PEN, scale=-PEN, by=each)
             act(H("ibp"), H("l5b"), AF.Relu, bias=31 * BIG, scale=-2 * BIG, by=each)
-            tt(H("bk"), w1, H("gk"), ALU.mult)
-            tt(w0, w1, H("gs"), ALU.mult)
-            tt(w3, w0, H("bk"), ALU.max)
-            tt(H("dp"), w3, H("aP"), ALU.subtract)
-            act(cb, w3, AF.Relu, bias=-15.5 * 16384, scale=16384.0)
+            if h in GK:
+                act(H("k1b"), H("zb"), AF.Sign, bias=tau + 0.5, scale=-1.0, by=each)
+            else:
+                act(H("k1b"), H("kpb"), AF.Sign)
+            total(w3, ("idb", H("kpb")), ("idn", H("spb")))
+            total(p2, ("idn", H("ca")), ("idn", H("spb")))
+            xb, Y, ta = [out(n, h) for n in ("xb", "Y", "ta")]
+            bo, wo = H("bF"), w3
+            if last:
+                bo, wo = H("fb"), H("sp2")
+                decode(bo, H("bF"), H("tbp"), 512 + lo)
+                tt(wo, bo, w3, ALU.add)
+            tt(w3, H("bF"), w3, ALU.add)
+            tt(ta, bo, p2, ALU.add)
+            tt(H("dp"), w3, aP[h], ALU.subtract)
+            act(wx, w3, AF.Relu, bias=-15.5 * 16384, scale=16384.0)
             if h in SAMEV:
                 ts(ns, H("dp"), C4096, ALU.add, C4096, ALU.is_equal)
             else:
                 act(H("dp"), H("dp"), AF.Abs)
                 act(ns, H("dp"), AF.Relu, bias=-2047.5 * BIG, scale=BIG)
-            ts(H("bkc"), H("bk"), -16, ALU.bitwise_and)
-            tt(H("wbx"), H("Ia"), H("bkc"), ALU.add)
-            tt(w2, H("Ap"), H("ibp"), ALU.subtract)
-            tt(H("r1"), w2, H("aP"), ALU.max)
-            tt(w2, w3, H("r1"), ALU.max)
-            tt(H("rr"), w2, H("wbx"), ALU.max)
-            tt(H("tb"), H("aw"), cb, ALU.subtract)
-            tt(H("xb"), w3, H("tb"), ALU.max)
-            tt(w1, H("rr"), ns, ALU.mult if h in SAMEV else ALU.subtract)
-            tt(H("nb") if last else H("sb%d" % t), w1, H("xb"), ALU.max)
-            tt(w0, w0, H("ca"), ALU.subtract)
-            tt(H("xa"), w0, H("aP"), ALU.max)
-            Wn = B("W", 256 * h, 256 * h + 128)
-            tt(H("na") if last else Wn, w1, H("xa"), ALU.max)
+            dla, dlb = B("dl", 2 * lo, lo + hi), B("dl", lo + hi, 2 * hi)
+            dqa, dqb = B("dq%d" % h, 0, hi - lo), B("dq%d" % h, hi - lo)
+            total(dqa, ("idb", H("da")), ("idn", H("ibp")))
+            if not JOINT:
+                act(dla, dqa, AF.Relu)
+            total(dqb, ("idn", H("iap")), ("idk", H("kpb")), ("idw", H("k1b")))
+            if JOINT:
+                act(B("dl", 2 * lo, 2 * hi), dq, AF.Relu)
+            else:
+                act(dlb, dqb, AF.Relu)
+            tt(H("tb"), H("fy" if last else "aw"), wx, ALU.subtract)
+            tt(H("w1"), out("aP", h) if last else H("w1"), dla, ALU.add)
+            tt(H("bt"), wo, dlb, ALU.add)
+            tt(H("X"), H("w1"), H("bt"), ALU.max)
+            tt(xb, wo, H("tb"), ALU.max)
+            tt(Y, H("X"), ns, ALU.mult if h in SAMEV else ALU.subtract)
             if h:
                 behind("met", AHEAD[1])
             mark("met")
-            if last:
-                decode(H("sb%d" % t), H("nb"), ns, lo)
-                decode(Wn, H("na"), cb, lo)
-            act(H("sa%d" % t), B("W", 256 * h, 256 * h + 256), AF.Copy, by=sel)
-            for m in "ab":
-                send("%s%d%d" % (m, t, h))
-                if h:
-                    behind("%s%d0" % (m, t), AHEAD[3])
-            if not last and TWICE:
+            send("a%d%d" % (t, h), also="b%d%d" % (t, h))
+            if h:
+                behind("a%d0" % t, AHEAD[3])
+            if not last:
                 cp(B("pos", k0, k1), pos)
-                scatter(B("LB"), B("pos", k0, k1), H("sb%d" % t))
+                scatter(B(LB), B("pos", k0, k1), xb, Y)
                 if h:
                     behind("scatter", AHEAD[3])
-                mark("scatter")
-            elif not last and h:
-                cp(B("pos"), B("sb%d" % t, 256, 272))
-                scatter(B("LB"), B("pos"), B("sb%d" % t, 0, 256))
                 mark("scatter")
         if not last:
             for h in (2, 0, 1):
@@ -720,7 +912,7 @@ def record(T):
 
     expect("T%d" % NR)
     for c in range(4):
-        decode(B("yo", 256 * c, 256 * c + 256), B("TB4", 256 * c, 256 * c + 256), B("spare"), 256)
+        decode(B("yo", 256 * c, 256 * c + 256), B("TB4", 256 * c, 256 * c + 256), B("spare"), 256 * c)
     complete(NR, "yo")
     put("dma", "y", lambda e: e.dma_start(T.yent[:], ap(B("yo", 0, 1024))), [B("yo")], [], 4.5, sem="st", inc=16)
     return ops
@@ -734,7 +926,7 @@ def plan(T):
         ops = record(T)
         pre = links(ops)
         seq = arrange(ops, pre, WAKE)
-        ORDER["o"] = (pre, seq, [ops[i]["msg"] for i in seq if ops[i]["kind"] == "send"])
+        ORDER["o"] = (pre, seq, [m for i in seq if ops[i]["kind"] == "send" for m in ops[i]["msg"]])
     return ORDER["o"]
 
 
@@ -755,7 +947,7 @@ def rank_program(g, core, T, topo):
         if o["kind"] == "land":
             m = o["msg"]
             src = T.cores[(rank - MSG[m][3]) % n]
-            tok[i] = (m, sum(bits(topo.mask(((src,) + chain)[-1], core)) for chain, lo, hi in route(topo, T, src, core, m)))
+            tok[i] = (m, sum(bits(share(topo, T, ((src,) + chain)[-1], core, m)) for chain, lo, hi in route(topo, T, src, core, m)))
             continue
         need = {}
         for j in pre[i]:
@@ -775,14 +967,22 @@ def rank_program(g, core, T, topo):
             tok[i] = (o["sem"], o["inc"])
             o["fn"](eng[q]).then_inc(T.sem[o["sem"]], 16)
         else:
-            m = o["msg"]
-            dst = T.cores[(rank + MSG[m][3]) % n]
-            for chain, lo, hi in route(topo, T, core, dst, m):
-                to = (chain + (dst,))[0]
-                rid, pid = topo.addr(to, core)
-                mk = topo.mask(core, to)
-                g.remote_dma(view(T, MSG[m][1], lo, hi), view(T, MSG[m][0], lo, hi), T.sem[m], T.sem.lsem, pid, rid, mk)
-                sent += bits(mk)
+            folds = []
+            for m in o["msg"]:
+                dst = T.cores[(rank + MSG[m][3]) % n]
+                for chain, lo, hi in route(topo, T, core, dst, m):
+                    to = (chain + (dst,))[0]
+                    rid, pid = topo.addr(to, core)
+                    mk = share(topo, T, core, to, m)
+                    srcs = [view(T, s, lo, hi) for s in MSG[m][0]]
+                    if len(srcs) == 1:
+                        g.remote_dma(view(T, MSG[m][1], lo, hi), srcs[0], T.sem[m], T.sem.lsem, pid, rid, mk)
+                    else:
+                        folds.append(RemoteDMATransfer(dst_ids=[DstId(rid=rid, pnc=pid)], dma_engine_mask=mk, remote_sem=T.sem[m],
+                                                       srcs=srcs, dsts=[view(T, MSG[m][1], lo, hi)], alu_op=2))
+                    sent += bits(mk)
+            if folds:
+                g.remote_dma_fused(folds, local_sem=T.sem.lsem)
             continue
         snaps[tok[i]] = dict(known[q])
     g.wait_ge(T.sem.st, 16)

@@ -5,11 +5,11 @@ from concourse.mybir import AluOpType as ALU, ActivationFunctionType as AF, Axis
 NR = 4
 BIG = float(1 << 24)
 C16, C4096, C1 = 1.5 * (1 << 27), 1.5 * (1 << 35), 1.5 * (1 << 23)
-FV = (1, 3, 5)
+FV = (1, 3)
 PARTS = ((0, 8, "SSVV"), (8, 16, "SSVV"))
 AHEAD = (2.5, 2.5, 0.0, 1.5, 2.0)
 PEN = 2 * BIG
-SHIFT = {"S": 0.0, "M": 131072.0, "V": -131072.0}
+SHIFT = {"S": 131072.0, "M": 262144.0, "V": 0.0}
 LAT = {"A": 6.0, "U": 4.2, "T": 14.0, "f": 14.0, "b": 5.5, "a": 5.5, "c": 4.7}
 WAKE = 0.2
 FIX, FIXS = 0.0, 0.0
@@ -17,14 +17,25 @@ FIXP, SAME = 0.0, 0.25
 CY, G, SC, CALL = 0.00083, 1.3, 3.8, 0.7
 VFIRST = 2
 SAMEV = (1,)
-EH, ROWS, GK = True, True, (0, 1)
-US, ES, JOINT = True, True, True
+EH, ROWS, KI, TC, TAP, TBP, EX = (), True, True, False, False, False, (0, 1)
+W3P, FL = False, ("", "")
+HS, W1P, GI = 0, (0, 1), False
+JP, JE, JT, HF = 8, 4, 2, 1
+MOVE = {"p2": "pu", "wx": "tk", "ns": "pk"}
+SUMS, LS, DA = ((0, 1, 2), (0, 1, 2)), True, True
+EPV, HB, FV0 = (), (), (1, 3, 5, 7)
+US, JOINT = (0, 1), True
 PICKS = None
 JOG, TRIES = 0.5, 60
 WIDE = 2
-SWAPS, SLACK = 40000, 0.02
+LISTS = ("lstP", "lstQ", "lstI", "lst8", "off", "eu", "e16", "pos", "pos2", "sel")
+CASES = ((1.0, 1.3, 3.8, 0.2, 0.25, 1.0, 0.4), (1.1, 1.6, 3.0, 0.15, 0.18, 0.85, 0.35), (1.35, 2.2, 6.0, 0.2, 0.25, 1.15, 0.25))
+TURNS = 10
+SWAPS, SLACK = 4000, 0.02
 PASSES = 6
 
+DA, WIDE, PICKS, VFIRST, TRIES, SWAPS, TURNS = False, 0, (0, 2, 3, 1, 4, 5, 6, 7), 1, 10, 600, 45
+LS, SLACK, FV, W1P = True, 0.005, (1, 3, 5), ()
 SCRATCH, PART = {}, {}
 
 
@@ -43,21 +54,22 @@ def _ps(bank, **views):
 
 
 _sb("int32", entx=1024, wti=1, kpi=1, ci=1024, pmi=16, pmj=16, n1=512, q=256, k1=256, za=256, l5a=256, ui=32, ub=32,
-    ei=256, em=256, ky=32, er=32, qb=256, zb=256, l5b=256, jd=16)
-_sb("bfloat16", fx0=2064, fx2=2064, fx3=2064, one=128, blka=128, blk=128, idb=128, idn=128, idk=128, idw=128, zer=32, zz=576, dlt=16,
+    ei=256, em=256, ky=32, er=32, qb=256, zb=256, l5b=256, jd=16, kx=256)
+_sb("bfloat16", fx0=2064, fx2=2064, fx3=2064, one=128, blka=128, blk=128, idb=128, idn=128, idk=128, idw=128, idx=128, hid=128, cb=256, zer=32, zz=576, dlt=16,
     rA=256, rK=16, sgm=512, fl=16, spa=256, kpa=256, k1a=256, iap=256, ca=256, da=256, spb=256, kpb=256, k1b=256, ibp=256, dl=512,
-    blw=128, blx=128, thr=192, lab=256, Yg=4096, Ys=4096, Xb=4096, NM=4096, NM2=4096)
+    blw=128, blx=128, thr=192, lab=256, Yg=4096, Ys=4096, Xb=4096, ebx=256, erx=32, Ctb=1024, l5g=256, zag=256)
 SCRATCH["EQ"] = ("sbuf", [128, 16, 256], "bfloat16")
+SCRATCH["NM"] = SCRATCH["NM2"] = ("sbuf", [128, 16, 16, 16], "bfloat16")
 _sb("float16", eh=256, idh=128)
-_sb("uint16", lstP=16, lstI=16, lst8=4, off=256, eu=256, e16=16, ebc=256, pos=16, pos2=16, sel=16)
+_sb("uint16", lstP=16, lstQ=16, lstI=16, lst8=8, off=256, eu=256, e16=16, ebc=256, pos=16, pos2=16, sel=16)
 _sb("float32", old0=288, Ct=1024, la0=288, old1=288, iot=1024, la1=288, old2=288, TB0=1024, la2=288, old3=288, TB4=1024, la3=288, TB1=1320,
-    TB2=1320, TB3=1320, aw=256, sv=256, cap=16, pw=16, x128=192, t128=192, LB0=1320, LB1=1320, yo=1320, D=4096, idf=128, allf=128, pmf=16,
+    TB2=1320, TB3=1320, aw=256, sv=256, kv=256, cap=16, pw=16, x128=192, t128=192, LB0=1320, LB1=1320, yo=1320, D=4096, TC=1024, idf=128, allf=128, pmf=16,
     x16=16, cmk=16, lI=16, mio=256, wk=2, pr=256, x1=256, oc=256, oT=1536, kyf=16, sU=80, lU=80, uk=80, uq=32,
     sA=256, lA=256, ef=256, erf=32, wacc=3, ta=1, bF=256, dp=256, tb=256, bt=256, X=256, fa=256, fb=256, fy=256, ft=256,
-    d1=1024, d2=1024, ep=256, lpf=16, YP=8 * 288)
+    d1=1024, d2=1024, ep=256, lpf=16, lpq=2, xq=8, lcx=1, YP=8 * 288)
 for _t in range(NR):
-    _sb("float32", **{"xb%d" % _t: 288, "lb%d" % _t: 288, "ta%d" % _t: 288, "sc%d" % _t: 1, "lc%d" % _t: 1})
-    PART["Y%d" % _t] = (PART["YP"][0], PART["YP"][1] + 576 * _t, 288, "Y%d" % _t)
+    _sb("float32", **{"xb%d" % _t: 288, "lb%d" % _t: 288, "Y%d" % _t: 288, "sc%d" % _t: 1, "lc%d" % _t: 1})
+    PART["ta%d" % _t] = (PART["YP"][0], PART["YP"][1] + 576 * _t, 288, "ta%d" % _t)
     PART["aP%d" % _t] = (PART["YP"][0], PART["YP"][1] + 576 * _t + 288, 288, "aP%d" % _t)
     PART["win%d" % _t] = PART["old%d" % _t][:2] + (1600, "win")
 GAP, FAR = ("Ct", "iot", "TB0", "TB4"), 1312.0
@@ -73,6 +85,8 @@ for _h, (_k0, _k1, _) in enumerate(PARTS):
         _ps("m" + _h, **{"ns" + _h: (2 * _n, _n), "wx" + _h: (3 * _n, _n)})
     else:
         _ps("tk", **{"ns" + _h: (0, _n), "wx" + _h: (256, _n)})
+    for _v, _b in MOVE.items():
+        PART[_v + _h] = {"tk": ("tk", 16 * _k0, _n, "tk"), "pk": ("pk" + _h, 128, _n, "pk" + _h), "pu": ("pu", 256 + 16 * _k0, _n, "pu")}[_b]
 for _i, _n in enumerate(("zS", "zM", "zP", "zw")):
     PART[_n] = (PART["zz"][0], PART["zz"][1] + 144 * _i, 144, "zz")
 
@@ -106,7 +120,7 @@ def messages(n):
 
 
 MSG = messages(8)
-SEMAPHORES = ["qv", "qs", "qp", "qg", "ld0", "ld1", "ld4", "ld5", "ld6", "st", "lsem"] + ["oc%d" % _i for _i in range(2 * NR)] + sorted(MSG)
+SEMAPHORES = ["qv", "qs", "qp", "qg", "ld0", "ld1", "ld4", "ld5", "ld6", "st", "lsem"] + ["oc%d" % _i for _i in range(2 * NR)] + ["t%s%d" % (_c, _i) for _i in range(NR) for _c in "cd"] + sorted(MSG)
 
 
 def bits(m):
@@ -186,12 +200,12 @@ def B(name, lo=0, hi=None, st=1):
 
 
 def rows(k0, k1, lo, hi):
-    return ("EQ", 256 * k0 + lo, 256 * (k1 - 1) + hi, 1, "EQ", (k0, k1, lo, hi))
+    return ("EQ", 256 * k0 + lo, 256 * (k1 - 1) + hi, 1, "EQ", ((k0, k1) if k1 > k0 + 1 else k0, (lo, hi)))
 
 
 def width(x):
     if len(x) > 5:
-        return (x[5][1] - x[5][0]) * (x[5][3] - x[5][2])
+        return math.prod(i[1] - i[0] for i in x[5] if isinstance(i, tuple))
     return (x[2] - x[1] + x[3] - 1) // x[3]
 
 
@@ -228,17 +242,31 @@ def links(ops):
     return out
 
 
-def polish(ops, pre, seq, wake):
-    n = len(ops)
-    dur = [o["dur"] for o in ops]
-    hold = [o["dur"] if o["kind"] in ("run", "send") else 0.05 for o in ops]
-    q = [o["q"] if o["kind"] != "land" else None for o in ops]
-    dep = [[(j, dur[j] + (0.0 if ops[j]["kind"] == "send" else wake if q[i] != q[j] else SAME)) for j in pre[i]
-            if not (q[i] == "p" and q[j] == "p") and (ops[j]["kind"] != "send" or q[i] is None)] for i in range(n)]
-    banks = [[([b + r for r in "vsp" if r != q[i]], b + q[i]) for b in ops[i]["banks"]] for i in range(n)]
-    needs = [set(pre[i]) | set(j for j, lag in ops[i]["behind"] if ops[i]["kind"] != "run") for i in range(n)]
+def lasts(o, case):
+    if o["kind"] != "run":
+        return o["dur"] * (case[5] if o["kind"] == "land" else 1.0)
+    if "each" in o:
+        return o["dur"] + o["each"][0] * CY * (case[o["each"][1]] - (G, SC)[o["each"][1] - 1])
+    return o["dur"] * case[0]
 
-    def run(seq, at, was):
+
+def polish(ops, pre, seq, wake, turn):
+    n = len(ops)
+    q = [o["q"] if o["kind"] != "land" else None for o in ops]
+    banks = [[([b + r for r in "vsp" if r != q[i]], b + q[i]) for b in ops[i]["banks"]] for i in range(n)]
+    needs = [set(pre[i]) | set(j for j, lag in ops[i]["behind"] if ops[i]["kind"] != "run" or "firm" in ops[i]) for i in range(n)]
+    cases = []
+    for case in CASES:
+        dur = [lasts(o, case) for o in ops]
+        cases.append((dur, [dur[i] if ops[i]["kind"] in ("run", "send") else 0.05 for i in range(n)],
+                      [[(j, dur[j] + (0.0 if ops[j]["kind"] == "send" else case[3] if q[i] != q[j] else case[4])) for j in pre[i]
+                        if not (q[i] == "p" and q[j] == "p") and (ops[j]["kind"] != "send" or q[i] is None)] for i in range(n)], case[3]))
+
+    def runs(seq, at, was):
+        got = [run(seq, at, was and was[1][c], *cases[c]) for c in range(len(cases))]
+        return sum(got[c][0] * CASES[c][6] for c in range(len(cases))), got
+
+    def run(seq, at, was, dur, hold, dep, wake):
         at -= at % 64
         st, by, marks = (list(was[2]), list(was[3]), was[4][:at // 64]) if at else ([0.0] * n, [-1] * n, [])
         last, end, who = (dict(was[4][at // 64]) if at else {}), 0.0, -1
@@ -284,21 +312,22 @@ def polish(ops, pre, seq, wake):
             return None
         return seq[:pa] + [i for i in mid if i not in move] + [i for i in mid if i in move] + seq[pb + 1:]
 
-    seed = [7]
+    seed = [7 + turn]
 
     def draw(k):
         seed[0] = (seed[0] * 1103515245 + 12345) % 2147483648
         return (seed[0] >> 8) % k
-    cur, left = run(seq, 0, None), SWAPS
-    best = (cur[0], seq)
+    cur, left = runs(seq, 0, None), SWAPS
+    best = (cur[0], seq, cur[1][0][2])
     while left > 0:
         place = {i: x for x, i in enumerate(seq)}
-        seq = sorted(seq, key=lambda i: (cur[2][i], place[i]))
-        cur = run(seq, 0, None)
+        seq = sorted(seq, key=lambda i: (cur[1][0][2][i], place[i]))
+        cur = runs(seq, 0, None)
         for _ in range(40):
-            place, pairs, i = {i: x for x, i in enumerate(seq)}, [], cur[1]
-            while cur[3][i] != -1:
-                j = cur[3][i]
+            one = cur[1][draw(len(cases))]
+            place, pairs, i = {i: x for x, i in enumerate(seq)}, [], one[1]
+            while one[3][i] != -1:
+                j = one[3][i]
                 if j < -1:
                     j = -2 - j
                     pairs.append((j, i))
@@ -312,15 +341,15 @@ def polish(ops, pre, seq, wake):
                 while hop and not forth and k and pairs[k - 1][0] == b:
                     k, b, hop = k - 1, pairs[k - 1][1], hop - 1
                 other = swap(seq, place[a], place[b], forth)
+                bar = cur[0] - SLACK * math.log((draw(1000) + 1) / 1001)
                 if other:
-                    new = run(other, place[a], cur)
-                    if new[0] < cur[0] - SLACK * math.log((draw(1000) + 1) / 1001):
+                    new = runs(other, place[a], cur)
+                    if new[0] < bar:
                         seq, cur = other, new
                         break
             if cur[0] < best[0]:
-                best = (cur[0], seq)
-    ORDER["end"] = best[0]
-    return best[1]
+                best = (cur[0], seq, cur[1][0][2])
+    return best
 
 
 def arrange(ops, pre, wake):
@@ -395,7 +424,19 @@ def arrange(ops, pre, wake):
         if turn < PASSES:
             late = place(bwd, fwd, lambda i: (-start[i] - dur[i], -i))
     ORDER["end"] = best[0]
-    seq, seen = polish(ops, pre, sorted(range(n), key=lambda i: (best[1][i], i)), wake), {}
+    soft = set((j, i) for i in range(n) for j, lag in ops[i]["behind"] if ops[i]["kind"] == "run" and j not in pre[i] and "firm" not in ops[i])
+    fwd = [[e for e in fwd[j] if (j, e[0]) not in soft] for j in range(n)]
+    bwd = [[e for e in bwd[i] if (e[0], i) not in soft] for i in range(n)]
+    start, best = best[1], None
+    for turn in range(TURNS):
+        got = polish(ops, pre, sorted(range(n), key=lambda i: (start[i], i)), wake, turn)
+        if best is None or got[0] < best[0]:
+            best = got
+        start = (got if got[0] < best[0] + 1.0 else best)[2]
+        late = place(bwd, fwd, lambda i: (-start[i] - dur[i], -i))
+        start = place(fwd, bwd, lambda i: (-late[i] - dur[i], i))
+    ORDER["end"] = best[0]
+    seq, seen = best[1], {}
     for i in seq:
         for b in ops[i]["banks"]:
             pre[i] = pre[i] + [seen[b + r] for r in "vsp" if r != ops[i]["q"] and b + r in seen]
@@ -409,10 +450,22 @@ def record(T):
     def put(kind, q, fn, r, w, dur, after=(), **more):
         d = {"kind": kind, "q": q, "fn": fn, "r": list(r), "w": list(w), "dur": dur, "after": list(after), "behind": []}
         d.update(more)
+        if kind == "run" and q in "vs" and any(SCRATCH[x[0]][2] == "uint16" and x[4] in LISTS for x in r) and (w[0][4] not in LISTS or len(r) > 1):
+            n = (dur - (0.05 if q == "v" else 0.065)) / CY
+            d["each"] = (n / SC, 2) if r[-1][4] in ("pos", "pos2") else (n / G, 1)
         key = (q,) + tuple((w or r or [(kind, 0, 0, 0, kind)])[0][1:3]) + ((w or r or [(kind, 0, 0, 0, kind)])[0][4].rstrip("0123"),)
         seen[key] = seen.get(key, 0) + 1
         d["role"] = key + (seen[key],)
         ops.append(d)
+
+    def join(k):
+        first = ops[-k]
+        for o in ops[len(ops) - k + 1:]:
+            first["more"] = first.get("more", []) + [o["fn"]]
+            first["r"] += [x for x in o["r"] if x not in first["r"]]
+            first["w"] += [x for x in o["w"] if x not in first["w"]]
+            first["dur"] += o["dur"]
+        del ops[len(ops) - k + 1:]
 
     def mark(name):
         where[name] = len(ops) - 1
@@ -423,8 +476,7 @@ def record(T):
     def ap(x):
         name, lo, hi, st = x[:4]
         if len(x) > 5:
-            k0, k1, lo, hi = x[5]
-            return T[name][:, k0, lo:hi] if k1 == k0 + 1 else T[name][:, k0:k1, lo:hi]
+            return T[name][(slice(None),) + tuple(slice(*i) if isinstance(i, tuple) else i for i in x[5])]
         return T[name][:, lo:hi:st] if st != 1 else T[name][:, lo:hi]
 
     def val(s):
@@ -538,11 +590,10 @@ def record(T):
     cp(B("fx0", 2056, 2057), B("wti"))
     cp(B("fx0", 2057, 2058), B("kpi"))
     ms(B("one"), 1.0)
+    ms(B("sU", 16, 64), 0.0)
     iota(B("ci"), [[37, 1024]], 0, 0)
     iota(B("pmi"), [[0, 16]], 0, 1)
     iota(B("x16"), [[1, 16]], 0, 0)
-    for k0, k1, path in PARTS:
-        iota(B("mio", 16 * k0, 16 * k1), [[1, 16], [0, k1 - k0]], 0, 0)
     sift(B("blka"), B("one"), [[-16, 8], [0, 16]], ALU.is_ge, 0.0, 0, 1)
     sift(B("blk"), B("blka"), [[16, 8], [0, 16]], ALU.is_ge, 0.0, 15, -1)
     sift(B("idb"), B("one"), [[-1, 128]], ALU.is_equal, 0.0, 0, 1)
@@ -566,6 +617,12 @@ def record(T):
         tt(B("lpf", k0, k1), B("lpf", k0, k1), B("lI", 0, nk), ALU.add)
         ts(B("lstP", k0, k1), B("lpf", k0, k1), 16.0, ALU.mult)
         ts(B("lst8", 2 * h, 2 * h + 1), pm, nk - 1.0, ALU.min)
+        ts(B("lst8", 4 + 2 * h, 5 + 2 * h), pm, *((nk - 1.0, ALU.min) if h else (nk - 16.0, ALU.add)))
+    ts(B("jd", 0, 1), B("pmj", 0, 1), 1, ALU.bitwise_and)
+    for k0, k1, path in PARTS:
+        ts(B("lpq", 0, 1), B("jd", 0, 1), 7.5 * (k1 - k0), ALU.mult)
+        ts(B("lpq", 1, 2), pm, (k1 - k0) / 2, ALU.mult, B("lpq", 0, 1), ALU.add)
+        ts(B("lstQ", k0, k1), B("x16", 0, k1 - k0), B("lpq", 1, 2), ALU.add)
     ts(B("cap"), B("lI"), -1.0, ALU.mult, FAR, ALU.add)
     ms(B("lab"), 4 * BIG)
     ts(B("lab", 0, 241, 16), B("lI"), -1.0, ALU.mult)
@@ -576,14 +633,15 @@ def record(T):
     for h, (k0, k1, path) in enumerate(PARTS):
         for j in range(272, 272 + k1 - k0) if h else range(16 - k1, 16):
             act(B("YP", j, 8 * 288, 288), B("one", 0, 8), AF.Copy, scale=-4096.0)
-            ops[-1]["w"] = [B(n + str(t), j, j + 1) for n in ("Y", "aP") for t in range(NR)]
+            ops[-1]["w"] = [B(n + str(t), j, j + 1) for n in ("ta", "aP") for t in range(NR)]
     for k0, k1, path in PARTS:
-        n = 16 * (k1 - k0) // len(path)
+        n = 16 // len(path)
         for c in range(len(path)):
-            at = 16 * k0 + n * c
-            act(B("rA", at, at + n), B("mio", at, at + n), AF.Identity, bias=15360.0 + SHIFT[path[c]], scale=-1024.0)
+            act(B("mio", n * c, n * c + n), B("x16", n * c, n * c + n), AF.Identity, bias=15360.0 + SHIFT[path[c]], scale=-1024.0)
+        for m in range(16):
+            act(B("rA", 16 * k0 + m % 8 * 2 + m // 8, 16 * k1, 16), B("one", 0, k1 - k0), AF.Copy, scale=B("mio", m, m + 1))
     act(B("idf"), B("idb"), AF.Copy)
-    for n, s in (("idn", -1.0), ("idk", 1 / PEN), ("idw", 6.5)):
+    for n, s in (("idn", -1.0), ("idk", 1 / PEN), ("idw", 6.5), ("idx", 16.0), ("hid", 1.5 * (1 << 22))):
         act(B(n), B("idb"), AF.Copy, scale=s)
     for n, s in (("zS", -8192.0), ("zM", -16384.0), ("zP", 16384.0)):
         act(B(n, 15, 128, 16), B("blk", 0, 113, 16), AF.Copy, scale=s)
@@ -633,9 +691,10 @@ def record(T):
             expect("b%d%d" % (c, h))
             cp(B("pos2", k0, k1), vals(lb, h)[1])
         scatter(B(name), B("pos2"), B(lb, 16, 272))
+        mark("whole")
 
-    ID = B("lstI")
-    act(B("ctp"), cls("Ct", 0), AF.Copy)
+    act(B("Ctb"), B("Ct"), AF.Copy)
+    mm(B("ctp"), B("idb"), cls("Ctb", 0), True, True)
     for t in range(NR):
         last = t == NR - 1
         seen.clear()
@@ -664,34 +723,51 @@ def record(T):
             ts(B("off", lo, hi), B("pr", lo, hi), 2.0 ** (-16 if t else -4), ALU.mult, 127.0 / 256 if t else 0.0, ALU.add, by=B("lstP", k0, k1))
             for c in range(k0 // 2, k1 // 2):
                 o, l = B("Yg", 512 * c, 512 * c + 512), B("off", 32 * c, 32 * c + 32)
-                if c in FV:
+                if c in (FV if t else FV0):
                     pick(o, B(fx, 0, 2049), l)
                 else:
                     act(o, B(fx, 0, 2049), AF.Copy, by=l)
+                mark("look%d" % c)
+                if h and HF and ops[-1]["q"] == "v":
+                    behind("scan")
+                    ops[-1]["firm"] = True
                 scan(B("Ys", 512 * c, 512 * c + 512), B("sgm"), o)
+                if h and HF > 1:
+                    behind("scan")
+                    ops[-1]["firm"] = True
+                if not h:
+                    mark("scan")
                 for p in range(32 * (c - k0 // 2) // nk, 32 * (c + 1 - k0 // 2) // nk):
-                    mm(B("up", k0, k1), slide("zw", p), B("Ys", 16 * (lo + nk * p) + 15, 16 * (lo + nk * p + nk), 16), p == 0, p == 15)
+                    mm(B("w3%d" % h, 0, nk), slide("zw", p), B("Ys", 16 * (lo + nk * p) + 15, 16 * (lo + nk * p + nk), 16), p == 0, p == 15)
+                join(32 * (c + 1 - k0 // 2) // nk - 32 * (c - k0 // 2) // nk)
             ui, ub, uq, few = B("ui", 16 * h, 16 * h + nk), B("ub", 16 * h, 16 * h + nk), B("uq", 16 * h, 16 * h + nk), B("lst8", 2 * h, 2 * h + 1)
-            cp(ui, B("up", k0, k1))
+            cp(ui, B("w3%d" % h, 0, nk))
             if h:
                 behind("sum", AHEAD[4])
             mark("sum")
             ts(ub, ui, 4095, ALU.bitwise_and)
             at = 16 + 32 * h
-            act(B(U, at, at + 16), ub, AF.Copy, by=few)
-            act(B("uq", 16 * h, 16 * h + 16), ub, AF.Square, by=few)
-            act(B(U, at + 16, at + 16 + nk), uq, AF.Identity, scale=2.0 ** -5, bias=(15.5 if t else 0.0) - 13.0 / 32)
+            more = (15.5 if t else 0.0) - 13.0 / 32
+            if h in US:
+                act(B(U, at, at + 16), ub, AF.Copy, by=few)
+                act(B("uq", 16 * h, 16 * h + 16), ub, AF.Square, by=few)
+                act(B(U, at + 16, at + 16 + nk), uq, AF.Identity, scale=2.0 ** -5, bias=more)
+            else:
+                tt(uq, ub, ub, ALU.mult)
+                cp(B(U, at, at + nk), ub)
+                ts(B(U, at + 16, at + 16 + nk), uq, 2.0 ** -5, ALU.mult, more, ALU.add)
             if not t:
                 send("U%d" % h)
         if not t:
             for h in range(2):
                 expect("A%d" % h)
             A, U = B("lA"), "lU"
-            tt(B("q"), B("ctp"), A, ALU.add)
-            act(B("a75"), A, AF.Identity, bias=-7.5)
-        act(B("x1"), B("a75"), AF.Identity, bias=C16)
-        act(B("oc"), B("x1"), AF.Identity, bias=-C16)
+            for h in range(2):
+                tt(half(B("q"), h), half(B("ctp"), h), half(A, h), ALU.add)
+                act(half(B("a75"), h), half(A, h), AF.Identity, bias=-7.5)
         for h, (k0, k1, path) in enumerate(PARTS):
+            act(half(B("x1"), h), half(B("a75"), h), AF.Identity, bias=C16)
+            act(half(B("oc"), h), half(B("x1"), h), AF.Identity, bias=-C16)
             n, reps = 16 * (k1 - k0), 16 // len(path)
             first = 1 if t else reps
             for j in range(first):
@@ -700,33 +776,49 @@ def record(T):
             for j in range(1, reps):
                 o, a = B("oT", 768 * h + n * j, 768 * h + n * j + n), B("oT", 768 * h, 768 * h + n)
                 put("dma", "y", lambda e, o=o, a=a: e.dma_start(ap(o), ap(a)), [a], [o], 2.2, sem="oc%d" % (2 * t + h), inc=16 * (reps - 1))
-        ts(B("za"), B("q"), 0x3801F, ALU.bitwise_and)
-        ts(B("l5a"), B("q"), 31, ALU.bitwise_and)
-        act(B("spa"), B("l5a"), AF.Relu, bias=(tau + 0.5) * PEN, scale=-PEN, by=ID)
-        act(B("kpa"), B("za"), AF.Relu, bias=(tau + 0.5) * PEN, scale=-PEN, by=ID)
-        act(B("k1a"), B("kpa"), AF.Sign)
+                mark("own")
 
         def total(o, *terms):
             for j, (l, r) in enumerate(terms):
                 mm(o, B(l), r, j == 0, j == len(terms) - 1)
-        total(B("w1"), ("idb", B("kpa")), ("idn", B("spa")), ("idf", A))
-        total(B("sp2"), ("idf", A), ("idn", B("spa")))
-        act(B("aw"), B("sp2"), AF.Relu)
-        if last:
-            decode(B("fy"), B("aw"), B("sp2"), 256)
-        total(B("tbp"), ("idk", B("kpa")), ("idw", B("k1a")))
-        act(B("da"), B("tbp"), AF.Copy)
 
         def out(name, h):
             return vals(name + str(t), h)[0]
         aP = [half(B("fa"), h) if last else out("aP", h) for h in range(2)]
-        for h in range(2):
-            act(aP[h], half(B("w1"), h), AF.Relu)
+        cut = -9.5
+        for k0, k1 in [x[:2] for x in PARTS] if LS else [(0, 16)]:
+            lo, hi, each = 16 * k0, 16 * k1, B("lstI", 0, k1 - k0)
+            mine = (A[0], A[1] + lo * A[3], A[1] + (hi - 1) * A[3] + 1) + A[3:]
+
+            def H(n):
+                return B(n, lo, hi)
+            ts(H("za"), H("q"), 0x3801F, ALU.bitwise_and)
+            ts(H("l5a"), H("q"), 31, ALU.bitwise_and)
+            l5a, za = H("l5a"), H("za")
+            if GI:
+                l5a, za, each = H("l5g"), H("zag"), None
+                gcp(za, H("za"))
+                gcp(l5a, H("l5a"))
+            act(H("spa"), l5a, AF.Relu, bias=(tau + 0.5) * PEN, scale=-PEN, by=each)
+            act(H("kpa"), za, AF.Relu, bias=(tau + 0.5) * PEN, scale=-PEN, by=each)
+            act(H("k1a"), H("kpa"), AF.Sign)
+            total(H("w1"), ("idb", H("kpa")), ("idn", H("spa")), ("idf", mine))
+            total(H("sp2"), ("idf", mine), ("idn", H("spa")))
+            act(H("aw"), H("sp2"), AF.Relu)
             if last:
-                decode(out("aP", h), aP[h], half(B("ctp"), h), 16 * PARTS[h][0])
-        act(B("ca"), B("w1"), AF.Relu, bias=-15.5 * 16384, scale=16384.0)
-        mark("lanes")
-        act(B("iap"), B("l5a"), AF.Relu, bias=31 * BIG, scale=-2 * BIG, by=ID)
+                decode(H("fy"), H("aw"), H("sp2"), 256 + lo)
+            if DA:
+                total(H("tbp"), ("idk", H("kpa")), ("idw", H("k1a")))
+                act(H("da"), H("tbp"), AF.Identity, bias=-cut)
+            for h in range(2):
+                if k0 <= PARTS[h][0] < k1:
+                    act(aP[h], half(B("w1"), h), AF.Relu)
+                    if last:
+                        decode(out("aP", h), aP[h], half(B("ctp"), h), 16 * PARTS[h][0])
+            act(H("ca"), H("w1"), AF.Relu, bias=-15.5 * 16384, scale=16384.0)
+            if not k0:
+                mark("lanes")
+            act(H("iap"), l5a, AF.Relu, bias=31 * BIG, scale=-2 * BIG, by=each)
         if t:
             expect("T%d" % t)
             complete(t, TB)
@@ -736,12 +828,17 @@ def record(T):
             for h in range(2):
                 expect("U%d" % h)
         send("T%d" % (t + 1), [] if t else [B("lU")])
+        if t:
+            behind("own", 1.5)
         if t + 2 < NR:
             send("f%d" % (t + 2))
             behind("T%d" % (t + 1))
         if not last:
             gcp(cls(LB, t + 1), cls(TB, t + 1))
         RT = B(TB, 0, 1024)
+        if TC:
+            put("dma", "y", lambda e: e.dma_start(ap(B("TC")), ap(B("Ct"))), [B("Ct")], [B("TC")], 3.0, sem="tc%d" % t, inc=16)
+            put("dma", "g", lambda e, a=RT: e.dma_start(ap(B("TC")), ap(a), accum_op=ALU.add), [RT, B("TC")], [B("TC")], 6.0, sem="td%d" % t, inc=16)
 
         for h, (k0, k1, path) in enumerate(PARTS):
             lo, hi, nk = 16 * k0, 16 * k1, k1 - k0
@@ -755,13 +852,23 @@ def record(T):
             for k in range(k0, k1):
                 at = 16 + 32 * h + k - k0
                 act(B("ep", lo + k - k0, hi, nk), B(U, 0, 16), AF.Identity, bias=B(U, at + 16, at + 17), scale=B(U, at, at + 1))
+                if (k - k0) % JE == JE - 1:
+                    join(JE)
+            if t and not h:
+                for c in HB:
+                    ops[where["look%d" % c]]["behind"].append((len(ops) - 1, 0.0))
+                    ops[where["look%d" % c]]["firm"] = True
             ts(H("ei"), H("ep"), B("lc%d" % (t - 1)) if t else 0.0, ALU.add)
             ts(H("em"), H("ei"), 1023, ALU.bitwise_and)
             cp(H("eu"), H("em"))
-            if EH:
-                cp(H("eh"), H("eu"))
+            if t and not h and HS:
+                ops[where["whole"]]["behind"].append((len(ops) - HS, 0.0))
+                ops[where["whole"]]["firm"] = True
+            mc = 16 // len(path)
+            if h in EH:
+                pick(H("eh"), H("em"), B("lstQ", k0, k1))
             else:
-                act(H("ef"), H("em"), AF.Copy, by=B("lstI", 0, nk))
+                act(H("ef"), H("em"), AF.Copy, by=B("lstQ", k0, k1))
             own = B("oT", 768 * h, 768 * h + 16 * cw)
             for c in range(len(path)):
                 l = B("eu", lo + cw * c, lo + cw * c + cw)
@@ -783,54 +890,83 @@ def record(T):
                     act(ch("D" if path[c] == "S" else "Xb", c0, n), ch("D", c0, n), AF.Abs)
                     if h or c0:
                         behind("sign")
+                ms_ = range(mc * c0, mc * (c0 + n))
+
+                def one(name, m):
+                    return B(name, 16 * lo + 16 * nk * m, 16 * lo + 16 * nk * (m + 1))
+
+                def turned(name, m):
+                    return (name, 0, 1, 1, "%s.%d.%d." % (name, h, m), ((k0, k1), m, (0, 16)))
                 if path[c] == "S":
                     act(ch("D", c0, n), ch("D", c0, n), AF.Abs, bias=-1032.25)
-                    act(ch("NM", c0, n), ch("D", c0, n), AF.Sign, bias=-1024.0)
+                    for m in ms_:
+                        act(turned("NM", m), one("D", m), AF.Sign, bias=-1024.0)
+                        if m % JT == JT - 1:
+                            join(JT)
                     mark("sign")
                 elif path[c] == "M":
                     mark("sign")
                     ts(ch("Xb", c0, n), ch("Xb", c0, n), 3000.0, ALU.min, 262144.0 + 1016.0, ALU.add)
-                    act(ch("NM", c0, n), ch("Xb", c0, n), AF.Square, bias=-129.0, scale=2.0 ** -11)
+                    for m in ms_:
+                        act(turned("NM", m), one("Xb", m), AF.Square, bias=-129.0, scale=2.0 ** -11)
                 else:
-                    ts(ch("NM", c0, n), ch("Xb", c0, n), C16, ALU.add, C16, ALU.is_equal)
-                    ts(ch("NM2", c0, n), ch("Xb", c0, n), C4096, ALU.add, C4096, ALU.is_equal)
+                    for name, cc in (("NM", C16), ("NM2", C4096)):
+                        for m in ms_:
+                            ts(turned(name, m), one("Xb", m), cc, ALU.add, cc, ALU.is_equal)
+                            if m % JT == JT - 1:
+                                join(JT)
                     if VFIRST > 1:
                         mark("pick")
             key = "key%d" % h
             mm(B(key, 0, 16 * nk), B("idb"), H("rA"), True, False)
-            mm(B(key, 0, 16 * nk), B("idh" if EH else "idf"), H("eh" if EH else "ef"), False, False)
+            mm(B(key, 0, 16 * nk), B("idh" if h in EH else "idf"), H("eh" if h in EH else "ef"), False, False)
             runs = []
             for c in range(len(path)):
-                if runs and path[runs[-1][0]] == path[c] and cw * runs[-1][1] < 64:
+                if runs and path[runs[-1][0]] == path[c] and runs[-1][1] < 2:
                     runs[-1][1] += 1
                 else:
                     runs.append([c, 1])
             todo = []
             for c, n in sorted(runs, key=lambda r: VFIRST and path[r[0]] != "V"):
+                m0, m1 = mc * c, mc * (c + n)
                 for z, src in {"S": [("zS", "NM")], "M": [("zM", "NM")], "V": [("zM", "NM"), ("zP", "NM2")]}[path[c]]:
                     for p in range(16):
-                        todo.append((B(key, cw * c, cw * (c + n)), slide(z, p), B(src, 16 * (lo + cw * c) + p, 16 * (lo + cw * (c + n)), 16)))
-            for i, (o, l, r) in enumerate(todo):
+                        todo.append((B(key, m0 // 8, 16 * nk, 2), slide(z, p), (src, 0, 1, 1, src, ((k0, k1), (m0, m1), p)),
+                                     [turned(src, m) for m in range(m0, m1)]))
+            todo = [x for j in SUMS[h] for x in todo[16 * j:16 * j + 16]]
+            for i, (o, l, r, reads) in enumerate(todo):
                 mm(o, l, r, False, i == len(todo) - 1)
-            for k in range(k0, k1):
-                most(B("kyf", k, k + 1), B(key, k - k0, 16 * nk, nk))
+                ops[-1]["r"] += reads
+                if i % JP == JP - 1:
+                    join(JP)
+            ky, er = [B(n, 16 * h, 16 * h + nk) for n in ("ky", "er")]
+            scan(H("kx" if KI else "kv"), B("sgm", 0, hi - lo), B(key, 0, 16 * nk))
             behind("keys" if h else "lanes", AHEAD[0 if h else 2])
             mark("keys")
-            ky, er, erf = [B(n, 16 * h, 16 * h + nk) for n in ("ky", "er", "erf")]
-            cp(ky, B("kyf", k0, k1))
+            if KI:
+                ky = B("kx", lo + 15, hi, 16)
+            else:
+                cp(ky, B("kv", lo + 15, hi, 16))
             ts(er, ky, 1023, ALU.bitwise_and)
             cp(B("e16", k0, k1), er)
-            if ES:
-                act(B("erf", 16 * h, 16 * h + 16), er, AF.Copy, by=B("lst8", 2 * h, 2 * h + 1))
-            else:
-                cp(erf, er)
+            erf, z = vals("xb%d" % t, h)[1], vals("Y%d" % t, h)[1]
+            act(B("xb%d" % t, 272 * h, 272 * h + 16), er, AF.Copy, by=B("lst8", 4 + 2 * h, 5 + 2 * h))
             e = B("e16", k0, k1)
-            pick(H("ebc"), B("iot"), e)
+            if h in EX:
+                act(H("ebx"), B("iot"), AF.Exp, scale=0.01, by=e)
+            else:
+                pick(H("ebc"), B("iot"), e)
+            if 1 in EX or h in EX:
+                act(B("erx", 16 * h, 16 * h + 16), er, AF.Exp, scale=0.01, by=B("lst8", 2 * h, 2 * h + 1))
             mm(H("pcp"), B("idb"), B("thr", 0, hi - lo), True, False)
             for k in range(k1):
                 a, at = max(16 * k, lo), 16 * k if k >= k0 else 0
-                j = k if k < PARTS[0][1] else 16 + k - k0
-                ts(rows(k, k + 1, a - at, hi - at), B("ebc", a, hi), B("erf", j, j + 1), ALU.is_equal)
+                j = 16 - PARTS[0][1] + k if k < PARTS[0][1] else 272 + k - k0
+                s = B("xb%d" % t, j, j + 1)
+                if h in EX:
+                    j = k if k < PARTS[0][1] else 16 + k - k0
+                    s = B("erx", j, j + 1)
+                ts(rows(k, k + 1, a - at, hi - at), B("ebx" if h in EX else "ebc", a, hi), s, ALU.is_equal)
                 a = max(16 * k + 16, lo)
                 if a < hi:
                     mm(B("pcp", a, hi), B("blx"), rows(k, k + 1, a - at, hi - at), False, False)
@@ -840,35 +976,43 @@ def record(T):
                 mm(H("pcp"), B("blw"), rows(k0, k1, 0, 16), False, True)
             scan(H("sv"), H("lab"), H("pcp"), 0.0, ALU.min)
             sv = B("sv", lo + 15, hi, 16)
-            z, pos = [vals(n + str(t), h)[1] for n in ("ta", "xb")]
             act(B("fl", k0, k1), sv, AF.Sign, bias=-600.0, accum=B("wacc", h, h + 1))
             tt(z, sv, B("cap", k0, k1), ALU.min)
-            tt(pos, z, erf, ALU.max)
             w3, p2, ns, wx, dq = [B(n + str(h)) for n in ("w3", "p2", "ns", "wx", "dq")]
             act(H("bF"), RT, AF.Copy, by=e)
-            pick(H("qb"), B("Ct"), e, H("bF"), ALU.add)
+            if TC:
+                pick(H("qb"), B("TC"), e)
+            else:
+                pick(H("qb"), B("Ct"), e, H("bF"), ALU.add)
             ts(H("zb"), H("qb"), 0x3801F, ALU.bitwise_and)
             ts(H("l5b"), H("qb"), 31, ALU.bitwise_and)
             each = B("lstI", 0, nk)
-            act(H("kpb"), H("zb"), AF.Relu, bias=(tau + 0.5) * PEN, scale=-PEN, by=each)
+            act(H("k1b"), H("zb"), AF.Sign, bias=tau + 0.5, scale=-1.0, by=each)
+            act(H("kpb"), H("l5b"), AF.Sign, bias=-tau - 0.5, by=each)
             act(H("spb"), H("l5b"), AF.Relu, bias=(tau + 0.5) * PEN, scale=-PEN, by=each)
-            act(H("ibp"), H("l5b"), AF.Relu, bias=31 * BIG, scale=-2 * BIG, by=each)
-            if h in GK:
-                act(H("k1b"), H("zb"), AF.Sign, bias=tau + 0.5, scale=-1.0, by=each)
+            if "i" in FL[h]:
+                ts(H("ibp"), H("l5b"), 15.5, ALU.is_lt, PEN, ALU.mult)
             else:
-                act(H("k1b"), H("kpb"), AF.Sign)
-            total(w3, ("idb", H("kpb")), ("idn", H("spb")))
-            total(p2, ("idn", H("ca")), ("idn", H("spb")))
+                act(H("ibp"), H("l5b"), AF.Relu, bias=31 * BIG, scale=-2 * BIG, by=each)
+            if W3P:
+                total(w3, ("idf", H("bF")), ("hid", H("kpb")), ("hid", H("k1b")))
+            else:
+                total(w3, ("hid", H("kpb")), ("hid", H("k1b")))
+                tt(w3, H("bF"), w3, ALU.add)
             xb, Y, ta = [out(n, h) for n in ("xb", "Y", "ta")]
             bo, wo = H("bF"), w3
             if last:
                 bo, wo = H("fb"), H("sp2")
-                decode(bo, H("bF"), H("tbp"), 512 + lo)
-                tt(wo, bo, w3, ALU.add)
-            tt(w3, H("bF"), w3, ALU.add)
-            tt(ta, bo, p2, ALU.add)
+                decode(bo, H("bF"), wo, 512 + lo)
+                total(wo, ("idf", bo), ("hid", H("kpb")), ("hid", H("k1b")))
+            if TAP:
+                total(p2, ("idf", bo), ("idn", H("ca")), ("idn", H("spb")))
+                act(ta, p2, AF.Copy)
+            else:
+                total(p2, ("idn", H("ca")), ("idn", H("spb")))
+                tt(ta, bo, p2, ALU.add)
             tt(H("dp"), w3, aP[h], ALU.subtract)
-            act(wx, w3, AF.Relu, bias=-15.5 * 16384, scale=16384.0)
+            act(H("cb") if TBP else wx, w3, AF.Relu, bias=-15.5 * 16384, scale=16384.0)
             if h in SAMEV:
                 ts(ns, H("dp"), C4096, ALU.add, C4096, ALU.is_equal)
             else:
@@ -876,18 +1020,30 @@ def record(T):
                 act(ns, H("dp"), AF.Relu, bias=-2047.5 * BIG, scale=BIG)
             dla, dlb = B("dl", 2 * lo, lo + hi), B("dl", lo + hi, 2 * hi)
             dqa, dqb = B("dq%d" % h, 0, hi - lo), B("dq%d" % h, hi - lo)
-            total(dqa, ("idb", H("da")), ("idn", H("ibp")))
-            if not JOINT:
-                act(dla, dqa, AF.Relu)
-            total(dqb, ("idn", H("iap")), ("idk", H("kpb")), ("idw", H("k1b")))
-            if JOINT:
-                act(B("dl", 2 * lo, 2 * hi), dq, AF.Relu)
+            if DA:
+                total(dqa, ("idb", H("da")), ("idn", H("ibp")))
             else:
-                act(dlb, dqb, AF.Relu)
-            tt(H("tb"), H("fy" if last else "aw"), wx, ALU.subtract)
-            tt(H("w1"), out("aP", h) if last else H("w1"), dla, ALU.add)
+                total(dqa, ("idk", H("kpa")), ("idx", H("k1a")), ("idn", H("ibp")))
+            if not JOINT:
+                act(dla, dqa, AF.Relu, bias=cut)
+            total(dqb, ("idn", H("iap")), ("idk", H("spb")), ("idx", H("k1b")))
+            if JOINT:
+                act(B("dl", 2 * lo, 2 * hi), dq, AF.Relu, bias=cut)
+            else:
+                act(dlb, dqb, AF.Relu, bias=cut)
+            if TBP:
+                total(H("tbp"), ("idf", H("fy" if last else "aw")), ("idn", H("cb")))
+                act(H("tb"), H("tbp"), AF.Relu)
+            else:
+                tt(H("tb"), H("fy" if last else "aw"), wx, ALU.subtract)
+            wa = H("w1")
+            if h in W1P and not last:
+                wa = H("a75" if h else "tbp")
+                total(wa, ("idb", H("kpa")), ("idn", H("spa")), ("idf", half(A, h)), ("idb", dla))
+            else:
+                tt(wa, out("aP", h) if last else wa, dla, ALU.add)
             tt(H("bt"), wo, dlb, ALU.add)
-            tt(H("X"), H("w1"), H("bt"), ALU.max)
+            tt(H("X"), wa, H("bt"), ALU.max)
             tt(xb, wo, H("tb"), ALU.max)
             tt(Y, H("X"), ns, ALU.mult if h in SAMEV else ALU.subtract)
             if h:
@@ -897,7 +1053,8 @@ def record(T):
             if h:
                 behind("a%d0" % t, AHEAD[3])
             if not last:
-                cp(B("pos", k0, k1), pos)
+                tt(B("erf", k0, k1), z, erf, ALU.max)
+                cp(B("pos", k0, k1), B("erf", k0, k1))
                 scatter(B(LB), B("pos", k0, k1), xb, Y)
                 if h:
                     behind("scatter", AHEAD[3])
@@ -908,7 +1065,7 @@ def record(T):
             ts(B("ta"), B("cnt"), 2 * C16, ALU.add, 2 * C16, ALU.subtract)
             tt(B("sc%d" % t), B("cnt"), B("ta"), ALU.subtract)
             send("c%d" % t)
-            act(B("ctp"), cls("Ct", t + 1), AF.Copy)
+            mm(B("ctp"), B("idb"), cls("Ctb", t + 1), True, True)
 
     expect("T%d" % NR)
     for c in range(4):
@@ -960,9 +1117,10 @@ def rank_program(g, core, T, topo):
                 for s2, v2 in snaps.get((s, need[s]), {}).items():
                     known[q][s2] = max(known[q].get(s2, 0), v2)
         if o["kind"] == "run":
-            cnt[q] += 1
+            for fn in [o["fn"]] + o.get("more", []):
+                cnt[q] += 1
+                fn(eng[q]).then_inc(T.sem["q" + q], 1)
             tok[i] = ("q" + q, cnt[q])
-            o["fn"](eng[q]).then_inc(T.sem["q" + q], 1)
         elif o["kind"] == "dma":
             tok[i] = (o["sem"], o["inc"])
             o["fn"](eng[q]).then_inc(T.sem[o["sem"]], 16)

@@ -28,7 +28,7 @@ US, JOINT = (0, 1), True
 PICKS = None
 JOG, TRIES = 0.5, 60
 WIDE = 2
-LISTS = ("lstP", "lstQ", "lstI", "lst8", "off", "eu", "e16", "pos", "pos2", "sel")
+LISTS = ("lstP", "lstQ", "lstI", "lstR", "lst8", "off", "eu", "e16", "pos", "pos2", "sel")
 CASES = ((1.0, 1.3, 3.8, 0.2, 0.25, 1.0, 0.4), (1.1, 1.6, 3.0, 0.15, 0.18, 0.85, 0.35), (1.35, 2.2, 6.0, 0.2, 0.25, 1.15, 0.25))
 TURNS = 10
 SWAPS, SLACK = 4000, 0.02
@@ -36,6 +36,20 @@ PASSES = 6
 
 DA, WIDE, PICKS, VFIRST, TRIES, SWAPS, TURNS = False, 0, (0, 2, 3, 1, 4, 5, 6, 7), 1, 10, 600, 45
 LS, SLACK, FV, W1P = True, 0.005, (1, 3, 5), ()
+KC, KB = ("ss", "ss"), (("m0", 128), ("m1", 128))
+STEP, NEAR, SWAPS, SLACK, TURNS = 50, 0.1, 350, 0.04, 6
+UF, OD = 2, (0, 1)
+FAST, FL, TC = (), ("", ""), True
+GI, JP, HF = True, 4, 0
+WXP, XP = (), ()
+SEED, HOPS, EVERY, COPIES = 11, (0, 0, 0, 1, 2), 4, ((1, 2), (2, 1), (3, 2), (2, 3), (0, 1))
+LONG, TC, GAP2 = 0.5, True, 1.7
+CASES = ((1.0, 1.15, 3.0, 0.2, 0.25, 1.05, 0.5, 1.2, 1.2), (1.1, 1.6, 3.0, 0.15, 0.18, 0.85, 0.35, 0.85, 1.0), (1.35, 2.2, 6.0, 0.2, 0.25, 1.15, 0.15, 1.15, 1.3))
+TCP = (1,)
+TW, F3, TF = 0.5, 0, True
+HOPS, STEP, SWAPS, SLACK = (0, 0, 1, 2, 4), 35, 250, 0.03
+PICKS, AHEAD, TURNS = (0, 1, 2, 4, 3, 5, 6, 7), (2.0, 2.0, 0.0, 1.8, 2.0), 44
+CS = (0, 1, 2, 3)
 SCRATCH, PART = {}, {}
 
 
@@ -53,22 +67,28 @@ def _ps(bank, **views):
         PART[n] = (bank, views[n][0], views[n][1], bank)
 
 
-_sb("int32", entx=1024, wti=1, kpi=1, ci=1024, pmi=16, pmj=16, n1=512, q=256, k1=256, za=256, l5a=256, ui=32, ub=32,
+_sb("int32", entx=1024, wti=1, kpi=1, ci=64, pmi=16, pmj=16, n1=256, q=256, k1=256, za=256, l5a=256, ui=32, ub=32,
     ei=256, em=256, ky=32, er=32, qb=256, zb=256, l5b=256, jd=16, kx=256)
-_sb("bfloat16", fx0=2064, fx2=2064, fx3=2064, one=128, blka=128, blk=128, idb=128, idn=128, idk=128, idw=128, idx=128, hid=128, cb=256, zer=32, zz=576, dlt=16,
-    rA=256, rK=16, sgm=512, fl=16, spa=256, kpa=256, k1a=256, iap=256, ca=256, da=256, spb=256, kpb=256, k1b=256, ibp=256, dl=512,
-    blw=128, blx=128, thr=192, lab=256, Yg=4096, Ys=4096, Xb=4096, ebx=256, erx=32, Ctb=1024, l5g=256, zag=256)
+_sb("bfloat16", fx0=2064, fx2=2064, fx3=2064, one=128, blka=128, blk=128, idb=128, idn=128, idk=128, idw=128, idx=128, hid=128, cb=256, zer=32, dlt=16,
+    rA=128, rK=16, sgm=512, fl=16, spa=256, kpa=256, k1a=256, iap=256, ca=256, da=256, spb=256, kpb=256, k1b=256, ibp=256, dl=512,
+    blw=128, blx=128, thr=128, lab=256, Yg=4096, Ys=4096, Xb=4096, ebx=256, erx=32, l5g=256, zag=256)
 SCRATCH["EQ"] = ("sbuf", [128, 16, 256], "bfloat16")
-SCRATCH["NM"] = SCRATCH["NM2"] = ("sbuf", [128, 16, 16, 16], "bfloat16")
+SCRATCH["KT"] = ("sbuf", [128, 32, 2, 8], "bfloat16")
+RUNS = sorted(set(_p[2][_i:_i + 2] for _p in PARTS for _i in (0, 2)))
+_sb("bfloat16", NM=4096, NM2=4096, b8n=8, prm=64, **{"prm" + _r: 64 for _r in RUNS})
+PATHS = sorted(set(_p[2] for _p in PARTS))
+_sb("bfloat16", x128=128, zw=144, **{"nil" + _r: 128 for _r in PATHS})
+_sb("bfloat16", idp=128, hi2=128, ix2=128, iw2=128)
+_sb("float32", msk=2, rsc=1, t128=1, d0=256, mid=8, ksq=128)
 _sb("float16", eh=256, idh=128)
-_sb("uint16", lstP=16, lstQ=16, lstI=16, lst8=8, off=256, eu=256, e16=16, ebc=256, pos=16, pos2=16, sel=16)
+_sb("uint16", lstP=16, lstQ=16, lstI=16, lstR=8, lst8=8, off=256, eu=256, e16=16, ebc=256, pos=16, pos2=16, sel=16)
 _sb("float32", old0=288, Ct=1024, la0=288, old1=288, iot=1024, la1=288, old2=288, TB0=1024, la2=288, old3=288, TB4=1024, la3=288, TB1=1320,
-    TB2=1320, TB3=1320, aw=256, sv=256, kv=256, cap=16, pw=16, x128=192, t128=192, LB0=1320, LB1=1320, yo=1320, D=4096, TC=1024, idf=128, allf=128, pmf=16,
-    x16=16, cmk=16, lI=16, mio=256, wk=2, pr=256, x1=256, oc=256, oT=1536, kyf=16, sU=80, lU=80, uk=80, uq=32,
-    sA=256, lA=256, ef=256, erf=32, wacc=3, ta=1, bF=256, dp=256, tb=256, bt=256, X=256, fa=256, fb=256, fy=256, ft=256,
-    d1=1024, d2=1024, ep=256, lpf=16, lpq=2, xq=8, lcx=1, YP=8 * 288)
+    TB2=1320, TB3=1320, aw=256, sv=256, cap=16, pw=16, LB0=1320, LB1=1320, yo=1320, D=4096, TC0=1024, TC1=1024, idf=128, allf=128, pmf=16,
+    x16=16, cmk=16, lI=16, wk=2, pr=256, x1=256, oc=256, oT=1536, kyf=16, sU=80, lU=80, uk=80, uq=32,
+    sA=256, lR=256, lA=256, ef=256, erf=32, wacc=3, ta=1, bF=256, dp=256, tb=256, bt=256, X=256, fa=256, fb=256, fy=256,
+    d1=1024, d2=1024, lpf=16, lpq=2, xq=8, lcx=1, YP=8 * 288)
 for _t in range(NR):
-    _sb("float32", **{"xb%d" % _t: 288, "lb%d" % _t: 288, "Y%d" % _t: 288, "sc%d" % _t: 1, "lc%d" % _t: 1})
+    _sb("float32", **{"xb%d" % _t: 288, "lb%d" % _t: 288, "Y%d" % _t: 288, "sc%d" % _t: 2, "lc%d" % _t: 2})
     PART["ta%d" % _t] = (PART["YP"][0], PART["YP"][1] + 576 * _t, 288, "ta%d" % _t)
     PART["aP%d" % _t] = (PART["YP"][0], PART["YP"][1] + 576 * _t + 288, 288, "aP%d" % _t)
     PART["win%d" % _t] = PART["old%d" % _t][:2] + (1600, "win")
@@ -76,7 +96,7 @@ GAP, FAR = ("Ct", "iot", "TB0", "TB4"), 1312.0
 _ps("pu", up=(0, 16), cnt=(32, 1), kmp=(128, 16), spare=(256, 256))
 _ps("pc", pcp=(0, 256), ctp=(256, 256))
 _ps("pa", a75=(0, 256), w1=(256, 256))
-_ps("tk", tbp=(0, 256), sp2=(256, 256))
+_ps("tk", tbp=(0, 256), sp2=(256, 256), tb0=(0, 128), tb1=(128, 128))
 for _h, (_k0, _k1, _) in enumerate(PARTS):
     _n, _h = 16 * (_k1 - _k0), str(_h)
     _ps("pk" + _h, **{"big" + _h: (0, 512), "key" + _h: (0, _n), "dq" + _h: (512 - 2 * _n, 2 * _n)})
@@ -87,8 +107,9 @@ for _h, (_k0, _k1, _) in enumerate(PARTS):
         _ps("tk", **{"ns" + _h: (0, _n), "wx" + _h: (256, _n)})
     for _v, _b in MOVE.items():
         PART[_v + _h] = {"tk": ("tk", 16 * _k0, _n, "tk"), "pk": ("pk" + _h, 128, _n, "pk" + _h), "pu": ("pu", 256 + 16 * _k0, _n, "pu")}[_b]
-for _i, _n in enumerate(("zS", "zM", "zP", "zw")):
-    PART[_n] = (PART["zz"][0], PART["zz"][1] + 144 * _i, 144, "zz")
+for _h in "01":
+    PART["kt" + _h] = (KB[int(_h)][0], KB[int(_h)][1], 128, KB[int(_h)][0])
+    PART["ep" + _h] = ("m" + _h, 256, 128, "m" + _h)
 
 
 def messages(n):
@@ -104,14 +125,14 @@ def messages(n):
             PART[name + m] = (PART[name][0], PART[name][1] + lo, hi - lo, name)
         out[m] = (tuple(s + m for s in src), dst + m, hi - lo, by, kind)
     for h, (k0, k1, path) in enumerate(PARTS):
-        piece("U%d" % h, "sU", "lU", 48 * h, 32 + 32 * h + k1 - k0, -x[0], "cb"[h])
-        piece("A%d" % h, "sA", "lA", 16 * k0, 16 * k1, -x[0], "ba"[h])
+        piece("U%d" % h, "sU", "lU", (16 + k0) * h, 16 + k1, -x[0], "cb"[h])
+        piece("A%d" % h, "sA", "lR", 16 * k0, 16 * k1, -x[0], "ba"[h])
     for t in range(NR):
         piece("T%d" % (t + 1), "TB%d" % t, "TB%d" % (t + 1), 0, 1024, hold[t] - hold[t + 1], "T")
         if t > 1:
             piece("f%d" % t, "fx0", "fx%d" % t, 0, 2064, -x[t], "f")
         if t + 1 < NR:
-            piece("c%d" % t, "sc%d" % t, "lc%d" % t, 0, 1, x[t] - x[t + 1], "c")
+            piece("c%d" % t, "sc%d" % t, "lc%d" % t, 0, 2, x[t] - x[t + 1], "c")
         for h, (k0, k1, path) in enumerate(PARTS):
             lo, hi = (16 * k0 + 16, 272 + k1 - k0) if h else (16 - k1, 16 * k1 + 16)
             piece("b%d%d" % (t, h), ("xb%d" % t, "Y%d" % t), "lb%d" % t, lo, hi, hold[t] - hold[t + 1], "b")
@@ -150,8 +171,12 @@ def ways(topo, T, src, dst, w, kind, alone):
         chains = [(c,) for c in free if topo.may_write(c, dst) and c not in mine] + [(c,) for c in near]
     else:
         far = [c for c in range(256) if topo.mates(c, dst) and topo.may_write(c, dst) and topo.die(c) == topo.die(src)]
-        chains = [(c, far[0]) for c in mine if c not in near] + [(c,) for c in near]
-    cut = [(w * j // len(chains) + 15) // 16 * 16 for j in range(len(chains))] + [w]
+        round_ = [c for c in mine if c not in near]
+        chains = [(c, far[0]) for c in round_] + [(c,) for c in near if c not in round_]
+        if kind == "F":
+            chains = [(round_[0], far[-1])]
+    part = [LONG if len(c) > 1 else 1.0 for c in chains]
+    cut = [(int(w * sum(part[:j]) / sum(part)) + 15) // 16 * 16 for j in range(len(chains))] + [w]
     return [(chains[j], cut[j], cut[j + 1]) for j in range(len(chains))]
 
 
@@ -244,7 +269,7 @@ def links(ops):
 
 def lasts(o, case):
     if o["kind"] != "run":
-        return o["dur"] * (case[5] if o["kind"] == "land" else 1.0)
+        return o["dur"] * (case[8] if o["kind"] == "send" else 1.0 if o["kind"] != "land" else case[7] if o["msg"][0] in "Tf" else case[5])
     if "each" in o:
         return o["dur"] + o["each"][0] * CY * (case[o["each"][1]] - (G, SC)[o["each"][1] - 1])
     return o["dur"] * case[0]
@@ -352,6 +377,350 @@ def polish(ops, pre, seq, wake, turn):
     return best
 
 
+def refine(ops, pre, seq):
+    n, nc = len(ops), len(CASES)
+    q = [o["q"] if o["kind"] != "land" else None for o in ops]
+    own = [[b + q[i] for b in ops[i]["banks"]] for i in range(n)]
+    other = [[b + r for b in ops[i]["banks"] for r in "vsp" if r != q[i]] for i in range(n)]
+    needs = [set(pre[i]) | set(j for j, lag in ops[i]["behind"] if ops[i]["kind"] != "run" or "firm" in ops[i]) for i in range(n)]
+    dur = [[lasts(o, case) for o in ops] for case in CASES]
+    hold = [[d[i] if ops[i]["kind"] in ("run", "send") else 0.05 for i in range(n)] for d in dur]
+    shut = [[x + case[3] for x in d] for d, case in zip(dur, CASES)]
+    dep = [[[(j, d[j] + (0.0 if ops[j]["kind"] == "send" else case[3] if q[i] != q[j] else case[4])) for j in pre[i]
+             if not (q[i] == "p" and q[j] == "p") and (ops[j]["kind"] != "send" or q[i] is None)] for i in range(n)] for d, case in zip(dur, CASES)]
+    suc = [[[] for _ in ops] for _ in CASES]
+    for c in range(nc):
+        for i in range(n):
+            for j, lag in dep[c][i]:
+                suc[c][j].append((i, lag))
+    head, tail, by = [[0.0] * n for _ in CASES], [[0.0] * n for _ in CASES], [[-1] * n for _ in CASES]
+    seed = [11]
+
+    def draw(k):
+        seed[0] = (seed[0] * 1103515245 + 12345) % 2147483648
+        return (seed[0] >> 8) % k
+
+    def forth(part, last, c, keep=None):
+        h, ho, sh, de, w = head[c], hold[c], shut[c], dep[c], by[c]
+        for i in part:
+            if keep is not None:
+                keep.append(dict(last))
+            t, who, k = 0.0, -1, q[i]
+            if k:
+                if k in last:
+                    who = last[k]
+                    t = h[who] + ho[who]
+                last[k] = i
+            for j, lag in de[i]:
+                if h[j] + lag > t:
+                    t, who = h[j] + lag, -1
+            for r in other[i]:
+                if r in last and h[last[r]] + sh[last[r]] > t:
+                    who = last[r]
+                    t = h[who] + sh[who]
+            for r in own[i]:
+                last[r] = i
+            h[i], w[i] = t, who
+
+    def back(part, nxt, c, keep=None):
+        h, g, ho, sh, su, du, top = head[c], tail[c], hold[c], shut[c], suc[c], dur[c], 0.0
+        for i in part[::-1]:
+            if keep is not None:
+                keep.append(dict(nxt))
+            t, k = du[i], q[i]
+            if k:
+                if k in nxt and ho[i] + g[nxt[k]] > t:
+                    t = ho[i] + g[nxt[k]]
+                nxt[k] = i
+            for j, lag in su[i]:
+                if lag + g[j] > t:
+                    t = lag + g[j]
+            for r in other[i]:
+                if r in nxt and sh[i] + g[nxt[r]] > t:
+                    t = sh[i] + g[nxt[r]]
+            for r in own[i]:
+                nxt[r] = i
+            g[i] = t
+            if h[i] + t > top:
+                top = h[i] + t
+        return top
+
+    def both(part, last, nxt):
+        before, after = [], []
+        for c in range(nc):
+            forth(part, dict(last), c, None if c else before)
+        return [back(part, dict(nxt), c, None if c else after) for c in range(nc)], before, after[::-1]
+
+    def worth(ends):
+        return sum(e * case[6] for e, case in zip(ends, CASES))
+
+    def turned(mid, up):
+        move = {mid[-1] if up else mid[0]}
+        for i in mid[::-1] if up else mid:
+            if up and i in move:
+                move |= needs[i]
+            elif not up and needs[i] & move:
+                move.add(i)
+        if mid[0 if up else -1] in move:
+            return None
+        a, b = [i for i in mid if i in move], [i for i in mid if i not in move]
+        return a + b if up else b + a
+
+    def stretch(seq, lo, hi, slack):
+        ends, before, after = both(seq, {}, {})
+        part, last, nxt = seq[lo:hi], before[lo], after[hi - 1]
+        ends, before, after = both(part, last, nxt)
+        best, left = (worth(ends), part), SWAPS
+        while left > 0:
+            place = {i: x for x, i in enumerate(part)}
+            pairs = [(by[c][i], i) for c in range(nc) for i in part
+                     if by[c][i] in place and head[c][i] + tail[c][i] > ends[c] - NEAR and by[c][i] not in needs[i]]
+            if not pairs:
+                break
+            for _ in range(60):
+                left -= 1
+                a, b = pairs[draw(len(pairs))]
+                pa, pb, up = place[a], place[b], draw(2)
+                for _ in range((0, 0, 0, 1, 2)[draw(5)]):
+                    if up and before[pa].get(q[a]) in place:
+                        pa = place[before[pa][q[a]]]
+                    if not up and after[pb].get(q[b]) in place:
+                        pb = place[after[pb][q[b]]]
+                mid = part[pa:pb + 1]
+                new = turned(mid, up)
+                if not new:
+                    continue
+                bar, old, guess = worth(ends) - slack * math.log((draw(1000) + 1) / 1001), [], []
+                for c in range(nc):
+                    old.append([(head[c][i], tail[c][i], by[c][i]) for i in mid])
+                    was = max(x[0] + x[1] for x in old[c])
+                    forth(new, dict(before[pa]), c)
+                    top = back(new, dict(after[pb]), c)
+                    guess.append(top if was > ends[c] - 1e-9 else max(top, ends[c]))
+                if worth(guess) < bar:
+                    whole, ahead, behind = part[:pa] + new + part[pb + 1:], [], []
+                    for c in range(nc):
+                        forth(whole[pa:], dict(before[pa]), c, None if c else ahead)
+                        back(whole[:pb + 1], dict(after[pb]), c, None if c else behind)
+                    got = [max([h[i] + g[i] for i in part]) for h, g in zip(head, tail)]
+                    if worth(got) < bar:
+                        part, ends, before, after = whole, got, before[:pa] + ahead, behind[::-1] + after[pb + 1:]
+                        break
+                    both(part, last, nxt)
+                else:
+                    for c in range(nc):
+                        for i, x in zip(mid, old[c]):
+                            head[c][i], tail[c][i], by[c][i] = x
+            if worth(ends) < best[0]:
+                best = (worth(ends), part)
+        return seq[:lo] + best[1] + seq[hi:]
+
+    for turn in range(TURNS):
+        both(seq, {}, {})
+        place = {i: x for x, i in enumerate(seq)}
+        seq = sorted(seq, key=lambda i: (head[0][i], place[i]))
+        for lo in range(-(turn * 37 % STEP), n, STEP):
+            seq = stretch(seq, max(lo, 0), min(lo + 2 * STEP, n), SLACK * (1 - turn / TURNS))
+    return worth(both(seq, {}, {})[0]), seq
+
+
+def better(ops, pre, seq):
+    n = len(ops)
+    w0, w1, w2 = [case[6] for case in CASES]
+    q = [o["q"] if o["kind"] != "land" else "land" for o in ops]
+    own = [[q[i]] + [b + q[i] for b in ops[i]["banks"]] for i in range(n)]
+    other = [[b + r for b in ops[i]["banks"] for r in "vsp" if r != q[i]] for i in range(n)]
+    needs = [set(pre[i]) | set(j for j, lag in ops[i]["behind"] if ops[i]["kind"] != "run" or "firm" in ops[i]) for i in range(n)]
+    dur = [tuple(lasts(o, case) for case in CASES) for o in ops]
+    hold = [dur[i] if ops[i]["kind"] in ("run", "send") else (ops[i].get("hold", 0.05),) * 3 if q[i] != "land" else (-99.0,) * 3 for i in range(n)]
+    shut = [tuple(x + case[3] for x, case in zip(d, CASES)) for d in dur]
+    dep, suc = [[] for _ in ops], [[] for _ in ops]
+    for i in range(n):
+        for j in pre[i]:
+            if not (q[i] == "p" and q[j] == "p") and (ops[j]["kind"] != "send" or q[i] == "land"):
+                lag = tuple(x + (0.0 if ops[j]["kind"] == "send" else case[3 if q[i] != q[j] else 4]) for x, case in zip(dur[j], CASES))
+                dep[i].append((j,) + lag)
+                suc[j].append((i,) + lag)
+        if "gap" in ops[i]:
+            j, lag = ops[i]["gap"], tuple(GAP2 * case[5] for case in CASES)
+            needs[i].add(j)
+            dep[i].append((j,) + lag)
+            suc[j].append((i,) + lag)
+    head, tail, seed = [None] * n, [None] * n, [SEED]
+
+    def draw(k):
+        seed[0] = (seed[0] * 1103515245 + 12345) % 2147483648
+        return (seed[0] >> 8) % k
+
+    def forth(part, last, keep=None):
+        for i in part:
+            if keep is not None:
+                keep.append(dict(last))
+            a = b = c = 0.0
+            if q[i] in last:
+                j = last[q[i]]
+                (a, b, c), (x, y, z) = head[j], hold[j]
+                a, b, c = a + x, b + y, c + z
+            for j, x, y, z in dep[i]:
+                u, v, w = head[j]
+                if u + x > a:
+                    a = u + x
+                if v + y > b:
+                    b = v + y
+                if w + z > c:
+                    c = w + z
+            for r in other[i]:
+                if r in last:
+                    (u, v, w), (x, y, z) = head[last[r]], shut[last[r]]
+                    if u + x > a:
+                        a = u + x
+                    if v + y > b:
+                        b = v + y
+                    if w + z > c:
+                        c = w + z
+            for r in own[i]:
+                last[r] = i
+            head[i] = (a, b, c)
+
+    def back(part, nxt, keep=None):
+        for i in part[::-1]:
+            if keep is not None:
+                keep.append(dict(nxt))
+            a, b, c = dur[i]
+            for j, x, y, z in suc[i] + [(nxt[r],) + shut[i] for r in other[i] if r in nxt] + ([(nxt[q[i]],) + hold[i]] if q[i] in nxt else []):
+                u, v, w = tail[j]
+                if u + x > a:
+                    a = u + x
+                if v + y > b:
+                    b = v + y
+                if w + z > c:
+                    c = w + z
+            for r in own[i]:
+                nxt[r] = i
+            tail[i] = (a, b, c)
+
+    def longest(part):
+        a = b = c = 0.0
+        for i in part:
+            (u, v, w), (x, y, z) = head[i], tail[i]
+            if u + x > a:
+                a = u + x
+            if v + y > b:
+                b = v + y
+            if w + z > c:
+                c = w + z
+        return a, b, c
+
+    def both(part, last, nxt):
+        before, after = [], []
+        forth(part, dict(last), before)
+        back(part, dict(nxt), after)
+        return longest(part), before, after[::-1]
+
+    def worth(ends):
+        return w0 * ends[0] + w1 * ends[1] + w2 * ends[2]
+
+    def turned(mid, up):
+        move = {mid[-1] if up else mid[0]}
+        for i in mid[::-1] if up else mid:
+            if up and i in move:
+                move |= needs[i]
+            elif not up and needs[i] & move:
+                move.add(i)
+        if mid[0 if up else -1] in move:
+            return None
+        a, b = [i for i in mid if i in move], [i for i in mid if i not in move]
+        return a + b if up else b + a
+
+    def stretch(seq, lo, hi, slack):
+        ends, before, after = both(seq, {}, {})
+        part, last, nxt = seq[lo:hi], before[lo], after[hi - 1]
+        ends, before, after = both(part, last, nxt)
+        best, left = (worth(ends), part), SWAPS
+        while left > 0:
+            place, pairs = {i: x for x, i in enumerate(part)}, []
+            for x, i in enumerate(part):
+                for c in range(3):
+                    if head[i][c] + tail[i][c] > ends[c] - NEAR:
+                        for r, lag in [(q[i], hold)] + [(r, shut) for r in other[i]]:
+                            j = before[x].get(r)
+                            if j in place and j not in needs[i] and head[j][c] + lag[j][c] > head[i][c] - 1e-9:
+                                pairs.append((j, i))
+            if not pairs:
+                break
+            for _ in range(60):
+                left -= 1
+                a, b = pairs[draw(len(pairs))]
+                pa, pb, up = place[a], place[b], draw(2)
+                for _ in range(HOPS[draw(len(HOPS))]):
+                    if up and before[pa].get(q[a]) in place:
+                        pa = place[before[pa][q[a]]]
+                    if not up and after[pb].get(q[b]) in place:
+                        pb = place[after[pb][q[b]]]
+                mid = part[pa:pb + 1]
+                new = turned(mid, up)
+                if not new:
+                    continue
+                bar, old, was = worth(ends) - slack * math.log((draw(1000) + 1) / 1001), [(head[i], tail[i]) for i in mid], longest(mid)
+                forth(new, dict(before[pa]))
+                back(new, dict(after[pb]))
+                if worth([t if s > e - 1e-9 else max(t, e) for s, t, e in zip(was, longest(mid), ends)]) < bar:
+                    whole, ahead, behind = part[:pa] + new + part[pb + 1:], [], []
+                    forth(whole[pa:], dict(before[pa]), ahead)
+                    back(whole[:pb + 1], dict(after[pb]), behind)
+                    got = longest(part)
+                    if worth(got) < bar:
+                        part, ends, before, after = whole, got, before[:pa] + ahead, behind[::-1] + after[pb + 1:]
+                        break
+                    both(part, last, nxt)
+                else:
+                    for i, x in zip(mid, old):
+                        head[i], tail[i] = x
+            if worth(ends) < best[0]:
+                best = (worth(ends), part)
+        return seq[:lo] + best[1] + seq[hi:]
+
+    def copied(seq, t, s):
+        both(seq, {}, {})
+        like = {ops[i]["role"]: i for i in seq if ops[i]["round"] == s}
+        pairs = [(i, like[ops[i]["role"]]) for i in seq if ops[i]["round"] == t and ops[i]["role"] in like]
+        off = sorted(head[i][0] - head[j][0] for i, j in pairs)[len(pairs) // 2]
+        key = {i: (head[i][0], x) for x, i in enumerate(seq)}
+        place = {i: x for x, i in enumerate(seq)}
+        for i, j in pairs:
+            key[i] = (head[j][0] + off, place[j])
+        out, done = [], set()
+
+        def take(i):
+            if i not in done:
+                done.add(i)
+                for j in sorted(needs[i], key=key.get):
+                    take(j)
+                out.append(i)
+        for i in sorted(seq, key=key.get):
+            take(i)
+        return out
+
+    def sweep(seq, slack, turn, lo=0, hi=n):
+        both(seq, {}, {})
+        place = {i: x for x, i in enumerate(seq)}
+        seq = sorted(seq, key=lambda i: (head[i][0], place[i]))
+        for at in range(lo - turn * 37 % STEP, hi, STEP):
+            seq = stretch(seq, max(at, 0), min(at + 2 * STEP, n), slack)
+        return seq
+
+    for turn in range(TURNS):
+        both(seq, {}, {})
+        seq = sweep(seq, SLACK * (1 - turn / TURNS), turn)
+        if turn % EVERY == EVERY - 1:
+            for t, s in COPIES:
+                at = [x for x, i in enumerate(seq) if ops[i]["round"] == t]
+                new = sweep(copied(seq, t, s), SLACK / 4, 0, at[0], at[-1])
+                if worth(both(new, {}, {})[0]) < worth(both(seq, {}, {})[0]):
+                    seq = new
+    return worth(both(seq, {}, {})[0]), seq
+
+
 def arrange(ops, pre, wake):
     n = len(ops)
     dur = [o["dur"] for o in ops]
@@ -427,14 +796,8 @@ def arrange(ops, pre, wake):
     soft = set((j, i) for i in range(n) for j, lag in ops[i]["behind"] if ops[i]["kind"] == "run" and j not in pre[i] and "firm" not in ops[i])
     fwd = [[e for e in fwd[j] if (j, e[0]) not in soft] for j in range(n)]
     bwd = [[e for e in bwd[i] if (e[0], i) not in soft] for i in range(n)]
-    start, best = best[1], None
-    for turn in range(TURNS):
-        got = polish(ops, pre, sorted(range(n), key=lambda i: (start[i], i)), wake, turn)
-        if best is None or got[0] < best[0]:
-            best = got
-        start = (got if got[0] < best[0] + 1.0 else best)[2]
-        late = place(bwd, fwd, lambda i: (-start[i] - dur[i], -i))
-        start = place(fwd, bwd, lambda i: (-late[i] - dur[i], i))
+    start = best[1]
+    best = better(ops, pre, sorted(range(n), key=lambda i: (start[i], i)))
     ORDER["end"] = best[0]
     seq, seen = best[1], {}
     for i in seq:
@@ -453,9 +816,10 @@ def record(T):
         if kind == "run" and q in "vs" and any(SCRATCH[x[0]][2] == "uint16" and x[4] in LISTS for x in r) and (w[0][4] not in LISTS or len(r) > 1):
             n = (dur - (0.05 if q == "v" else 0.065)) / CY
             d["each"] = (n / SC, 2) if r[-1][4] in ("pos", "pos2") else (n / G, 1)
-        key = (q,) + tuple((w or r or [(kind, 0, 0, 0, kind)])[0][1:3]) + ((w or r or [(kind, 0, 0, 0, kind)])[0][4].rstrip("0123"),)
+        x = (w or r or [(kind, 0, 0, 1, kind)])[0]
+        key = (q, (x[1] - PART[x[4]][1]) // 8 if x[4] in PART else x[1], x[4].rstrip("01234") if SCRATCH.get(x[0], "s")[0] != "psum" else x[4])
         seen[key] = seen.get(key, 0) + 1
-        d["role"] = key + (seen[key],)
+        d["role"], d["round"] = key + (seen[key],), where.get("round", -1)
         ops.append(d)
 
     def join(k):
@@ -535,7 +899,7 @@ def record(T):
     def mm(o, l, r, st, sp):
         if st:
             where[o[0]] = o
-        put("run", "p", lambda e: e.matmul(ap(o), ap(l), ap(r), st, sp), [l, r], [where[o[0]] if sp else o], (vd(width(r)) - FIX) * (4 if SCRATCH[l[0]][2] == "float32" else 1) + FIXP)
+        put("run", "p", lambda e: e.matmul(ap(o), ap(l), ap(r), st, sp), [l, r], [where[o[0]] if sp else o], max(min(64, width(l)), width(r)) * CY * (4 if SCRATCH[l[0]][2] == "float32" else 1) + FIXP)
 
     def iota(o, pat, base, cm):
         d = 0.13 + 2 * width(o) * CY
@@ -557,10 +921,14 @@ def record(T):
         ms = [m, also] if also else [m]
         for x in ms:
             where[x] = len(ops)
-        put("send", "g", None, [B(s, 0, MSG[x][2]) for x in ms for s in MSG[x][0]] + list(after), [], 3 * CALL if m[0] in "Tf" else CALL, msg=ms)
+        put("send", "g", None, [B(s, 0, MSG[x][2]) for x in ms for s in MSG[x][0]] + list(after), [], 3 * CALL if MSG[m][4] in "Tf" else CALL, msg=ms)
 
     def expect(m):
         put("land", None, None, [], [B(MSG[m][1], 0, MSG[m][2])], LAT[m[0]], [where[m]], msg=m)
+        if m[0] in "ab" and m[2] == "1":
+            ops[-1]["gap"] = where["land" + m[0]]
+            behind("land" + m[0])
+        mark("land" + m[0])
 
     def cls(name, c):
         return B(name, c, 1021 + c, 4)
@@ -590,26 +958,29 @@ def record(T):
     cp(B("fx0", 2056, 2057), B("wti"))
     cp(B("fx0", 2057, 2058), B("kpi"))
     ms(B("one"), 1.0)
-    ms(B("sU", 16, 64), 0.0)
-    iota(B("ci"), [[37, 1024]], 0, 0)
+    ms(B("mid"), -2047.5)
+    iota(B("ci"), [[37, 64]], 0, 0)
     iota(B("pmi"), [[0, 16]], 0, 1)
     iota(B("x16"), [[1, 16]], 0, 0)
     sift(B("blka"), B("one"), [[-16, 8], [0, 16]], ALU.is_ge, 0.0, 0, 1)
     sift(B("blk"), B("blka"), [[16, 8], [0, 16]], ALU.is_ge, 0.0, 15, -1)
     sift(B("idb"), B("one"), [[-1, 128]], ALU.is_equal, 0.0, 0, 1)
-    ms(B("zz"), 0.0)
+    ms(B("zw"), 0.0)
     ms(B("zer"), 0.0)
-    ms(B("allf"), -0.5)
+    ms(B("allf"), 16.0)
     ms(B("wacc", 2, 3), 16.0 + 31.0 / 128)
     ms(B("sgm"), 1.0)
     cp(B("sgm", 0, 497, 16), B("zer", 0, 32))
     ts(B("ci"), B("ci"), 63, ALU.bitwise_and)
-    ts(B("Ct"), B("ci"), 4096.0, ALU.mult, 262144.0 - 2048.0, ALU.add)
+    ts(B("Ct", 0, 64), B("ci"), 4096.0, ALU.mult, 262144.0 - 2048.0, ALU.add)
+    for n in (64, 128, 256, 512):
+        act(B("Ct", n, 2 * n), B("Ct", 0, n), AF.Copy)
     ts(B("pmj"), B("pmi"), 15, ALU.bitwise_and)
     cp(B("pmf"), B("pmj"))
     pm = B("pmf", 0, 1)
     ts(B("lI"), B("x16"), 16.0, ALU.mult, pm, ALU.add)
     cp(B("lstI"), B("lI"))
+    ts(B("lstR"), B("lI", 0, 8), -3.5, ALU.add, 0.125, ALU.mult)
     for h, (k0, k1, path) in enumerate(PARTS):
         nk = k1 - k0
         ts(B("jd", k0, k1), B("lI", 0, nk), (1 - nk) / 2, ALU.add, 1 / nk, ALU.mult)
@@ -634,41 +1005,69 @@ def record(T):
         for j in range(272, 272 + k1 - k0) if h else range(16 - k1, 16):
             act(B("YP", j, 8 * 288, 288), B("one", 0, 8), AF.Copy, scale=-4096.0)
             ops[-1]["w"] = [B(n + str(t), j, j + 1) for n in ("ta", "aP") for t in range(NR)]
-    for k0, k1, path in PARTS:
-        n = 16 // len(path)
-        for c in range(len(path)):
-            act(B("mio", n * c, n * c + n), B("x16", n * c, n * c + n), AF.Identity, bias=15360.0 + SHIFT[path[c]], scale=-1024.0)
-        for m in range(16):
-            act(B("rA", 16 * k0 + m % 8 * 2 + m // 8, 16 * k1, 16), B("one", 0, k1 - k0), AF.Copy, scale=B("mio", m, m + 1))
+    iota(B("rA"), [[0, 8], [-1024, 8], [-8192, 2]], 15360, 0)
     act(B("idf"), B("idb"), AF.Copy)
-    for n, s in (("idn", -1.0), ("idk", 1 / PEN), ("idw", 6.5), ("idx", 16.0), ("hid", 1.5 * (1 << 22))):
-        act(B(n), B("idb"), AF.Copy, scale=s)
-    for n, s in (("zS", -8192.0), ("zM", -16384.0), ("zP", 16384.0)):
-        act(B(n, 15, 128, 16), B("blk", 0, 113, 16), AF.Copy, scale=s)
+    used = "".join(FL)
+    for n, s, need in (("idn", -1.0, 1), ("idk", 1 / PEN, 1), ("idw", 6.0, FAST), ("idx", 16.0, len(FAST) < 2), ("hid", 1.5 * (1 << 22), 1), ("idp", PEN, "s" in used),
+                       ("hi2", 3.0 * (1 << 22), "k" in used or "p" in used), ("ix2", 32.0, "k" in used), ("iw2", 12.0, "k" in used)):
+        if need:
+            act(B(n), B("idb"), AF.Copy, scale=s)
+    act(B("b8n"), B("blk", 0, 113, 16), AF.Copy, scale=-1.0)
+    sift(B("prm"), B("one", 0, 64), [[-2, 8], [-16, 8]], ALU.is_ge, 0.0, 0, 1)
+    sift(B("prm"), B("prm"), [[2, 8], [16, 8]], ALU.is_ge, 0.0, 1, -1)
+    ts(B("jd", 0, 1), B("pmi", 0, 1), 1, ALU.bitwise_and)
+    cp(B("msk", 1, 2), B("jd", 0, 1))
+    ts(B("msk", 0, 1), B("jd", 0, 1), -1.0, ALU.mult, 1.0, ALU.add)
+    for r in RUNS:
+        a, b = [8192.0 if x == "S" else 16384.0 for x in r]
+        if a != b:
+            ts(B("rsc"), B("pmi", 0, 1), 63.5, ALU.is_gt, b - a, ALU.mult)
+            ts(B("rsc"), B("rsc"), a, ALU.add)
+        act(B("prm" + r), B("prm"), AF.Copy, scale=a if a == b else B("rsc"))
+    for path in PATHS:
+        for r in range(2):
+            a, b = [0.0 if x == "V" else 16.0 for x in path[2 * r:2 * r + 2]]
+            if a == b:
+                ms(B("nil" + path, 64 * r, 64 * r + 64), a)
+            else:
+                ts(B("rsc"), B("pmi", 0, 1), 63.5, ALU.is_gt, b - a, ALU.mult)
+                ts(B("nil" + path, 64 * r, 64 * r + 64), B("one", 0, 64), B("rsc"), ALU.mult, a, ALU.add)
+    for k0, k1, path in PARTS:
+        for c in range(4):
+            if path[c] != "V" and path[c ^ 1] == "V":
+                ms(B("NM2", 256 * k0 + 512 * c, 256 * k0 + 512 * c + 512), 0.0)
     cp(B("idh"), B("idb"))
     ts(B("cmk"), B("x16"), pm, ALU.is_gt, 1.0, ALU.add)
     scan(B("pw"), B("cmk"), B("zer", 0, 16), 2048.0)
     act(B("blw"), B("blk"), AF.Copy, scale=B("pw", 15, 16))
     act(B("blx"), B("blk"), AF.Copy, scale=8 * BIG)
-    iota(B("x128"), [[0, 12], [1, 16]], 0, 0)
-    ts(B("x128"), B("x128"), pm, ALU.is_equal)
-    ts(B("t128"), B("x128"), B("pw", 15, 16), ALU.mult, -2.0, ALU.mult)
-    ts(B("x128"), B("x128"), -1.0, ALU.add, BIG * 8192, ALU.mult)
-    tt(B("thr"), B("x128"), B("t128"), ALU.add)
+    sift(B("x128"), B("one"), [[0, 8], [-1, 16]], ALU.is_equal, 0.0, 0, 1)
+    mm(B("pcp", 0, 128), B("x128"), B("x128"), True, True)
+    ts(B("t128"), B("pw", 15, 16), -2.0, ALU.mult, BIG * 4096, ALU.add)
+    act(B("thr"), B("pcp", 0, 128), AF.Identity, scale=B("t128"), bias=-BIG * 4096)
 
     def convert(o, x, w, at=0):
         n1, w = B("n1", at, at + width(x)), B(w, 0, width(x))
         ts(n1, x, 2.0 ** -11, ALU.mult, 0.5 - 2.0 ** -12, ALU.add)
         ts(w, n1, 2048.0, ALU.mult, 15.0, ALU.add)
         tt(o, w, x, ALU.add)
+
+    def convert2(o, x, w, at):
+        r, w = B("d1" if SCRATCH[x[0]][2] == "int32" else "d2", at, at + width(x)), B(w, 0, width(x))
+        ts(r, x, 1023.5, ALU.add, C4096 / 2, ALU.add)
+        act(r, r, AF.Identity, bias=-C4096 / 2)
+        act(w, r, AF.Identity, bias=15.0)
+        tt(o, w, x, ALU.add)
     for h in range(2):
+        gcp(half(B("sA"), h), half(cls("entx", 0), h))
         ts(half(B("q"), h), half(cls("entx", 0), h), 15.0, ALU.add)
-        convert(half(B("sA"), h), half(cls("entx", 0), h), "u%d" % h, 16 * PARTS[h][0])
+        ts(half(B("n1"), h), half(cls("entx", 0), h), 2.0 ** -11, ALU.mult, 0.5 - 2.0 ** -12, ALU.add)
         ts(half(B("k1"), h), half(B("q"), h), 16, ALU.bitwise_and)
         tt(half(B("pr"), h), half(B("n1"), h), half(B("k1"), h), ALU.mult)
         send("A%d" % h)
     iota(B("iot"), [[1, 1024]], 0, 0)
     behind("A1")
+    ops[-1]["firm"] = True
 
     def decode(o, a, w, k):
         d1, d2 = B("d1", k, k + width(a)), B("d2", k, k + width(a))
@@ -693,11 +1092,11 @@ def record(T):
         scatter(B(name), B("pos2"), B(lb, 16, 272))
         mark("whole")
 
-    act(B("Ctb"), B("Ct"), AF.Copy)
-    mm(B("ctp"), B("idb"), cls("Ctb", 0), True, True)
+    mm(B("ctp"), B("idf"), cls("Ct", 0), True, True)
     for t in range(NR):
         last = t == NR - 1
         seen.clear()
+        where["round"] = t
         LB = "LB%d" % ((t + 1) % 2)
         A, fx, TB, U = cls("LB%d" % (t % 2), t) if t else B("sA"), "fx%d" % (t if t > 1 else 0), "TB%d" % t, "uk" if t else "sU"
         tau, clock = 5.0 + t, 12.0 + t
@@ -710,7 +1109,7 @@ def record(T):
             act(B("zw", 15, 128, 16), B("blk", 0, 113, 16), AF.Copy, scale=B("wk", 0, 1))
             act(B("rK"), B("dlt"), AF.Copy, scale=B("wk", 1, 2))
             mm(B("kmp"), B("blk"), B("rK"), True, True)
-        act(B(U, 0, 16), B("kmp"), AF.Copy)
+        act(B(U, 0, 16), B("kmp"), AF.Identity, scale=16.0, bias=2047.5)
         if t:
             expect("c%d" % (t - 1))
         for h, (k0, k1, path) in enumerate(PARTS):
@@ -721,6 +1120,7 @@ def record(T):
                 ts(B("k1", lo, hi), B("q", lo, hi), 16, ALU.bitwise_and)
                 tt(B("pr", lo, hi), B("a75", lo, hi), B("k1", lo, hi), ALU.mult)
             ts(B("off", lo, hi), B("pr", lo, hi), 2.0 ** (-16 if t else -4), ALU.mult, 127.0 / 256 if t else 0.0, ALU.add, by=B("lstP", k0, k1))
+            mm(B("w3%d" % h, 0, nk), B("idf"), B("mid"), True, False)
             for c in range(k0 // 2, k1 // 2):
                 o, l = B("Yg", 512 * c, 512 * c + 512), B("off", 32 * c, 32 * c + 32)
                 if c in (FV if t else FV0):
@@ -731,6 +1131,9 @@ def record(T):
                 if h and HF and ops[-1]["q"] == "v":
                     behind("scan")
                     ops[-1]["firm"] = True
+                if h and not t and UF > 1 and ops[-1]["q"] == "v":
+                    behind("ub")
+                    ops[-1]["firm"] = True
                 scan(B("Ys", 512 * c, 512 * c + 512), B("sgm"), o)
                 if h and HF > 1:
                     behind("scan")
@@ -738,29 +1141,20 @@ def record(T):
                 if not h:
                     mark("scan")
                 for p in range(32 * (c - k0 // 2) // nk, 32 * (c + 1 - k0 // 2) // nk):
-                    mm(B("w3%d" % h, 0, nk), slide("zw", p), B("Ys", 16 * (lo + nk * p) + 15, 16 * (lo + nk * p + nk), 16), p == 0, p == 15)
+                    mm(B("w3%d" % h, 0, nk), slide("zw", p), B("Ys", 16 * (lo + nk * p) + 15, 16 * (lo + nk * p + nk), 16), False, p == 15)
                 join(32 * (c + 1 - k0 // 2) // nk - 32 * (c - k0 // 2) // nk)
-            ui, ub, uq, few = B("ui", 16 * h, 16 * h + nk), B("ub", 16 * h, 16 * h + nk), B("uq", 16 * h, 16 * h + nk), B("lst8", 2 * h, 2 * h + 1)
-            cp(ui, B("w3%d" % h, 0, nk))
+            ts(B("uq", k0, k1), B("w3%d" % h, 0, nk), C4096, ALU.add, C4096, ALU.subtract)
             if h:
                 behind("sum", AHEAD[4])
             mark("sum")
-            ts(ub, ui, 4095, ALU.bitwise_and)
-            at = 16 + 32 * h
-            more = (15.5 if t else 0.0) - 13.0 / 32
-            if h in US:
-                act(B(U, at, at + 16), ub, AF.Copy, by=few)
-                act(B("uq", 16 * h, 16 * h + 16), ub, AF.Square, by=few)
-                act(B(U, at + 16, at + 16 + nk), uq, AF.Identity, scale=2.0 ** -5, bias=more)
-            else:
-                tt(uq, ub, ub, ALU.mult)
-                cp(B(U, at, at + nk), ub)
-                ts(B(U, at + 16, at + 16 + nk), uq, 2.0 ** -5, ALU.mult, more, ALU.add)
+            tt(B(U, 16 + k0, 16 + k1), B("w3%d" % h, 0, nk), B("uq", k0, k1), ALU.subtract)
+            mark("ub")
             if not t:
                 send("U%d" % h)
         if not t:
             for h in range(2):
                 expect("A%d" % h)
+                convert2(half(B("lA"), h), half(B("lR"), h), "tb%d" % h, 128 * h)
             A, U = B("lA"), "lU"
             for h in range(2):
                 tt(half(B("q"), h), half(B("ctp"), h), half(A, h), ALU.add)
@@ -769,7 +1163,7 @@ def record(T):
             act(half(B("x1"), h), half(B("a75"), h), AF.Identity, bias=C16)
             act(half(B("oc"), h), half(B("x1"), h), AF.Identity, bias=-C16)
             n, reps = 16 * (k1 - k0), 16 // len(path)
-            first = 1 if t else reps
+            first = 1 if t or h in OD else reps
             for j in range(first):
                 act(B("oT", 768 * h + n * j, 768 * h + n * j + n), B("oc", 16 * k0, 16 * k1), AF.Identity, bias=7.5)
             n, reps = n * first, reps // first
@@ -777,6 +1171,7 @@ def record(T):
                 o, a = B("oT", 768 * h + n * j, 768 * h + n * j + n), B("oT", 768 * h, 768 * h + n)
                 put("dma", "y", lambda e, o=o, a=a: e.dma_start(ap(o), ap(a)), [a], [o], 2.2, sem="oc%d" % (2 * t + h), inc=16 * (reps - 1))
                 mark("own")
+                mark("own%d" % h)
 
         def total(o, *terms):
             for j, (l, r) in enumerate(terms):
@@ -799,17 +1194,14 @@ def record(T):
                 l5a, za, each = H("l5g"), H("zag"), None
                 gcp(za, H("za"))
                 gcp(l5a, H("l5a"))
-            act(H("spa"), l5a, AF.Relu, bias=(tau + 0.5) * PEN, scale=-PEN, by=each)
-            act(H("kpa"), za, AF.Relu, bias=(tau + 0.5) * PEN, scale=-PEN, by=each)
+            act(H("spa"), l5a, AF.Relu, bias=(tau + 1) * PEN, scale=-PEN, by=each)
+            act(H("kpa"), za, AF.Relu, bias=(tau + 1) * PEN, scale=-PEN, by=each)
             act(H("k1a"), H("kpa"), AF.Sign)
             total(H("w1"), ("idb", H("kpa")), ("idn", H("spa")), ("idf", mine))
             total(H("sp2"), ("idf", mine), ("idn", H("spa")))
             act(H("aw"), H("sp2"), AF.Relu)
             if last:
                 decode(H("fy"), H("aw"), H("sp2"), 256 + lo)
-            if DA:
-                total(H("tbp"), ("idk", H("kpa")), ("idw", H("k1a")))
-                act(H("da"), H("tbp"), AF.Identity, bias=-cut)
             for h in range(2):
                 if k0 <= PARTS[h][0] < k1:
                     act(aP[h], half(B("w1"), h), AF.Relu)
@@ -819,26 +1211,41 @@ def record(T):
             if not k0:
                 mark("lanes")
             act(H("iap"), l5a, AF.Relu, bias=31 * BIG, scale=-2 * BIG, by=each)
+        if not last:
+            mm(B("ctp"), B("idf"), cls("Ct", t + 1), True, True)
         if t:
             expect("T%d" % t)
             complete(t, TB)
         else:
-            for j in range(2):
-                convert(B(TB, 512 * j, 512 * j + 512), B("entx", 512 * j, 512 * j + 512), "big%d" % j)
+            for c in range(4):
+                (convert2 if c in CS else convert)(B(TB, 256 * c, 256 * c + 256), B("entx", 256 * c, 256 * c + 256), ("big0", "big1", "spare", "pcp")[c], 256 * c)
             for h in range(2):
                 expect("U%d" % h)
-        send("T%d" % (t + 1), [] if t else [B("lU")])
-        if t:
-            behind("own", 1.5)
+        send("T%d" % (t + 1), [B("oT", 0, 512), B("oT", 768, 1280)] + ([] if t else [B("lU", 0, 32)]))
+        if TC:
+            tc, tn = B("TC%d" % (t % 2)), B("TC%d" % (1 - t % 2))
+            if not t:
+                put("dma", "y", lambda e, o=tc: e.dma_start(ap(o), ap(B("Ct"))), [B("Ct")], [tc], 3.0, sem="tc0", inc=16)
+                behind("own0")
+            put("dma", "g", lambda e, o=tc, a=B(TB, 0, 1024): e.dma_start(ap(o), ap(a), accum_op=ALU.add), [B(TB, 0, 1024), tc], [tc], 6.5,
+                sem="td%d" % t, inc=16, hold=1.2)
+            if TF:
+                behind("T%d" % (t + 1))
+            else:
+                ops[where["T%d" % (t + 1)]]["behind"].append((len(ops) - 1, 0.0))
+            mark("T%d+" % (t + 1))
+            if not last:
+                put("dma", "y", lambda e, o=tn: e.dma_start(ap(o), ap(B("Ct"))), [B("Ct"), tc], [tn], 3.0, sem="tc%d" % (t + 1), inc=16)
         if t + 2 < NR:
             send("f%d" % (t + 2))
+            behind("T%d%s" % (t + 1, "+" * TC))
             behind("T%d" % (t + 1))
         if not last:
             gcp(cls(LB, t + 1), cls(TB, t + 1))
+        act(B("ksq"), B(U, 0, 16), AF.Square, bias=-2047.5, by=B("lstR"))
+        if t:
+            ts(B("ksq"), B("ksq"), B("lc%d" % (t - 1), 0, 1), ALU.add, B("lc%d" % (t - 1), 1, 2), ALU.subtract)
         RT = B(TB, 0, 1024)
-        if TC:
-            put("dma", "y", lambda e: e.dma_start(ap(B("TC")), ap(B("Ct"))), [B("Ct")], [B("TC")], 3.0, sem="tc%d" % t, inc=16)
-            put("dma", "g", lambda e, a=RT: e.dma_start(ap(B("TC")), ap(a), accum_op=ALU.add), [RT, B("TC")], [B("TC")], 6.0, sem="td%d" % t, inc=16)
 
         for h, (k0, k1, path) in enumerate(PARTS):
             lo, hi, nk = 16 * k0, 16 * k1, k1 - k0
@@ -850,16 +1257,15 @@ def record(T):
             def ch(n, c, more=1):
                 return B(n, 16 * (lo + cw * c), 16 * (lo + cw * (c + more)))
             for k in range(k0, k1):
-                at = 16 + 32 * h + k - k0
-                act(B("ep", lo + k - k0, hi, nk), B(U, 0, 16), AF.Identity, bias=B(U, at + 16, at + 17), scale=B(U, at, at + 1))
+                act(B("ep%d" % h, k - k0, hi - lo, nk), B(U, 0, 16), AF.Square, bias=B(U, 16 + k, 17 + k))
                 if (k - k0) % JE == JE - 1:
                     join(JE)
             if t and not h:
                 for c in HB:
                     ops[where["look%d" % c]]["behind"].append((len(ops) - 1, 0.0))
                     ops[where["look%d" % c]]["firm"] = True
-            ts(H("ei"), H("ep"), B("lc%d" % (t - 1)) if t else 0.0, ALU.add)
-            ts(H("em"), H("ei"), 1023, ALU.bitwise_and)
+            tt(H("ei"), B("ep%d" % h), B("ksq"), ALU.subtract)
+            ts(H("em"), H("ei"), 5, ALU.logical_shift_right, 1023, ALU.bitwise_and)
             cp(H("eu"), H("em"))
             if t and not h and HS:
                 ops[where["whole"]]["behind"].append((len(ops) - HS, 0.0))
@@ -890,55 +1296,42 @@ def record(T):
                     act(ch("D" if path[c] == "S" else "Xb", c0, n), ch("D", c0, n), AF.Abs)
                     if h or c0:
                         behind("sign")
-                ms_ = range(mc * c0, mc * (c0 + n))
-
-                def one(name, m):
-                    return B(name, 16 * lo + 16 * nk * m, 16 * lo + 16 * nk * (m + 1))
-
-                def turned(name, m):
-                    return (name, 0, 1, 1, "%s.%d.%d." % (name, h, m), ((k0, k1), m, (0, 16)))
                 if path[c] == "S":
                     act(ch("D", c0, n), ch("D", c0, n), AF.Abs, bias=-1032.25)
-                    for m in ms_:
-                        act(turned("NM", m), one("D", m), AF.Sign, bias=-1024.0)
-                        if m % JT == JT - 1:
-                            join(JT)
+                    act(ch("NM", c0, n), ch("D", c0, n), AF.Sign, bias=-1024.0)
                     mark("sign")
                 elif path[c] == "M":
                     mark("sign")
                     ts(ch("Xb", c0, n), ch("Xb", c0, n), 3000.0, ALU.min, 262144.0 + 1016.0, ALU.add)
-                    for m in ms_:
-                        act(turned("NM", m), one("Xb", m), AF.Square, bias=-129.0, scale=2.0 ** -11)
+                    act(ch("NM", c0, n), ch("Xb", c0, n), AF.Square, bias=-129.0, scale=2.0 ** -11)
                 else:
                     for name, cc in (("NM", C16), ("NM2", C4096)):
-                        for m in ms_:
-                            ts(turned(name, m), one("Xb", m), cc, ALU.add, cc, ALU.is_equal)
-                            if m % JT == JT - 1:
-                                join(JT)
+                        ts(ch(name, c0, n), ch("Xb", c0, n), cc, ALU.add, cc, ALU.is_equal)
                     if VFIRST > 1:
                         mark("pick")
-            key = "key%d" % h
-            mm(B(key, 0, 16 * nk), B("idb"), H("rA"), True, False)
+            key, kt, todo = "key%d" % h, "kt%d" % h, []
+            mm(B(key, 0, 16 * nk), B("idb"), B("rA"), True, False)
             mm(B(key, 0, 16 * nk), B("idh" if h in EH else "idf"), H("eh" if h in EH else "ef"), False, False)
-            runs = []
-            for c in range(len(path)):
-                if runs and path[runs[-1][0]] == path[c] and runs[-1][1] < 2:
-                    runs[-1][1] += 1
-                else:
-                    runs.append([c, 1])
-            todo = []
-            for c, n in sorted(runs, key=lambda r: VFIRST and path[r[0]] != "V"):
-                m0, m1 = mc * c, mc * (c + n)
-                for z, src in {"S": [("zS", "NM")], "M": [("zM", "NM")], "V": [("zM", "NM"), ("zP", "NM2")]}[path[c]]:
-                    for p in range(16):
-                        todo.append((B(key, m0 // 8, 16 * nk, 2), slide(z, p), (src, 0, 1, 1, src, ((k0, k1), (m0, m1), p)),
-                                     [turned(src, m) for m in range(m0, m1)]))
-            todo = [x for j in SUMS[h] for x in todo[16 * j:16 * j + 16]]
-            for i, (o, l, r, reads) in enumerate(todo):
+            mm(B(kt), B("idb"), B("nil" + path), True, False)
+            for r in sorted(range(2), key=lambda r: VFIRST and path[2 * r] != "V"):
+                at = 16 * lo + 1024 * r
+                for src, z in [("NM", B("b8n"))] + [("NM2", B("blk", 0, 113, 16))] * ("V" in path[2 * r:2 * r + 2]):
+                    todo.append([(B(kt, 64 * r + p, 64 * r + 64, 8), B(src, at + p, at + 1024, 8), z) for p in range(8)])
+            todo = [x for j in SUMS[h] if j < len(todo) for x in todo[j]]
+            for i, (o, l, r) in enumerate(todo):
                 mm(o, l, r, False, i == len(todo) - 1)
-                ops[-1]["r"] += reads
                 if i % JP == JP - 1:
                     join(JP)
+            for pp in range(2):
+                o = ("KT", 0, 1, 1, "KT.%d.%d." % (h, pp), ((16 * h, 16 * h + 16), pp, (0, 8)))
+                if KC[h][pp] == "s":
+                    act(o, B(kt), AF.Copy, scale=B("msk", pp, pp + 1))
+                else:
+                    ts(o, B(kt), B("msk", pp, pp + 1), ALU.mult)
+            for r in range(2):
+                a = 16 * h + 8 * r
+                mm(B(key, r, 16 * nk, 2), ("KT", 0, 1, 1, "KT.%d.0." % h, ((a, a + 8), (0, 2), (0, 8))), B("prm" + path[2 * r:2 * r + 2]), False, r == 1)
+                ops[-1]["r"].append(("KT", 0, 1, 1, "KT.%d.1." % h))
             ky, er = [B(n, 16 * h, 16 * h + nk) for n in ("ky", "er")]
             scan(H("kx" if KI else "kv"), B("sgm", 0, hi - lo), B(key, 0, 16 * nk))
             behind("keys" if h else "lanes", AHEAD[0 if h else 2])
@@ -980,72 +1373,95 @@ def record(T):
             tt(z, sv, B("cap", k0, k1), ALU.min)
             w3, p2, ns, wx, dq = [B(n + str(h)) for n in ("w3", "p2", "ns", "wx", "dq")]
             act(H("bF"), RT, AF.Copy, by=e)
-            if TC:
-                pick(H("qb"), B("TC"), e)
+            if TC and h in TCP:
+                pick(H("qb"), tc, e)
             else:
                 pick(H("qb"), B("Ct"), e, H("bF"), ALU.add)
             ts(H("zb"), H("qb"), 0x3801F, ALU.bitwise_and)
             ts(H("l5b"), H("qb"), 31, ALU.bitwise_and)
             each = B("lstI", 0, nk)
-            act(H("k1b"), H("zb"), AF.Sign, bias=tau + 0.5, scale=-1.0, by=each)
-            act(H("kpb"), H("l5b"), AF.Sign, bias=-tau - 0.5, by=each)
-            act(H("spb"), H("l5b"), AF.Relu, bias=(tau + 0.5) * PEN, scale=-PEN, by=each)
+            hk, hp, xk, wk, ns_, ks_ = "hid", "hid", "idx", "idw", "idn", "idk"
+            if "k" in FL[h]:
+                ts(H("k1b"), H("zb"), tau + 0.5, ALU.is_lt, 0.5, ALU.subtract)
+                hk, xk, wk = "hi2", "ix2", "iw2"
+            else:
+                act(H("k1b"), H("zb"), AF.Sign, bias=tau + 0.5, scale=-1.0, by=each)
+            if "p" in FL[h]:
+                ts(H("kpb"), H("l5b"), tau + 0.5, ALU.is_gt, 0.5, ALU.subtract)
+                hp = "hi2"
+            else:
+                act(H("kpb"), H("l5b"), AF.Sign, bias=-tau - 0.5, by=each)
+            if "s" in FL[h]:
+                ts(H("spb"), H("l5b"), tau + 1, ALU.subtract, 0.0, ALU.min)
+                ns_, ks_ = "idp", "idn"
+            else:
+                act(H("spb"), H("l5b"), AF.Relu, bias=(tau + 1) * PEN, scale=-PEN, by=each)
             if "i" in FL[h]:
                 ts(H("ibp"), H("l5b"), 15.5, ALU.is_lt, PEN, ALU.mult)
             else:
                 act(H("ibp"), H("l5b"), AF.Relu, bias=31 * BIG, scale=-2 * BIG, by=each)
-            if W3P:
-                total(w3, ("idf", H("bF")), ("hid", H("kpb")), ("hid", H("k1b")))
-            else:
-                total(w3, ("hid", H("kpb")), ("hid", H("k1b")))
-                tt(w3, H("bF"), w3, ALU.add)
-            xb, Y, ta = [out(n, h) for n in ("xb", "Y", "ta")]
-            bo, wo = H("bF"), w3
-            if last:
-                bo, wo = H("fb"), H("sp2")
-                decode(bo, H("bF"), wo, 512 + lo)
-                total(wo, ("idf", bo), ("hid", H("kpb")), ("hid", H("k1b")))
-            if TAP:
-                total(p2, ("idf", bo), ("idn", H("ca")), ("idn", H("spb")))
-                act(ta, p2, AF.Copy)
-            else:
-                total(p2, ("idn", H("ca")), ("idn", H("spb")))
-                tt(ta, bo, p2, ALU.add)
-            tt(H("dp"), w3, aP[h], ALU.subtract)
-            act(H("cb") if TBP else wx, w3, AF.Relu, bias=-15.5 * 16384, scale=16384.0)
-            if h in SAMEV:
+            if h in FAST:
+                xb, Y, ta = [out(n, h) for n in ("xb", "Y", "ta")]
+                sa, sb, wx, bo = B("dq%d" % h, 0, hi - lo), H("sp2"), H("a75"), H("bF")
+                tt(H("d0"), bo, H("w1"), ALU.subtract)
+                act(H("cb"), bo, AF.Sign, bias=-15.5)
+                if last:
+                    bo = H("fb")
+                    decode(bo, H("bF"), sb, 512 + lo)
+                total(w3, (hp, H("kpb")), (hk, H("k1b")))
+                total(sa, ("idk", H("kpa")), ("idw", H("k1a")), ("idf", out("aP", h)), ("idn", H("ibp")))
+                total(sb, ("idn", H("iap")), ("idf", bo), (wk, H("k1b")), (ks_, H("spb")))
+                total(wx, ("hid", H("cb")), (hp, H("kpb")), (hk, H("k1b")))
+                total(p2, ("idn", H("ca")), (ns_, H("spb")))
+                tt(H("dp"), H("d0"), w3, ALU.add)
                 ts(ns, H("dp"), C4096, ALU.add, C4096, ALU.is_equal)
+                tt(H("bt"), bo, w3, ALU.add)
+                act(wx, wx, AF.Relu, scale=2.0)
+                tt(wx, H("fy" if last else "aw"), wx, ALU.subtract)
+                tt(xb, H("bt"), wx, ALU.max)
+                tt(ta, bo, p2, ALU.add)
+                tt(H("X"), out("aP", h), sa, ALU.max)
+                tt(sb, H("bt"), sb, ALU.max)
+                tt(H("X"), H("X"), sb, ALU.max)
+                tt(Y, H("X"), ns, ALU.mult)
             else:
-                act(H("dp"), H("dp"), AF.Abs)
-                act(ns, H("dp"), AF.Relu, bias=-2047.5 * BIG, scale=BIG)
-            dla, dlb = B("dl", 2 * lo, lo + hi), B("dl", lo + hi, 2 * hi)
-            dqa, dqb = B("dq%d" % h, 0, hi - lo), B("dq%d" % h, hi - lo)
-            if DA:
-                total(dqa, ("idb", H("da")), ("idn", H("ibp")))
-            else:
+                total(w3, (hp, H("kpb")), (hk, H("k1b")))
+                xb, Y, ta = [out(n, h) for n in ("xb", "Y", "ta")]
+                bo, wo = H("bF"), w3
+                if last:
+                    bo, wo = H("fb"), H("sp2")
+                    decode(bo, H("bF"), wo, 512 + lo)
+                    tt(wo, bo, w3, ALU.add)
+                tt(w3, H("bF"), w3, ALU.add)
+                total(p2, ("idn", H("ca")), (ns_, H("spb")))
+                tt(ta, bo, p2, ALU.add)
+                tt(H("dp"), w3, aP[h], ALU.subtract)
+                if h in WXP:
+                    act(H("cb"), H("bF"), AF.Sign, bias=-15.5)
+                    total(wx, ("hid", H("cb")), (hp, H("kpb")), (hk, H("k1b")))
+                    act(wx, wx, AF.Relu, scale=2.0)
+                else:
+                    act(wx, w3, AF.Relu, bias=-15.5 * 16384, scale=16384.0)
+                X = H("X")
+                if h in XP:
+                    X, ns = H("w1"), H("d0")
+                if h in SAMEV:
+                    ts(ns, H("dp"), C4096, ALU.add, C4096, ALU.is_equal)
+                else:
+                    act(H("dp"), H("dp"), AF.Abs)
+                    act(ns, H("dp"), AF.Relu, bias=-2047.5 * BIG, scale=BIG)
+                dla, dlb = B("dl", 2 * lo, lo + hi), B("dl", lo + hi, 2 * hi)
+                dqa, dqb = B("dq%d" % h, 0, hi - lo), B("dq%d" % h, hi - lo)
                 total(dqa, ("idk", H("kpa")), ("idx", H("k1a")), ("idn", H("ibp")))
-            if not JOINT:
-                act(dla, dqa, AF.Relu, bias=cut)
-            total(dqb, ("idn", H("iap")), ("idk", H("spb")), ("idx", H("k1b")))
-            if JOINT:
-                act(B("dl", 2 * lo, 2 * hi), dq, AF.Relu, bias=cut)
-            else:
-                act(dlb, dqb, AF.Relu, bias=cut)
-            if TBP:
-                total(H("tbp"), ("idf", H("fy" if last else "aw")), ("idn", H("cb")))
-                act(H("tb"), H("tbp"), AF.Relu)
-            else:
+                total(dqb, ("idn", H("iap")), (ks_, H("spb")), (xk, H("k1b")))
+                act(B("dl", 2 * lo, 2 * hi), dq, AF.Relu, bias=-10.0)
                 tt(H("tb"), H("fy" if last else "aw"), wx, ALU.subtract)
-            wa = H("w1")
-            if h in W1P and not last:
-                wa = H("a75" if h else "tbp")
-                total(wa, ("idb", H("kpa")), ("idn", H("spa")), ("idf", half(A, h)), ("idb", dla))
-            else:
+                wa = H("w1")
                 tt(wa, out("aP", h) if last else wa, dla, ALU.add)
-            tt(H("bt"), wo, dlb, ALU.add)
-            tt(H("X"), wa, H("bt"), ALU.max)
-            tt(xb, wo, H("tb"), ALU.max)
-            tt(Y, H("X"), ns, ALU.mult if h in SAMEV else ALU.subtract)
+                tt(H("bt"), wo, dlb, ALU.add)
+                tt(X, wa, H("bt"), ALU.max)
+                tt(xb, wo, H("tb"), ALU.max)
+                tt(Y, X, ns, ALU.mult if h in SAMEV else ALU.subtract)
             if h:
                 behind("met", AHEAD[1])
             mark("met")
@@ -1062,14 +1478,13 @@ def record(T):
         if not last:
             for h in (2, 0, 1):
                 mm(B("cnt"), B("allf"), B("wacc", h, h + 1), h == 2, h == 1)
-            ts(B("ta"), B("cnt"), 2 * C16, ALU.add, 2 * C16, ALU.subtract)
-            tt(B("sc%d" % t), B("cnt"), B("ta"), ALU.subtract)
+            ts(B("sc%d" % t, 0, 1), B("cnt"), -496.0, ALU.add)
+            ts(B("sc%d" % t, 1, 2), B("cnt"), C4096 / 4, ALU.add, C4096 / 4, ALU.subtract)
             send("c%d" % t)
-            mm(B("ctp"), B("idb"), cls("Ctb", t + 1), True, True)
 
     expect("T%d" % NR)
     for c in range(4):
-        decode(B("yo", 256 * c, 256 * c + 256), B("TB4", 256 * c, 256 * c + 256), B("spare"), 256 * c)
+        decode(B("yo", 256 * c, 256 * c + 256), B("TB4", 256 * c, 256 * c + 256), B(("spare", "ctp")[c % 2]), 256 * c)
     complete(NR, "yo")
     put("dma", "y", lambda e: e.dma_start(T.yent[:], ap(B("yo", 0, 1024))), [B("yo")], [], 4.5, sem="st", inc=16)
     return ops

import math
from concourse.bass import DstId, RemoteDMATransfer
from concourse.mybir import AluOpType as ALU, ActivationFunctionType as AF, AxisListType

NR = 4
BIG = float(1 << 24)
C16, C4096, C1 = 1.5 * (1 << 27), 1.5 * (1 << 35), 1.5 * (1 << 23)
FV = (1, 3)
PARTS = ((0, 8, "SSVV"), (8, 16, "SSVV"))
AHEAD = (2.5, 2.5, 0.0, 1.5, 2.0)
PEN = 2 * BIG
SHIFT = {"S": 131072.0, "M": 262144.0, "V": 0.0}
LAT = {"A": 6.0, "U": 4.2, "T": 14.0, "f": 14.0, "b": 5.5, "a": 5.5, "c": 4.7}
WAKE = 0.2
FIX, FIXS = 0.0, 0.0
FIXP, SAME = 0.0, 0.25
CY, G, SC, CALL = 0.00083, 1.3, 3.8, 0.7
VFIRST = 2
SAMEV = (1,)
EH, ROWS, KI, TC, TAP, TBP, EX = (), True, True, False, False, False, (0, 1)
W3P, FL = False, ("", "")
HS, W1P, GI = 0, (0, 1), False
JP, JE, JT, HF = 8, 4, 2, 1
MOVE = {"p2": "pu", "wx": "tk", "ns": "pk"}
SUMS, LS, DA = ((0, 1, 2), (0, 1, 2)), True, True
EPV, HB, FV0 = (), (), (1, 3, 5, 7)
US, JOINT = (0, 1), True
PICKS = None
JOG, TRIES = 0.5, 60
WIDE = 2
LISTS = ("lstP", "lstQ", "lstI", "lstR", "lst8", "off", "eu", "e16", "pos", "pos2", "sel")
CASES = ((1.0, 1.3, 3.8, 0.2, 0.25, 1.0, 0.4), (1.1, 1.6, 3.0, 0.15, 0.18, 0.85, 0.35), (1.35, 2.2, 6.0, 0.2, 0.25, 1.15, 0.25))
TURNS = 10
SWAPS, SLACK = 4000, 0.02
PASSES = 6

DA, WIDE, PICKS, VFIRST, TRIES, SWAPS, TURNS = False, 0, (0, 2, 3, 1, 4, 5, 6, 7), 1, 10, 600, 45
LS, SLACK, FV, W1P = True, 0.005, (1, 3, 5), ()
KC, KB = ("ss", "ss"), (("m0", 128), ("m1", 128))
STEP, NEAR, SWAPS, SLACK, TURNS = 50, 0.1, 350, 0.04, 6
UF, OD = 2, (0, 1)
FAST, FL, TC = (), ("", ""), True
GI, JP, HF = True, 4, 0
WXP, XP = (), ()
SEED, HOPS, EVERY, COPIES = 11, (0, 0, 0, 1, 2), 4, ((1, 2), (2, 1), (3, 2), (2, 3), (0, 1))
LONG, TC, GAP2 = 0.5, True, 1.7
CASES = ((1.0, 1.15, 3.0, 0.2, 0.25, 1.05, 0.5, 1.2, 1.2), (1.1, 1.6, 3.0, 0.15, 0.18, 0.85, 0.35, 0.85, 1.0), (1.35, 2.2, 6.0, 0.2, 0.25, 1.15, 0.15, 1.15, 1.3))
TCP = (1,)
TW, F3, TF = 0.5, 0, True
HOPS, STEP, SWAPS, SLACK = (0, 0, 1, 2, 4), 35, 250, 0.03
PICKS, AHEAD, TURNS = (0, 1, 2, 4, 3, 5, 6, 7), (2.0, 2.0, 0.0, 1.8, 2.0), 44
CS = (0, 1, 2, 3)
SCRATCH, PART = {}, {}


def _sb(dtype, **cols):
    b = "all" + dtype
    for n in cols:
        at = SCRATCH[b][1][1] if b in SCRATCH else 0
        SCRATCH[b] = ("sbuf", [128, at + (cols[n] + 15) // 16 * 16], dtype)
        PART[n] = (b, at, cols[n], n)


def _ps(bank, **views):
    SCRATCH[bank] = ("psum", [128, 512], "float32")
    for n in views:
        PART[n] = (bank, views[n][0], views[n][1], bank)


_sb("int32", entx=1024, wti=1, kpi=1, ci=64, pmi=16, pmj=16, n1=256, q=256, k1=256, za=256, l5a=256, ui=32, ub=32,
    ei=256, em=256, ky=32, er=32, qb=256, zb=256, l5b=256, jd=16, kx=256)
_sb("bfloat16", fx0=2064, fx2=2064, fx3=2064, one=128, blka=128, blk=128, idb=128, idn=128, idk=128, idw=128, idx=128, hid=128, cb=256, zer=32, dlt=16,
    rA=128, rK=16, sgm=512, fl=16, spa=256, kpa=256, k1a=256, iap=256, ca=256, da=256, spb=256, kpb=256, k1b=256, ibp=256, dl=512,
    blw=128, blx=128, thr=128, lab=256, Yg=4096, Ys=4096, Xb=4096, ebx=256, erx=32, l5g=256, zag=256)
SCRATCH["EQ"] = ("sbuf", [128, 16, 256], "bfloat16")
SCRATCH["KT"] = ("sbuf", [128, 32, 2, 8], "bfloat16")
RUNS = sorted(set(_p[2][_i:_i + 2] for _p in PARTS for _i in (0, 2)))
_sb("bfloat16", NM=4096, NM2=4096, b8n=8, prm=64, **{"prm" + _r: 64 for _r in RUNS})
PATHS = sorted(set(_p[2] for _p in PARTS))
_sb("bfloat16", x128=128, zw=144, **{"nil" + _r: 128 for _r in PATHS})
_sb("bfloat16", idp=128, hi2=128, ix2=128, iw2=128)
_sb("float32", msk=2, rsc=1, t128=1, d0=256, mid=8, ksq=128)
_sb("float16", eh=256, idh=128)
_sb("uint16", lstP=16, lstQ=16, lstI=16, lstR=8, lst8=8, off=256, eu=256, e16=16, ebc=256, pos=16, pos2=16, sel=16)
_sb("float32", old0=288, Ct=1024, la0=288, old1=288, iot=1024, la1=288, old2=288, TB0=1024, la2=288, old3=288, TB4=1024, la3=288, TB1=1320,
    TB2=1320, TB3=1320, aw=256, sv=256, cap=16, pw=16, LB0=1320, LB1=1320, yo=1320, D=4096, TC0=1024, TC1=1024, idf=128, allf=128, pmf=16,
    x16=16, cmk=16, lI=16, wk=2, pr=256, x1=256, oc=256, oT=1536, kyf=16, sU=80, lU=80, uk=80, uq=32,
    sA=256, lR=256, lA=256, ef=256, erf=32, wacc=3, ta=1, bF=256, dp=256, tb=256, bt=256, X=256, fa=256, fb=256, fy=256,
    d1=1024, d2=1024, lpf=16, lpq=2, xq=8, lcx=1, YP=8 * 288)
for _t in range(NR):
    _sb("float32", **{"xb%d" % _t: 288, "lb%d" % _t: 288, "Y%d" % _t: 288, "sc%d" % _t: 2, "lc%d" % _t: 2})
    PART["ta%d" % _t] = (PART["YP"][0], PART["YP"][1] + 576 * _t, 288, "ta%d" % _t)
    PART["aP%d" % _t] = (PART["YP"][0], PART["YP"][1] + 576 * _t + 288, 288, "aP%d" % _t)
    PART["win%d" % _t] = PART["old%d" % _t][:2] + (1600, "win")
GAP, FAR = ("Ct", "iot", "TB0", "TB4"), 1312.0
_ps("pu", up=(0, 16), cnt=(32, 1), kmp=(128, 16), spare=(256, 256))
_ps("pc", pcp=(0, 256), ctp=(256, 256))
_ps("pa", a75=(0, 256), w1=(256, 256))
_ps("tk", tbp=(0, 256), sp2=(256, 256), tb0=(0, 128), tb1=(128, 128))
for _h, (_k0, _k1, _) in enumerate(PARTS):
    _n, _h = 16 * (_k1 - _k0), str(_h)
    _ps("pk" + _h, **{"big" + _h: (0, 512), "key" + _h: (0, _n), "dq" + _h: (512 - 2 * _n, 2 * _n)})
    _ps("m" + _h, **{"u" + _h: (0, 512), "w3" + _h: (0, _n), "p2" + _h: (_n, _n)})
    if _n <= 128:
        _ps("m" + _h, **{"ns" + _h: (2 * _n, _n), "wx" + _h: (3 * _n, _n)})
    else:
        _ps("tk", **{"ns" + _h: (0, _n), "wx" + _h: (256, _n)})
    for _v, _b in MOVE.items():
        PART[_v + _h] = {"tk": ("tk", 16 * _k0, _n, "tk"), "pk": ("pk" + _h, 128, _n, "pk" + _h), "pu": ("pu", 256 + 16 * _k0, _n, "pu")}[_b]
for _h in "01":
    PART["kt" + _h] = (KB[int(_h)][0], KB[int(_h)][1], 128, KB[int(_h)][0])
    PART["ep" + _h] = ("m" + _h, 256, 128, "m" + _h)


def messages(n):
    x = [-1]
    for t in range(NR):
        x.append(x[-1] + 1 + t % (n - 1))
    hold = x[1:] + [0]
    out = {}

    def piece(m, src, dst, lo, hi, by, kind):
        src = src if isinstance(src, tuple) else (src,)
        for name in src + (dst,):
            PART[name + m] = (PART[name][0], PART[name][1] + lo, hi - lo, name)
        out[m] = (tuple(s + m for s in src), dst + m, hi - lo, by, kind)
    for h, (k0, k1, path) in enumerate(PARTS):
        piece("U%d" % h, "sU", "lU", (16 + k0) * h, 16 + k1, -x[0], "cb"[h])
        piece("A%d" % h, "sA", "lR", 16 * k0, 16 * k1, -x[0], "ba"[h])
    for t in range(NR):
        piece("T%d" % (t + 1), "TB%d" % t, "TB%d" % (t + 1), 0, 1024, hold[t] - hold[t + 1], "T")
        if t > 1:
            piece("f%d" % t, "fx0", "fx%d" % t, 0, 2064, -x[t], "f")
        if t + 1 < NR:
            piece("c%d" % t, "sc%d" % t, "lc%d" % t, 0, 2, x[t] - x[t + 1], "c")
        for h, (k0, k1, path) in enumerate(PARTS):
            lo, hi = (16 * k0 + 16, 272 + k1 - k0) if h else (16 - k1, 16 * k1 + 16)
            piece("b%d%d" % (t, h), ("xb%d" % t, "Y%d" % t), "lb%d" % t, lo, hi, hold[t] - hold[t + 1], "b")
            piece("a%d%d" % (t, h), ("ta%d" % t, "Y%d" % t, "aP%d" % t), "la%d" % t, lo, hi, x[t] - hold[t + 1], "a")
    return out


MSG = messages(8)
SEMAPHORES = ["qv", "qs", "qp", "qg", "ld0", "ld1", "ld4", "ld5", "ld6", "st", "lsem"] + ["oc%d" % _i for _i in range(2 * NR)] + ["t%s%d" % (_c, _i) for _i in range(NR) for _c in "cd"] + sorted(MSG)


def bits(m):
    return bin(m).count("1")


def route(topo, T, src, dst, m):
    if (src, dst, m) not in WAYS:
        here = topo.cores_of(src)
        alone = all(T.cores[(r + MSG[m][3]) % len(T.cores)] in here for r, c in enumerate(T.cores) if c in here and c != src)
        WAYS[(src, dst, m)] = ways(topo, T, src, dst, MSG[m][2], MSG[m][4], alone)
    return WAYS[(src, dst, m)]


WAYS = {}


def ways(topo, T, src, dst, w, kind, alone):
    if dst in topo.cores_of(src):
        return [((), 0, w)]
    free = [c for c in topo.cores_of(src) if T.rank_of(c) is None]
    mine = [c for c in free if topo.die(c) == topo.die(src)]
    near = [c for c in mine if topo.may_write(c, dst)]
    if kind in "abc":
        return [(() if topo.may_write(src, dst) else (near[0 if kind == "b" else 1],), 0, w)]
    if alone:
        chains = [(c,) for c in free if topo.may_write(c, dst) and c not in mine] + [(c,) for c in near]
    else:
        far = [c for c in range(256) if topo.mates(c, dst) and topo.may_write(c, dst) and topo.die(c) == topo.die(src)]
        round_ = [c for c in mine if c not in near]
        chains = [(c, far[0]) for c in round_] + [(c,) for c in near if c not in round_]
        if kind == "F":
            chains = [(round_[0], far[-1])]
    part = [LONG if len(c) > 1 else 1.0 for c in chains]
    cut = [(int(w * sum(part[:j]) / sum(part)) + 15) // 16 * 16 for j in range(len(chains))] + [w]
    return [(chains[j], cut[j], cut[j + 1]) for j in range(len(chains))]


def share(topo, T, core, to, m):
    rank = T.rank_of(core)
    if rank is None or m[0] not in "ab":
        return topo.mask(core, to)
    other = "ba"["ab".index(m[0])] + m[1:]
    dst = T.cores[(rank + MSG[other][3]) % len(T.cores)]
    mine, its = topo.engines(core, to), topo.engines(core, (route(topo, T, core, dst, other)[0][0] + (dst,))[0])
    if len(mine) > len(its):
        mine = [e for e in mine if e not in its]
    elif len(mine) == len(its):
        mine = mine[:len(mine) // 2] if m[0] == "a" else mine[len(mine) // 2:]
    return sum(1 << e for e in mine)


def view(T, name, lo, hi):
    b, at = PART[name][:2]
    return T[b][:, at + lo:at + hi]


def hand_on(g, core, T, topo):
    sent, n = 0, len(T.cores)
    for m in plan(T)[2]:
        for r in range(n):
            src, dst = T.cores[r], T.cores[(r + MSG[m][3]) % n]
            for chain, lo, hi in route(topo, T, src, dst, m):
                if core not in chain:
                    continue
                way = (src,) + chain + (dst,)
                before, to = way[way.index(core) - 1], way[way.index(core) + 1]
                b = view(T, MSG[m][1], lo, hi)
                g.wait_ge(T.sem[m], bits(share(topo, T, before, core, m)))
                rid, pid = topo.addr(to, core)
                mk = topo.mask(core, to)
                g.remote_dma(b, b, T.sem[m], T.sem.lsem, pid, rid, mk)
                sent += bits(mk)
    if sent:
        g.wait_ge(T.sem.lsem, sent)


def B(name, lo=0, hi=None, st=1):
    b, at, w, key = PART[name]
    return (b, at + lo, at + (w if hi is None else hi), st, key)


def rows(k0, k1, lo, hi):
    return ("EQ", 256 * k0 + lo, 256 * (k1 - 1) + hi, 1, "EQ", ((k0, k1) if k1 > k0 + 1 else k0, (lo, hi)))


def width(x):
    if len(x) > 5:
        return math.prod(i[1] - i[0] for i in x[5] if isinstance(i, tuple))
    return (x[2] - x[1] + x[3] - 1) // x[3]


def meets(a, b):
    if a[2] <= b[1] or b[2] <= a[1]:
        return False
    return not (a[3] == b[3] and a[3] > 1 and (a[1] - b[1]) % a[3])


def covers(a, b):
    return a[1] <= b[1] and b[2] <= a[2] and (a[3] == 1 or (a[3] == b[3] and (a[1] - b[1]) % a[3] == 0))


def links(ops):
    acc, out, group = {}, [], {}
    for i, o in enumerate(ops):
        pre = set(o["after"])
        o["banks"] = sorted(set(x[0] for x in o["r"] + o["w"] if SCRATCH[x[0]][0] == "psum"))
        if o["q"] == "p":
            if o["banks"][0] in group:
                pre.add(group[o["banks"][0]])
            group[o["banks"][0]] = i
        for wr, lst in ((False, o["r"]), (True, o["w"])):
            for x in lst:
                for (y, w2, j) in acc.get(x[4], []):
                    if j != i and (wr or w2) and meets(x, y):
                        pre.add(j)
        for x in o["w"]:
            acc[x[4]] = [a for a in acc.get(x[4], []) if a[2] == i or not covers(x, a[0])]
            acc[x[4]].append((x, True, i))
        for x in o["r"]:
            acc.setdefault(x[4], []).append((x, False, i))
        out.append(sorted(pre))
    return out


def lasts(o, case):
    if o["kind"] != "run":
        return o["dur"] * (case[8] if o["kind"] == "send" else 1.0 if o["kind"] != "land" else case[7] if o["msg"][0] in "Tf" else case[5])
    if "each" in o:
        return o["dur"] + o["each"][0] * CY * (case[o["each"][1]] - (G, SC)[o["each"][1] - 1])
    return o["dur"] * case[0]


def polish(ops, pre, seq, wake, turn):
    n = len(ops)
    q = [o["q"] if o["kind"] != "land" else None for o in ops]
    banks = [[([b + r for r in "vsp" if r != q[i]], b + q[i]) for b in ops[i]["banks"]] for i in range(n)]
    needs = [set(pre[i]) | set(j for j, lag in ops[i]["behind"] if ops[i]["kind"] != "run" or "firm" in ops[i]) for i in range(n)]
    cases = []
    for case in CASES:
        dur = [lasts(o, case) for o in ops]
        cases.append((dur, [dur[i] if ops[i]["kind"] in ("run", "send") else 0.05 for i in range(n)],
                      [[(j, dur[j] + (0.0 if ops[j]["kind"] == "send" else case[3] if q[i] != q[j] else case[4])) for j in pre[i]
                        if not (q[i] == "p" and q[j] == "p") and (ops[j]["kind"] != "send" or q[i] is None)] for i in range(n)], case[3]))

    def runs(seq, at, was):
        got = [run(seq, at, was and was[1][c], *cases[c]) for c in range(len(cases))]
        return sum(got[c][0] * CASES[c][6] for c in range(len(cases))), got

    def run(seq, at, was, dur, hold, dep, wake):
        at -= at % 64
        st, by, marks = (list(was[2]), list(was[3]), was[4][:at // 64]) if at else ([0.0] * n, [-1] * n, [])
        last, end, who = (dict(was[4][at // 64]) if at else {}), 0.0, -1
        for x in range(at, n):
            if not x % 64:
                marks.append(dict(last))
            i = seq[x]
            t, w, k = 0.0, -1, q[i]
            if k:
                j = last.get(k, -1)
                if j >= 0:
                    t, w = st[j] + hold[j], -2 - j
                last[k] = i
            for j, lag in dep[i]:
                if st[j] + lag > t:
                    t, w = st[j] + lag, j
            for others, me in banks[i]:
                for r in others:
                    j = last.get(r, -1)
                    if j >= 0 and st[j] + dur[j] + wake > t:
                        t, w = st[j] + dur[j] + wake, j if j in needs[i] else -2 - j
                last[me] = i
            st[i], by[i] = t, w
            if t + dur[i] > end:
                end, who = t + dur[i], i
        return end, who, st, by, marks

    def swap(seq, pa, pb, forth):
        mid = seq[pa:pb + 1]
        if forth:
            move = {mid[-1]}
            for i in mid[::-1]:
                if i in move:
                    move |= needs[i]
            if mid[0] in move:
                return None
            return seq[:pa] + [i for i in mid if i in move] + [i for i in mid if i not in move] + seq[pb + 1:]
        move = {mid[0]}
        for i in mid:
            if needs[i] & move:
                move.add(i)
        if mid[-1] in move:
            return None
        return seq[:pa] + [i for i in mid if i not in move] + [i for i in mid if i in move] + seq[pb + 1:]

    seed = [7 + turn]

    def draw(k):
        seed[0] = (seed[0] * 1103515245 + 12345) % 2147483648
        return (seed[0] >> 8) % k
    cur, left = runs(seq, 0, None), SWAPS
    best = (cur[0], seq, cur[1][0][2])
    while left > 0:
        place = {i: x for x, i in enumerate(seq)}
        seq = sorted(seq, key=lambda i: (cur[1][0][2][i], place[i]))
        cur = runs(seq, 0, None)
        for _ in range(40):
            one = cur[1][draw(len(cases))]
            place, pairs, i = {i: x for x, i in enumerate(seq)}, [], one[1]
            while one[3][i] != -1:
                j = one[3][i]
                if j < -1:
                    j = -2 - j
                    pairs.append((j, i))
                i = j
            while left > 0:
                left -= 1
                k, hop, forth = draw(len(pairs)), (0, 0, 1, 2, 4)[draw(5)], draw(2)
                a, b = pairs[k]
                while hop and forth and k + 1 < len(pairs) and pairs[k + 1][1] == a:
                    k, a, hop = k + 1, pairs[k + 1][0], hop - 1
                while hop and not forth and k and pairs[k - 1][0] == b:
                    k, b, hop = k - 1, pairs[k - 1][1], hop - 1
                other = swap(seq, place[a], place[b], forth)
                bar = cur[0] - SLACK * math.log((draw(1000) + 1) / 1001)
                if other:
                    new = runs(other, place[a], cur)
                    if new[0] < bar:
                        seq, cur = other, new
                        break
            if cur[0] < best[0]:
                best = (cur[0], seq, cur[1][0][2])
    return best


def refine(ops, pre, seq):
    n, nc = len(ops), len(CASES)
    q = [o["q"] if o["kind"] != "land" else None for o in ops]
    own = [[b + q[i] for b in ops[i]["banks"]] for i in range(n)]
    other = [[b + r for b in ops[i]["banks"] for r in "vsp" if r != q[i]] for i in range(n)]
    needs = [set(pre[i]) | set(j for j, lag in ops[i]["behind"] if ops[i]["kind"] != "run" or "firm" in ops[i]) for i in range(n)]
    dur = [[lasts(o, case) for o in ops] for case in CASES]
    hold = [[d[i] if ops[i]["kind"] in ("run", "send") else 0.05 for i in range(n)] for d in dur]
    shut = [[x + case[3] for x in d] for d, case in zip(dur, CASES)]
    dep = [[[(j, d[j] + (0.0 if ops[j]["kind"] == "send" else case[3] if q[i] != q[j] else case[4])) for j in pre[i]
             if not (q[i] == "p" and q[j] == "p") and (ops[j]["kind"] != "send" or q[i] is None)] for i in range(n)] for d, case in zip(dur, CASES)]
    suc = [[[] for _ in ops] for _ in CASES]
    for c in range(nc):
        for i in range(n):
            for j, lag in dep[c][i]:
                suc[c][j].append((i, lag))
    head, tail, by = [[0.0] * n for _ in CASES], [[0.0] * n for _ in CASES], [[-1] * n for _ in CASES]
    seed = [11]

    def draw(k):
        seed[0] = (seed[0] * 1103515245 + 12345) % 2147483648
        return (seed[0] >> 8) % k

    def forth(part, last, c, keep=None):
        h, ho, sh, de, w = head[c], hold[c], shut[c], dep[c], by[c]
        for i in part:
            if keep is not None:
                keep.append(dict(last))
            t, who, k = 0.0, -1, q[i]
            if k:
                if k in last:
                    who = last[k]
                    t = h[who] + ho[who]
                last[k] = i
            for j, lag in de[i]:
                if h[j] + lag > t:
                    t, who = h[j] + lag, -1
            for r in other[i]:
                if r in last and h[last[r]] + sh[last[r]] > t:
                    who = last[r]
                    t = h[who] + sh[who]
            for r in own[i]:
                last[r] = i
            h[i], w[i] = t, who

    def back(part, nxt, c, keep=None):
        h, g, ho, sh, su, du, top = head[c], tail[c], hold[c], shut[c], suc[c], dur[c], 0.0
        for i in part[::-1]:
            if keep is not None:
                keep.append(dict(nxt))
            t, k = du[i], q[i]
            if k:
                if k in nxt and ho[i] + g[nxt[k]] > t:
                    t = ho[i] + g[nxt[k]]
                nxt[k] = i
            for j, lag in su[i]:
                if lag + g[j] > t:
                    t = lag + g[j]
            for r in other[i]:
                if r in nxt and sh[i] + g[nxt[r]] > t:
                    t = sh[i] + g[nxt[r]]
            for r in own[i]:
                nxt[r] = i
            g[i] = t
            if h[i] + t > top:
                top = h[i] + t
        return top

    def both(part, last, nxt):
        before, after = [], []
        for c in range(nc):
            forth(part, dict(last), c, None if c else before)
        return [back(part, dict(nxt), c, None if c else after) for c in range(nc)], before, after[::-1]

    def worth(ends):
        return sum(e * case[6] for e, case in zip(ends, CASES))

    def turned(mid, up):
        move = {mid[-1] if up else mid[0]}
        for i in mid[::-1] if up else mid:
            if up and i in move:
                move |= needs[i]
            elif not up and needs[i] & move:
                move.add(i)
        if mid[0 if up else -1] in move:
            return None
        a, b = [i for i in mid if i in move], [i for i in mid if i not in move]
        return a + b if up else b + a

    def stretch(seq, lo, hi, slack):
        ends, before, after = both(seq, {}, {})
        part, last, nxt = seq[lo:hi], before[lo], after[hi - 1]
        ends, before, after = both(part, last, nxt)
        best, left = (worth(ends), part), SWAPS
        while left > 0:
            place = {i: x for x, i in enumerate(part)}
            pairs = [(by[c][i], i) for c in range(nc) for i in part
                     if by[c][i] in place and head[c][i] + tail[c][i] > ends[c] - NEAR and by[c][i] not in needs[i]]
            if not pairs:
                break
            for _ in range(60):
                left -= 1
                a, b = pairs[draw(len(pairs))]
                pa, pb, up = place[a], place[b], draw(2)
                for _ in range((0, 0, 0, 1, 2)[draw(5)]):
                    if up and before[pa].get(q[a]) in place:
                        pa = place[before[pa][q[a]]]
                    if not up and after[pb].get(q[b]) in place:
                        pb = place[after[pb][q[b]]]
                mid = part[pa:pb + 1]
                new = turned(mid, up)
                if not new:
                    continue
                bar, old, guess = worth(ends) - slack * math.log((draw(1000) + 1) / 1001), [], []
                for c in range(nc):
                    old.append([(head[c][i], tail[c][i], by[c][i]) for i in mid])
                    was = max(x[0] + x[1] for x in old[c])
                    forth(new, dict(before[pa]), c)
                    top = back(new, dict(after[pb]), c)
                    guess.append(top if was > ends[c] - 1e-9 else max(top, ends[c]))
                if worth(guess) < bar:
                    whole, ahead, behind = part[:pa] + new + part[pb + 1:], [], []
                    for c in range(nc):
                        forth(whole[pa:], dict(before[pa]), c, None if c else ahead)
                        back(whole[:pb + 1], dict(after[pb]), c, None if c else behind)
                    got = [max([h[i] + g[i] for i in part]) for h, g in zip(head, tail)]
                    if worth(got) < bar:
                        part, ends, before, after = whole, got, before[:pa] + ahead, behind[::-1] + after[pb + 1:]
                        break
                    both(part, last, nxt)
                else:
                    for c in range(nc):
                        for i, x in zip(mid, old[c]):
                            head[c][i], tail[c][i], by[c][i] = x
            if worth(ends) < best[0]:
                best = (worth(ends), part)
        return seq[:lo] + best[1] + seq[hi:]

    for turn in range(TURNS):
        both(seq, {}, {})
        place = {i: x for x, i in enumerate(seq)}
        seq = sorted(seq, key=lambda i: (head[0][i], place[i]))
        for lo in range(-(turn * 37 % STEP), n, STEP):
            seq = stretch(seq, max(lo, 0), min(lo + 2 * STEP, n), SLACK * (1 - turn / TURNS))
    return worth(both(seq, {}, {})[0]), seq


def better(ops, pre, seq):
    n = len(ops)
    w0, w1, w2 = [case[6] for case in CASES]
    q = [o["q"] if o["kind"] != "land" else "land" for o in ops]
    own = [[q[i]] + [b + q[i] for b in ops[i]["banks"]] for i in range(n)]
    other = [[b + r for b in ops[i]["banks"] for r in "vsp" if r != q[i]] for i in range(n)]
    needs = [set(pre[i]) | set(j for j, lag in ops[i]["behind"] if ops[i]["kind"] != "run" or "firm" in ops[i]) for i in range(n)]
    dur = [tuple(lasts(o, case) for case in CASES) for o in ops]
    hold = [dur[i] if ops[i]["kind"] in ("run", "send") else (ops[i].get("hold", 0.05),) * 3 if q[i] != "land" else (-99.0,) * 3 for i in range(n)]
    shut = [tuple(x + case[3] for x, case in zip(d, CASES)) for d in dur]
    dep, suc = [[] for _ in ops], [[] for _ in ops]
    for i in range(n):
        for j in pre[i]:
            if not (q[i] == "p" and q[j] == "p") and (ops[j]["kind"] != "send" or q[i] == "land"):
                lag = tuple(x + (0.0 if ops[j]["kind"] == "send" else case[3 if q[i] != q[j] else 4]) for x, case in zip(dur[j], CASES))
                dep[i].append((j,) + lag)
                suc[j].append((i,) + lag)
        if "gap" in ops[i]:
            j, lag = ops[i]["gap"], tuple(GAP2 * case[5] for case in CASES)
            needs[i].add(j)
            dep[i].append((j,) + lag)
            suc[j].append((i,) + lag)
    head, tail, seed = [None] * n, [None] * n, [SEED]

    def draw(k):
        seed[0] = (seed[0] * 1103515245 + 12345) % 2147483648
        return (seed[0] >> 8) % k

    def forth(part, last, keep=None):
        for i in part:
            if keep is not None:
                keep.append(dict(last))
            a = b = c = 0.0
            if q[i] in last:
                j = last[q[i]]
                (a, b, c), (x, y, z) = head[j], hold[j]
                a, b, c = a + x, b + y, c + z
            for j, x, y, z in dep[i]:
                u, v, w = head[j]
                if u + x > a:
                    a = u + x
                if v + y > b:
                    b = v + y
                if w + z > c:
                    c = w + z
            for r in other[i]:
                if r in last:
                    (u, v, w), (x, y, z) = head[last[r]], shut[last[r]]
                    if u + x > a:
                        a = u + x
                    if v + y > b:
                        b = v + y
                    if w + z > c:
                        c = w + z
            for r in own[i]:
                last[r] = i
            head[i] = (a, b, c)

    def back(part, nxt, keep=None):
        for i in part[::-1]:
            if keep is not None:
                keep.append(dict(nxt))
            a, b, c = dur[i]
            for j, x, y, z in suc[i] + [(nxt[r],) + shut[i] for r in other[i] if r in nxt] + ([(nxt[q[i]],) + hold[i]] if q[i] in nxt else []):
                u, v, w = tail[j]
                if u + x > a:
                    a = u + x
                if v + y > b:
                    b = v + y
                if w + z > c:
                    c = w + z
            for r in own[i]:
                nxt[r] = i
            tail[i] = (a, b, c)

    def longest(part):
        a = b = c = 0.0
        for i in part:
            (u, v, w), (x, y, z) = head[i], tail[i]
            if u + x > a:
                a = u + x
            if v + y > b:
                b = v + y
            if w + z > c:
                c = w + z
        return a, b, c

    def both(part, last, nxt):
        before, after = [], []
        forth(part, dict(last), before)
        back(part, dict(nxt), after)
        return longest(part), before, after[::-1]

    def worth(ends):
        return w0 * ends[0] + w1 * ends[1] + w2 * ends[2]

    def turned(mid, up):
        move = {mid[-1] if up else mid[0]}
        for i in mid[::-1] if up else mid:
            if up and i in move:
                move |= needs[i]
            elif not up and needs[i] & move:
                move.add(i)
        if mid[0 if up else -1] in move:
            return None
        a, b = [i for i in mid if i in move], [i for i in mid if i not in move]
        return a + b if up else b + a

    def stretch(seq, lo, hi, slack):
        ends, before, after = both(seq, {}, {})
        part, last, nxt = seq[lo:hi], before[lo], after[hi - 1]
        ends, before, after = both(part, last, nxt)
        best, left = (worth(ends), part), SWAPS
        while left > 0:
            place, pairs = {i: x for x, i in enumerate(part)}, []
            for x, i in enumerate(part):
                for c in range(3):
                    if head[i][c] + tail[i][c] > ends[c] - NEAR:
                        for r, lag in [(q[i], hold)] + [(r, shut) for r in other[i]]:
                            j = before[x].get(r)
                            if j in place and j not in needs[i] and head[j][c] + lag[j][c] > head[i][c] - 1e-9:
                                pairs.append((j, i))
            if not pairs:
                break
            for _ in range(60):
                left -= 1
                a, b = pairs[draw(len(pairs))]
                pa, pb, up = place[a], place[b], draw(2)
                for _ in range(HOPS[draw(len(HOPS))]):
                    if up and before[pa].get(q[a]) in place:
                        pa = place[before[pa][q[a]]]
                    if not up and after[pb].get(q[b]) in place:
                        pb = place[after[pb][q[b]]]
                mid = part[pa:pb + 1]
                new = turned(mid, up)
                if not new:
                    continue
                bar, old, was = worth(ends) - slack * math.log((draw(1000) + 1) / 1001), [(head[i], tail[i]) for i in mid], longest(mid)
                forth(new, dict(before[pa]))
                back(new, dict(after[pb]))
                if worth([t if s > e - 1e-9 else max(t, e) for s, t, e in zip(was, longest(mid), ends)]) < bar:
                    whole, ahead, behind = part[:pa] + new + part[pb + 1:], [], []
                    forth(whole[pa:], dict(before[pa]), ahead)
                    back(whole[:pb + 1], dict(after[pb]), behind)
                    got = longest(part)
                    if worth(got) < bar:
                        part, ends, before, after = whole, got, before[:pa] + ahead, behind[::-1] + after[pb + 1:]
                        break
                    both(part, last, nxt)
                else:
                    for i, x in zip(mid, old):
                        head[i], tail[i] = x
            if worth(ends) < best[0]:
                best = (worth(ends), part)
        return seq[:lo] + best[1] + seq[hi:]

    def copied(seq, t, s):
        both(seq, {}, {})
        like = {ops[i]["role"]: i for i in seq if ops[i]["round"] == s}
        pairs = [(i, like[ops[i]["role"]]) for i in seq if ops[i]["round"] == t and ops[i]["role"] in like]
        off = sorted(head[i][0] - head[j][0] for i, j in pairs)[len(pairs) // 2]
        key = {i: (head[i][0], x) for x, i in enumerate(seq)}
        place = {i: x for x, i in enumerate(seq)}
        for i, j in pairs:
            key[i] = (head[j][0] + off, place[j])
        out, done = [], set()

        def take(i):
            if i not in done:
                done.add(i)
                for j in sorted(needs[i], key=key.get):
                    take(j)
                out.append(i)
        for i in sorted(seq, key=key.get):
            take(i)
        return out

    def sweep(seq, slack, turn, lo=0, hi=n):
        both(seq, {}, {})
        place = {i: x for x, i in enumerate(seq)}
        seq = sorted(seq, key=lambda i: (head[i][0], place[i]))
        for at in range(lo - turn * 37 % STEP, hi, STEP):
            seq = stretch(seq, max(at, 0), min(at + 2 * STEP, n), slack)
        return seq

    for turn in range(TURNS):
        both(seq, {}, {})
        seq = sweep(seq, SLACK * (1 - turn / TURNS), turn)
        if turn % EVERY == EVERY - 1:
            for t, s in COPIES:
                at = [x for x, i in enumerate(seq) if ops[i]["round"] == t]
                new = sweep(copied(seq, t, s), SLACK / 4, 0, at[0], at[-1])
                if worth(both(new, {}, {})[0]) < worth(both(seq, {}, {})[0]):
                    seq = new
    return worth(both(seq, {}, {})[0]), seq


def arrange(ops, pre, wake):
    n = len(ops)
    dur = [o["dur"] for o in ops]
    fwd, bwd = [[] for _ in ops], [[] for _ in ops]
    for i in range(n):
        for j, lag in [(j, dur[j] + (wake if ops[i]["q"] != ops[j]["q"] else 0.0 if ops[i]["q"] == "p" else SAME)) for j in pre[i]] + ops[i]["behind"]:
            fwd[j].append((i, lag))
            bwd[i].append((j, lag + dur[i] - dur[j]))

    def after(line, t):
        lo, hi = 0, len(line)
        while lo < hi:
            mid = (lo + hi) // 2
            if line[mid][1] <= t + 1e-9:
                lo = mid + 1
            else:
                hi = mid
        return lo

    def place(edges, back, key):
        left, est, start, busy = [len(b) for b in back], [0.0] * n, [0.0] * n, {}
        rank = {i: r for r, i in enumerate(sorted(range(n), key=key))}
        ready = [i for i in range(n) if not left[i]]
        while ready:
            i = min(ready, key=rank.get)
            ready.remove(i)
            t = est[i]
            if ops[i]["kind"] in ("run", "send"):
                q = ops[i]["q"]
                lines = [(q, 0.0)] + [(b + r, wake) for b in ops[i]["banks"] for r in "vsp" if r != q]
                moved = True
                while moved:
                    moved = False
                    for name, pad in lines:
                        line = busy.get(name, [])
                        lo = after(line, t - pad)
                        while lo < len(line) and line[lo][0] < t + dur[i] + pad:
                            t, moved = line[lo][1] + pad, True
                            lo += 1
                for name in [q] + [b + q for b in ops[i]["banks"]]:
                    line = busy.setdefault(name, [])
                    line.insert(after(line, t), (t, t + dur[i]))
            start[i] = t
            for k, lag in edges[i]:
                est[k] = max(est[k], t + lag)
                left[k] -= 1
                if not left[k]:
                    ready.append(k)
        return start

    late = [0.0] * n
    for i in range(n - 1, -1, -1):
        for j, lag in bwd[i]:
            late[j] = max(late[j], late[i] + lag)
    best, seed = None, 1
    for turn in range(PASSES + TRIES):
        bias = {}
        if turn >= PASSES:
            late = best[2]
            for i in range(n):
                if ops[i]["role"] not in bias:
                    seed = (seed * 1103515245 + 12345) % 2147483648
                    bias[ops[i]["role"]] = JOG * (seed % 2001 - 1000) / 1000 if seed >> 16 & 7 == 0 else 0.0
            start = place(fwd, bwd, lambda i: (bias[ops[i]["role"]] - late[i] - dur[i], i))
            late = place(bwd, fwd, lambda i: (-start[i] - dur[i], -i))
        start = place(fwd, bwd, lambda i: (-late[i] - dur[i], i))
        end = max(start[i] + dur[i] for i in range(n))
        if best is None or end < best[0]:
            best = (end, start, late)
        if turn < PASSES:
            late = place(bwd, fwd, lambda i: (-start[i] - dur[i], -i))
    ORDER["end"] = best[0]
    soft = set((j, i) for i in range(n) for j, lag in ops[i]["behind"] if ops[i]["kind"] == "run" and j not in pre[i] and "firm" not in ops[i])
    fwd = [[e for e in fwd[j] if (j, e[0]) not in soft] for j in range(n)]
    bwd = [[e for e in bwd[i] if (e[0], i) not in soft] for i in range(n)]
    start = best[1]
    best = better(ops, pre, sorted(range(n), key=lambda i: (start[i], i)))
    ORDER["end"] = best[0]
    seq, seen = best[1], {}
    for i in seq:
        for b in ops[i]["banks"]:
            pre[i] = pre[i] + [seen[b + r] for r in "vsp" if r != ops[i]["q"] and b + r in seen]
            seen[b + ops[i]["q"]] = i
    return seq


def record(T):
    ops, where, seen = [], {}, {}

    def put(kind, q, fn, r, w, dur, after=(), **more):
        d = {"kind": kind, "q": q, "fn": fn, "r": list(r), "w": list(w), "dur": dur, "after": list(after), "behind": []}
        d.update(more)
        if kind == "run" and q in "vs" and any(SCRATCH[x[0]][2] == "uint16" and x[4] in LISTS for x in r) and (w[0][4] not in LISTS or len(r) > 1):
            n = (dur - (0.05 if q == "v" else 0.065)) / CY
            d["each"] = (n / SC, 2) if r[-1][4] in ("pos", "pos2") else (n / G, 1)
        x = (w or r or [(kind, 0, 0, 1, kind)])[0]
        key = (q, (x[1] - PART[x[4]][1]) // 8 if x[4] in PART else x[1], x[4].rstrip("01234") if SCRATCH.get(x[0], "s")[0] != "psum" else x[4])
        seen[key] = seen.get(key, 0) + 1
        d["role"], d["round"] = key + (seen[key],), where.get("round", -1)
        ops.append(d)

    def join(k):
        first = ops[-k]
        for o in ops[len(ops) - k + 1:]:
            first["more"] = first.get("more", []) + [o["fn"]]
            first["r"] += [x for x in o["r"] if x not in first["r"]]
            first["w"] += [x for x in o["w"] if x not in first["w"]]
            first["dur"] += o["dur"]
        del ops[len(ops) - k + 1:]

    def mark(name):
        where[name] = len(ops) - 1

    def behind(name, lag=0.0):
        ops[-1]["behind"].append((where[name], lag))

    def ap(x):
        name, lo, hi, st = x[:4]
        if len(x) > 5:
            return T[name][(slice(None),) + tuple(slice(*i) if isinstance(i, tuple) else i for i in x[5])]
        return T[name][:, lo:hi:st] if st != 1 else T[name][:, lo:hi]

    def val(s):
        return ap(s) if isinstance(s, tuple) else s

    def two(*xs):
        return 0.5 if all(SCRATCH[x[0]][2] in ("bfloat16", "uint16", "float16") for x in xs) else 1.0

    def vd(n, k=1.0):
        return max(64.0, n * k) * CY + FIX

    def ts(o, a, s1, op0, s2=None, op1=None, by=None):
        r = [x for x in (a, s1, s2, by) if isinstance(x, tuple)]
        d = vd(width(a), two(o, a)) if by is None else 0.05 + width(o) * G * CY
        tail = (op0,) if op1 is None else (op0, op1)
        put("run", "v", lambda e: e.tensor_scalar(ap(o), ap(a) if by is None else ap(a).indirect(ap(by)), val(s1), val(s2), *tail), r, [o], d)

    def tt(o, a, b, op):
        k = 1.0 if "psum" in (SCRATCH[a[0]][0], SCRATCH[b[0]][0]) else 2.0
        put("run", "v", lambda e: e.tensor_tensor(ap(o), ap(a), ap(b), op), [a, b], [o], vd(width(a), k))

    def cp(o, a):
        put("run", "v", lambda e: e.tensor_copy(ap(o), ap(a)), [a], [o], vd(width(a), two(o, a)))

    def most(o, a):
        put("run", "v", lambda e: e.tensor_reduce(ap(o), ap(a), AxisListType.X, ALU.max), [a], [o], vd(width(a)))

    def ms(o, c):
        put("run", "v", lambda e: e.memset(ap(o), c), [], [o], vd(width(o), two(o)))

    def pick(o, win, off, b=None, op=None):
        r, d = [win, off] + ([b] if b is not None else []), 0.05 + width(o) * G * CY
        if b is None:
            put("run", "v", lambda e: e.tensor_copy(ap(o), ap(win).indirect(ap(off))), r, [o], d)
        else:
            put("run", "v", lambda e: e.tensor_tensor(ap(o), ap(win).indirect(ap(off)), ap(b), op), r, [o], d)

    def scatter(win, off, a, b=None):
        d = 0.05 + width(a) * SC * CY
        if b is None:
            put("run", "v", lambda e: e.tensor_copy(ap(win).indirect(ap(off)), ap(a)), [a, off], [win], d)
        else:
            put("run", "v", lambda e: e.tensor_tensor(ap(win).indirect(ap(off)), ap(a), ap(b), ALU.max), [a, b, off], [win], d)

    def scan(o, m, a, first=0.0, op=ALU.mult):
        put("run", "v", lambda e: e.tensor_tensor_scan(ap(o), ap(m), ap(a), first, op, ALU.max), [m, a], [o], vd(width(a), two(o, m, a)))

    def act(o, a, f, bias=0.0, scale=1.0, accum=None, by=None, also=()):
        r = [x for x in (a, scale, bias, by) if isinstance(x, tuple)] + list(also)
        d = vd(width(a)) + FIXS if by is None else 0.065 + width(o) * G * CY
        if accum is not None:
            put("run", "s", lambda e: e.activation(ap(o), ap(a), f, bias=bias, scale=scale, accum_out=ap(accum)), r, [o, accum], d + 0.02)
        else:
            put("run", "s", lambda e: e.activation(ap(o), ap(a) if by is None else ap(a).indirect(ap(by)), f, bias=val(bias), scale=val(scale)), r, [o], d)

    def mm(o, l, r, st, sp):
        if st:
            where[o[0]] = o
        put("run", "p", lambda e: e.matmul(ap(o), ap(l), ap(r), st, sp), [l, r], [where[o[0]] if sp else o], max(min(64, width(l)), width(r)) * CY * (4 if SCRATCH[l[0]][2] == "float32" else 1) + FIXP)

    def iota(o, pat, base, cm):
        d = 0.13 + 2 * width(o) * CY
        if SCRATCH[o[0]][2] != "int32":
            put("run", "g", lambda e: e.iota(ap(o), pat, base, cm, allow_small_or_imprecise_dtypes=True), [], [o], d)
        else:
            put("run", "g", lambda e: e.iota(ap(o), pat, base, cm), [], [o], d)

    def sift(o, a, pat, op, fill, base, cm):
        put("run", "g", lambda e: e.affine_select(ap(o), ap(a), pat, op, fill, base, cm), [a], [o], 0.17 + 2 * width(o) * CY)

    def gcp(o, a):
        sift(o, a, [[0, width(o)]], ALU.is_ge, 0.0, 0, 0)

    def load(q, o, a, sem, dur, lo=0, hi=None):
        put("dma", q, lambda e: e.dma_start(ap(o), T[a][:] if hi is None else T[a][:, lo:hi]), [], [o], dur, sem=sem, inc=16)

    def send(m, after=(), also=None):
        ms = [m, also] if also else [m]
        for x in ms:
            where[x] = len(ops)
        put("send", "g", None, [B(s, 0, MSG[x][2]) for x in ms for s in MSG[x][0]] + list(after), [], 3 * CALL if MSG[m][4] in "Tf" else CALL, msg=ms)

    def expect(m):
        put("land", None, None, [], [B(MSG[m][1], 0, MSG[m][2])], LAT[m[0]], [where[m]], msg=m)
        if m[0] in "ab" and m[2] == "1":
            ops[-1]["gap"] = where["land" + m[0]]
            behind("land" + m[0])
        mark("land" + m[0])

    def cls(name, c):
        return B(name, c, 1021 + c, 4)

    def half(x, h):
        return (x[0], x[1] + 16 * PARTS[h][0] * x[3], x[1] + (16 * PARTS[h][1] - 1) * x[3] + 1) + x[3:]

    def vals(name, h):
        k0, k1 = PARTS[h][:2]
        return B(name, 16 * k0 + 16, 16 * k1 + 16), B(name, 272, 272 + k1 - k0) if h else B(name, 16 - k1, 16)

    def slide(name, p):
        return B(name, 15 - p, 143 - p)

    cut = 64 * PARTS[0][1]
    load("y", B("entx", 0, cut), "ent", "ld0", 3.4, 0, cut)
    mark("load")
    ms(B("fx0", 0, 16), 0.0)
    ms(B("fx0", 2048, 2064), 0.0)
    load("s", B("wti"), "wt", "ld4", 2.2)
    load("s", B("kpi"), "kap", "ld5", 2.2)
    load("y", B("fx0", 1, 2049), "feat", "ld6", 5.4)
    behind("load")
    mark("load")
    load("y", B("entx", cut), "ent", "ld1", 6.4, cut, 1024)
    behind("load")
    cp(B("fx0", 2056, 2057), B("wti"))
    cp(B("fx0", 2057, 2058), B("kpi"))
    ms(B("one"), 1.0)
    ms(B("mid"), -2047.5)
    iota(B("ci"), [[37, 64]], 0, 0)
    iota(B("pmi"), [[0, 16]], 0, 1)
    iota(B("x16"), [[1, 16]], 0, 0)
    sift(B("blka"), B("one"), [[-16, 8], [0, 16]], ALU.is_ge, 0.0, 0, 1)
    sift(B("blk"), B("blka"), [[16, 8], [0, 16]], ALU.is_ge, 0.0, 15, -1)
    sift(B("idb"), B("one"), [[-1, 128]], ALU.is_equal, 0.0, 0, 1)
    ms(B("zw"), 0.0)
    ms(B("zer"), 0.0)
    ms(B("allf"), 16.0)
    ms(B("wacc", 2, 3), 16.0 + 31.0 / 128)
    ms(B("sgm"), 1.0)
    cp(B("sgm", 0, 497, 16), B("zer", 0, 32))
    ts(B("ci"), B("ci"), 63, ALU.bitwise_and)
    ts(B("Ct", 0, 64), B("ci"), 4096.0, ALU.mult, 262144.0 - 2048.0, ALU.add)
    for n in (64, 128, 256, 512):
        act(B("Ct", n, 2 * n), B("Ct", 0, n), AF.Copy)
    ts(B("pmj"), B("pmi"), 15, ALU.bitwise_and)
    cp(B("pmf"), B("pmj"))
    pm = B("pmf", 0, 1)
    ts(B("lI"), B("x16"), 16.0, ALU.mult, pm, ALU.add)
    cp(B("lstI"), B("lI"))
    ts(B("lstR"), B("lI", 0, 8), -3.5, ALU.add, 0.125, ALU.mult)
    for h, (k0, k1, path) in enumerate(PARTS):
        nk = k1 - k0
        ts(B("jd", k0, k1), B("lI", 0, nk), (1 - nk) / 2, ALU.add, 1 / nk, ALU.mult)
        ts(B("lpf", k0, k1), B("jd", k0, k1), (1 - 16 * nk) / 16, ALU.mult)
        tt(B("lpf", k0, k1), B("lpf", k0, k1), B("lI", 0, nk), ALU.add)
        ts(B("lstP", k0, k1), B("lpf", k0, k1), 16.0, ALU.mult)
        ts(B("lst8", 2 * h, 2 * h + 1), pm, nk - 1.0, ALU.min)
        ts(B("lst8", 4 + 2 * h, 5 + 2 * h), pm, *((nk - 1.0, ALU.min) if h else (nk - 16.0, ALU.add)))
    ts(B("jd", 0, 1), B("pmj", 0, 1), 1, ALU.bitwise_and)
    for k0, k1, path in PARTS:
        ts(B("lpq", 0, 1), B("jd", 0, 1), 7.5 * (k1 - k0), ALU.mult)
        ts(B("lpq", 1, 2), pm, (k1 - k0) / 2, ALU.mult, B("lpq", 0, 1), ALU.add)
        ts(B("lstQ", k0, k1), B("x16", 0, k1 - k0), B("lpq", 1, 2), ALU.add)
    ts(B("cap"), B("lI"), -1.0, ALU.mult, FAR, ALU.add)
    ms(B("lab"), 4 * BIG)
    ts(B("lab", 0, 241, 16), B("lI"), -1.0, ALU.mult)
    ts(B("dlt"), B("x16"), pm, ALU.is_equal)
    for t in range(NR):
        ms(B("old%d" % t, 272, 288), 0.0)
        ms(B("la%d" % t, 0, 16 - PARTS[0][1]), 0.0)
    for h, (k0, k1, path) in enumerate(PARTS):
        for j in range(272, 272 + k1 - k0) if h else range(16 - k1, 16):
            act(B("YP", j, 8 * 288, 288), B("one", 0, 8), AF.Copy, scale=-4096.0)
            ops[-1]["w"] = [B(n + str(t), j, j + 1) for n in ("ta", "aP") for t in range(NR)]
    iota(B("rA"), [[0, 8], [-1024, 8], [-8192, 2]], 15360, 0)
    act(B("idf"), B("idb"), AF.Copy)
    used = "".join(FL)
    for n, s, need in (("idn", -1.0, 1), ("idk", 1 / PEN, 1), ("idw", 6.0, FAST), ("idx", 16.0, len(FAST) < 2), ("hid", 1.5 * (1 << 22), 1), ("idp", PEN, "s" in used),
                       ("hi2", 3.0 * (1 << 22), "k" in used or "p" in used), ("ix2", 32.0, "k" in used), ("iw2", 12.0, "k" in used)):
        if need:
            act(B(n), B("idb"), AF.Copy, scale=s)
    act(B("b8n"), B("blk", 0, 113, 16), AF.Copy, scale=-1.0)
    sift(B("prm"), B("one", 0, 64), [[-2, 8], [-16, 8]], ALU.is_ge, 0.0, 0, 1)
    sift(B("prm"), B("prm"), [[2, 8], [16, 8]], ALU.is_ge, 0.0, 1, -1)
    ts(B("jd", 0, 1), B("pmi", 0, 1), 1, ALU.bitwise_and)
    cp(B("msk", 1, 2), B("jd", 0, 1))
    ts(B("msk", 0, 1), B("jd", 0, 1), -1.0, ALU.mult, 1.0, ALU.add)
    for r in RUNS:
        a, b = [8192.0 if x == "S" else 16384.0 for x in r]
        if a != b:
            ts(B("rsc"), B("pmi", 0, 1), 63.5, ALU.is_gt, b - a, ALU.mult)
            ts(B("rsc"), B("rsc"), a, ALU.add)
        act(B("prm" + r), B("prm"), AF.Copy, scale=a if a == b else B("rsc"))
    for path in PATHS:
        for r in range(2):
            a, b = [0.0 if x == "V" else 16.0 for x in path[2 * r:2 * r + 2]]
            if a == b:
                ms(B("nil" + path, 64 * r, 64 * r + 64), a)
            else:
                ts(B("rsc"), B("pmi", 0, 1), 63.5, ALU.is_gt, b - a, ALU.mult)
                ts(B("nil" + path, 64 * r, 64 * r + 64), B("one", 0, 64), B("rsc"), ALU.mult, a, ALU.add)
    for k0, k1, path in PARTS:
        for c in range(4):
            if path[c] != "V" and path[c ^ 1] == "V":
                ms(B("NM2", 256 * k0 + 512 * c, 256 * k0 + 512 * c + 512), 0.0)
    cp(B("idh"), B("idb"))
    ts(B("cmk"), B("x16"), pm, ALU.is_gt, 1.0, ALU.add)
    scan(B("pw"), B("cmk"), B("zer", 0, 16), 2048.0)
    act(B("blw"), B("blk"), AF.Copy, scale=B("pw", 15, 16))
    act(B("blx"), B("blk"), AF.Copy, scale=8 * BIG)
    sift(B("x128"), B("one"), [[0, 8], [-1, 16]], ALU.is_equal, 0.0, 0, 1)
    mm(B("pcp", 0, 128), B("x128"), B("x128"), True, True)
    ts(B("t128"), B("pw", 15, 16), -2.0, ALU.mult, BIG * 4096, ALU.add)
    act(B("thr"), B("pcp", 0, 128), AF.Identity, scale=B("t128"), bias=-BIG * 4096)

    def convert(o, x, w, at=0):
        n1, w = B("n1", at, at + width(x)), B(w, 0, width(x))
        ts(n1, x, 2.0 ** -11, ALU.mult, 0.5 - 2.0 ** -12, ALU.add)
        ts(w, n1, 2048.0, ALU.mult, 15.0, ALU.add)
        tt(o, w, x, ALU.add)

    def convert2(o, x, w, at):
        r, w = B("d1" if SCRATCH[x[0]][2] == "int32" else "d2", at, at + width(x)), B(w, 0, width(x))
        ts(r, x, 1023.5, ALU.add, C4096 / 2, ALU.add)
        act(r, r, AF.Identity, bias=-C4096 / 2)
        act(w, r, AF.Identity, bias=15.0)
        tt(o, w, x, ALU.add)
    for h in range(2):
        gcp(half(B("sA"), h), half(cls("entx", 0), h))
        ts(half(B("q"), h), half(cls("entx", 0), h), 15.0, ALU.add)
        ts(half(B("n1"), h), half(cls("entx", 0), h), 2.0 ** -11, ALU.mult, 0.5 - 2.0 ** -12, ALU.add)
        ts(half(B("k1"), h), half(B("q"), h), 16, ALU.bitwise_and)
        tt(half(B("pr"), h), half(B("n1"), h), half(B("k1"), h), ALU.mult)
        send("A%d" % h)
    iota(B("iot"), [[1, 1024]], 0, 0)
    behind("A1")
    ops[-1]["firm"] = True

    def decode(o, a, w, k):
        d1, d2 = B("d1", k, k + width(a)), B("d2", k, k + width(a))
        act(d1, a, AF.Identity, bias=C1, scale=2.0 ** -12)
        act(w, d1, AF.Identity, bias=2048.0 * C1, scale=-2048.0)
        tt(d2, w, a, ALU.add)
        act(o, d2, AF.Relu, bias=-15.0)

    def complete(t, name):
        la, lb, old, c = "la%d" % (t - 1), "lb%d" % (t - 1), "old%d" % (t - 1), t - 1
        for h in range(2):
            gcp(vals(old, h)[0], half(cls(name, c), h))
        for h, (k0, k1, path) in enumerate(PARTS):
            lo, hi = 16, 16 * k1 + 16
            expect("a%d%d" % (c, h))
            ts(B("sel", k0, k1), vals(la, h)[1], -1.0, ALU.mult, FAR, ALU.add)
            act(half(cls(name, c), h), B("win%d" % c, lo, hi + int(FAR)), AF.Copy, by=B("sel", k0, k1),
                also=[B(la, 0, hi), B(GAP[c]), B(old, lo)])
        for h, (k0, k1, path) in enumerate(PARTS):
            expect("b%d%d" % (c, h))
            cp(B("pos2", k0, k1), vals(lb, h)[1])
        scatter(B(name), B("pos2"), B(lb, 16, 272))
        mark("whole")

    mm(B("ctp"), B("idf"), cls("Ct", 0), True, True)
    for t in range(NR):
        last = t == NR - 1
        seen.clear()
        where["round"] = t
        LB = "LB%d" % ((t + 1) % 2)
        A, fx, TB, U = cls("LB%d" % (t % 2), t) if t else B("sA"), "fx%d" % (t if t > 1 else 0), "TB%d" % t, "uk" if t else "sU"
        tau, clock = 5.0 + t, 12.0 + t
        if t > 1:
            expect("f%d" % t)
        if t != 1:
            act(B("wk"), B(fx, 2056, 2058), AF.Copy)
            if t:
                behind("scatter")
            act(B("zw", 15, 128, 16), B("blk", 0, 113, 16), AF.Copy, scale=B("wk", 0, 1))
            act(B("rK"), B("dlt"), AF.Copy, scale=B("wk", 1, 2))
            mm(B("kmp"), B("blk"), B("rK"), True, True)
        act(B(U, 0, 16), B("kmp"), AF.Identity, scale=16.0, bias=2047.5)
        if t:
            expect("c%d" % (t - 1))
        for h, (k0, k1, path) in enumerate(PARTS):
            lo, hi, nk = 16 * k0, 16 * k1, k1 - k0
            if t:
                tt(B("q", lo, hi), B("ctp", lo, hi), half(A, h), ALU.add)
                act(B("a75", lo, hi), half(A, h), AF.Identity, bias=-7.5)
                ts(B("k1", lo, hi), B("q", lo, hi), 16, ALU.bitwise_and)
                tt(B("pr", lo, hi), B("a75", lo, hi), B("k1", lo, hi), ALU.mult)
            ts(B("off", lo, hi), B("pr", lo, hi), 2.0 ** (-16 if t else -4), ALU.mult, 127.0 / 256 if t else 0.0, ALU.add, by=B("lstP", k0, k1))
            mm(B("w3%d" % h, 0, nk), B("idf"), B("mid"), True, False)
            for c in range(k0 // 2, k1 // 2):
                o, l = B("Yg", 512 * c, 512 * c + 512), B("off", 32 * c, 32 * c + 32)
                if c in (FV if t else FV0):
                    pick(o, B(fx, 0, 2049), l)
                else:
                    act(o, B(fx, 0, 2049), AF.Copy, by=l)
                mark("look%d" % c)
                if h and HF and ops[-1]["q"] == "v":
                    behind("scan")
                    ops[-1]["firm"] = True
                if h and not t and UF > 1 and ops[-1]["q"] == "v":
                    behind("ub")
                    ops[-1]["firm"] = True
                scan(B("Ys", 512 * c, 512 * c + 512), B("sgm"), o)
                if h and HF > 1:
                    behind("scan")
                    ops[-1]["firm"] = True
                if not h:
                    mark("scan")
                for p in range(32 * (c - k0 // 2) // nk, 32 * (c + 1 - k0 // 2) // nk):
                    mm(B("w3%d" % h, 0, nk), slide("zw", p), B("Ys", 16 * (lo + nk * p) + 15, 16 * (lo + nk * p + nk), 16), False, p == 15)
                join(32 * (c + 1 - k0 // 2) // nk - 32 * (c - k0 // 2) // nk)
            ts(B("uq", k0, k1), B("w3%d" % h, 0, nk), C4096, ALU.add, C4096, ALU.subtract)
            if h:
                behind("sum", AHEAD[4])
            mark("sum")
            tt(B(U, 16 + k0, 16 + k1), B("w3%d" % h, 0, nk), B("uq", k0, k1), ALU.subtract)
            mark("ub")
            if not t:
                send("U%d" % h)
        if not t:
            for h in range(2):
                expect("A%d" % h)
                convert2(half(B("lA"), h), half(B("lR"), h), "tb%d" % h, 128 * h)
            A, U = B("lA"), "lU"
            for h in range(2):
                tt(half(B("q"), h), half(B("ctp"), h), half(A, h), ALU.add)
                act(half(B("a75"), h), half(A, h), AF.Identity, bias=-7.5)
        for h, (k0, k1, path) in enumerate(PARTS):
            act(half(B("x1"), h), half(B("a75"), h), AF.Identity, bias=C16)
            act(half(B("oc"), h), half(B("x1"), h), AF.Identity, bias=-C16)
            n, reps = 16 * (k1 - k0), 16 // len(path)
            first = 1 if t or h in OD else reps
            for j in range(first):
                act(B("oT", 768 * h + n * j, 768 * h + n * j + n), B("oc", 16 * k0, 16 * k1), AF.Identity, bias=7.5)
            n, reps = n * first, reps // first
            for j in range(1, reps):
                o, a = B("oT", 768 * h + n * j, 768 * h + n * j + n), B("oT", 768 * h, 768 * h + n)
                put("dma", "y", lambda e, o=o, a=a: e.dma_start(ap(o), ap(a)), [a], [o], 2.2, sem="oc%d" % (2 * t + h), inc=16 * (reps - 1))
                mark("own")
                mark("own%d" % h)

        def total(o, *terms):
            for j, (l, r) in enumerate(terms):
                mm(o, B(l), r, j == 0, j == len(terms) - 1)

        def out(name, h):
            return vals(name + str(t), h)[0]
        aP = [half(B("fa"), h) if last else out("aP", h) for h in range(2)]
        cut = -9.5
        for k0, k1 in [x[:2] for x in PARTS] if LS else [(0, 16)]:
            lo, hi, each = 16 * k0, 16 * k1, B("lstI", 0, k1 - k0)
            mine = (A[0], A[1] + lo * A[3], A[1] + (hi - 1) * A[3] + 1) + A[3:]

            def H(n):
                return B(n, lo, hi)
            ts(H("za"), H("q"), 0x3801F, ALU.bitwise_and)
            ts(H("l5a"), H("q"), 31, ALU.bitwise_and)
            l5a, za = H("l5a"), H("za")
            if GI:
                l5a, za, each = H("l5g"), H("zag"), None
                gcp(za, H("za"))
                gcp(l5a, H("l5a"))
            act(H("spa"), l5a, AF.Relu, bias=(tau + 1) * PEN, scale=-PEN, by=each)
            act(H("kpa"), za, AF.Relu, bias=(tau + 1) * PEN, scale=-PEN, by=each)
            act(H("k1a"), H("kpa"), AF.Sign)
            total(H("w1"), ("idb", H("kpa")), ("idn", H("spa")), ("idf", mine))
            total(H("sp2"), ("idf", mine), ("idn", H("spa")))
            act(H("aw"), H("sp2"), AF.Relu)
            if last:
                decode(H("fy"), H("aw"), H("sp2"), 256 + lo)
            for h in range(2):
                if k0 <= PARTS[h][0] < k1:
                    act(aP[h], half(B("w1"), h), AF.Relu)
                    if last:
                        decode(out("aP", h), aP[h], half(B("ctp"), h), 16 * PARTS[h][0])
            act(H("ca"), H("w1"), AF.Relu, bias=-15.5 * 16384, scale=16384.0)
            if not k0:
                mark("lanes")
            act(H("iap"), l5a, AF.Relu, bias=31 * BIG, scale=-2 * BIG, by=each)
        if not last:
            mm(B("ctp"), B("idf"), cls("Ct", t + 1), True, True)
        if t:
            expect("T%d" % t)
            complete(t, TB)
        else:
            for c in range(4):
                (convert2 if c in CS else convert)(B(TB, 256 * c, 256 * c + 256), B("entx", 256 * c, 256 * c + 256), ("big0", "big1", "spare", "pcp")[c], 256 * c)
            for h in range(2):
                expect("U%d" % h)
        send("T%d" % (t + 1), [B("oT", 0, 512), B("oT", 768, 1280)] + ([] if t else [B("lU", 0, 32)]))
        if TC:
            tc, tn = B("TC%d" % (t % 2)), B("TC%d" % (1 - t % 2))
            if not t:
                put("dma", "y", lambda e, o=tc: e.dma_start(ap(o), ap(B("Ct"))), [B("Ct")], [tc], 3.0, sem="tc0", inc=16)
                behind("own0")
            put("dma", "g", lambda e, o=tc, a=B(TB, 0, 1024): e.dma_start(ap(o), ap(a), accum_op=ALU.add), [B(TB, 0, 1024), tc], [tc], 6.5,
                sem="td%d" % t, inc=16, hold=1.2)
            if TF:
                behind("T%d" % (t + 1))
            else:
                ops[where["T%d" % (t + 1)]]["behind"].append((len(ops) - 1, 0.0))
            mark("T%d+" % (t + 1))
            if not last:
                put("dma", "y", lambda e, o=tn: e.dma_start(ap(o), ap(B("Ct"))), [B("Ct"), tc], [tn], 3.0, sem="tc%d" % (t + 1), inc=16)
        if t + 2 < NR:
            send("f%d" % (t + 2))
            behind("T%d%s" % (t + 1, "+" * TC))
            behind("T%d" % (t + 1))
        if not last:
            gcp(cls(LB, t + 1), cls(TB, t + 1))
        act(B("ksq"), B(U, 0, 16), AF.Square, bias=-2047.5, by=B("lstR"))
        if t:
            ts(B("ksq"), B("ksq"), B("lc%d" % (t - 1), 0, 1), ALU.add, B("lc%d" % (t - 1), 1, 2), ALU.subtract)
        RT = B(TB, 0, 1024)

        for h, (k0, k1, path) in enumerate(PARTS):
            lo, hi, nk = 16 * k0, 16 * k1, k1 - k0
            cw = 16 * nk // len(path)

            def H(n):
                return B(n, lo, hi)

            def ch(n, c, more=1):
                return B(n, 16 * (lo + cw * c), 16 * (lo + cw * (c + more)))
            for k in range(k0, k1):
                act(B("ep%d" % h, k - k0, hi - lo, nk), B(U, 0, 16), AF.Square, bias=B(U, 16 + k, 17 + k))
                if (k - k0) % JE == JE - 1:
                    join(JE)
            if t and not h:
                for c in HB:
                    ops[where["look%d" % c]]["behind"].append((len(ops) - 1, 0.0))
                    ops[where["look%d" % c]]["firm"] = True
            tt(H("ei"), B("ep%d" % h), B("ksq"), ALU.subtract)
            ts(H("em"), H("ei"), 5, ALU.logical_shift_right, 1023, ALU.bitwise_and)
            cp(H("eu"), H("em"))
            if t and not h and HS:
                ops[where["whole"]]["behind"].append((len(ops) - HS, 0.0))
                ops[where["whole"]]["firm"] = True
            mc = 16 // len(path)
            if h in EH:
                pick(H("eh"), H("em"), B("lstQ", k0, k1))
            else:
                act(H("ef"), H("em"), AF.Copy, by=B("lstQ", k0, k1))
            own = B("oT", 768 * h, 768 * h + 16 * cw)
            for c in range(len(path)):
                l = B("eu", lo + cw * c, lo + cw * c + cw)
                pick(ch("Xb" if path[c] == "V" else "D", c), RT, l, own, ALU.subtract)
                if PICKS is None:
                    if h or c:
                        behind("pick")
                    mark("pick")
                else:
                    mark("pick%d" % (4 * h + c))
                    if 4 * h + c == 7:
                        for i, j in zip(PICKS, PICKS[1:]):
                            ops[where["pick%d" % j]]["behind"].append((where["pick%d" % i], 0.0))
                pair = WIDE and path[c] == path[c ^ 1] and (h or c > 1 or WIDE > 1)
                if pair and c % 2 == 0:
                    continue
                c0, n = (c - 1, 2) if pair else (c, 1)
                if path[c] != "V":
                    act(ch("D" if path[c] == "S" else "Xb", c0, n), ch("D", c0, n), AF.Abs)
                    if h or c0:
                        behind("sign")
                if path[c] == "S":
                    act(ch("D", c0, n), ch("D", c0, n), AF.Abs, bias=-1032.25)
                    act(ch("NM", c0, n), ch("D", c0, n), AF.Sign, bias=-1024.0)
                    mark("sign")
                elif path[c] == "M":
                    mark("sign")
                    ts(ch("Xb", c0, n), ch("Xb", c0, n), 3000.0, ALU.min, 262144.0 + 1016.0, ALU.add)
                    act(ch("NM", c0, n), ch("Xb", c0, n), AF.Square, bias=-129.0, scale=2.0 ** -11)
                else:
                    for name, cc in (("NM", C16), ("NM2", C4096)):
                        ts(ch(name, c0, n), ch("Xb", c0, n), cc, ALU.add, cc, ALU.is_equal)
                    if VFIRST > 1:
                        mark("pick")
            key, kt, todo = "key%d" % h, "kt%d" % h, []
            mm(B(key, 0, 16 * nk), B("idb"), B("rA"), True, False)
            mm(B(key, 0, 16 * nk), B("idh" if h in EH else "idf"), H("eh" if h in EH else "ef"), False, False)
            mm(B(kt), B("idb"), B("nil" + path), True, False)
            for r in sorted(range(2), key=lambda r: VFIRST and path[2 * r] != "V"):
                at = 16 * lo + 1024 * r
                for src, z in [("NM", B("b8n"))] + [("NM2", B("blk", 0, 113, 16))] * ("V" in path[2 * r:2 * r + 2]):
                    todo.append([(B(kt, 64 * r + p, 64 * r + 64, 8), B(src, at + p, at + 1024, 8), z) for p in range(8)])
            todo = [x for j in SUMS[h] if j < len(todo) for x in todo[j]]
            for i, (o, l, r) in enumerate(todo):
                mm(o, l, r, False, i == len(todo) - 1)
                if i % JP == JP - 1:
                    join(JP)
            for pp in range(2):
                o = ("KT", 0, 1, 1, "KT.%d.%d." % (h, pp), ((16 * h, 16 * h + 16), pp, (0, 8)))
                if KC[h][pp] == "s":
                    act(o, B(kt), AF.Copy, scale=B("msk", pp, pp + 1))
                else:
                    ts(o, B(kt), B("msk", pp, pp + 1), ALU.mult)
            for r in range(2):
                a = 16 * h + 8 * r
                mm(B(key, r, 16 * nk, 2), ("KT", 0, 1, 1, "KT.%d.0." % h, ((a, a + 8), (0, 2), (0, 8))), B("prm" + path[2 * r:2 * r + 2]), False, r == 1)
                ops[-1]["r"].append(("KT", 0, 1, 1, "KT.%d.1." % h))
            ky, er = [B(n, 16 * h, 16 * h + nk) for n in ("ky", "er")]
            scan(H("kx" if KI else "kv"), B("sgm", 0, hi - lo), B(key, 0, 16 * nk))
            behind("keys" if h else "lanes", AHEAD[0 if h else 2])
            mark("keys")
            if KI:
                ky = B("kx", lo + 15, hi, 16)
            else:
                cp(ky, B("kv", lo + 15, hi, 16))
            ts(er, ky, 1023, ALU.bitwise_and)
            cp(B("e16", k0, k1), er)
            erf, z = vals("xb%d" % t, h)[1], vals("Y%d" % t, h)[1]
            act(B("xb%d" % t, 272 * h, 272 * h + 16), er, AF.Copy, by=B("lst8", 4 + 2 * h, 5 + 2 * h))
            e = B("e16", k0, k1)
            if h in EX:
                act(H("ebx"), B("iot"), AF.Exp, scale=0.01, by=e)
            else:
                pick(H("ebc"), B("iot"), e)
            if 1 in EX or h in EX:
                act(B("erx", 16 * h, 16 * h + 16), er, AF.Exp, scale=0.01, by=B("lst8", 2 * h, 2 * h + 1))
            mm(H("pcp"), B("idb"), B("thr", 0, hi - lo), True, False)
            for k in range(k1):
                a, at = max(16 * k, lo), 16 * k if k >= k0 else 0
                j = 16 - PARTS[0][1] + k if k < PARTS[0][1] else 272 + k - k0
                s = B("xb%d" % t, j, j + 1)
                if h in EX:
                    j = k if k < PARTS[0][1] else 16 + k - k0
                    s = B("erx", j, j + 1)
                ts(rows(k, k + 1, a - at, hi - at), B("ebx" if h in EX else "ebc", a, hi), s, ALU.is_equal)
                a = max(16 * k + 16, lo)
                if a < hi:
                    mm(B("pcp", a, hi), B("blx"), rows(k, k + 1, a - at, hi - at), False, False)
                if not ROWS and k >= k0:
                    mm(B("pcp", 16 * k, 16 * k + 16), B("blw"), rows(k, k + 1, 0, 16), False, k == k1 - 1)
            if ROWS:
                mm(H("pcp"), B("blw"), rows(k0, k1, 0, 16), False, True)
            scan(H("sv"), H("lab"), H("pcp"), 0.0, ALU.min)
            sv = B("sv", lo + 15, hi, 16)
            act(B("fl", k0, k1), sv, AF.Sign, bias=-600.0, accum=B("wacc", h, h + 1))
            tt(z, sv, B("cap", k0, k1), ALU.min)
            w3, p2, ns, wx, dq = [B(n + str(h)) for n in ("w3", "p2", "ns", "wx", "dq")]
            act(H("bF"), RT, AF.Copy, by=e)
            if TC and h in TCP:
                pick(H("qb"), tc, e)
            else:
                pick(H("qb"), B("Ct"), e, H("bF"), ALU.add)
            ts(H("zb"), H("qb"), 0x3801F, ALU.bitwise_and)
            ts(H("l5b"), H("qb"), 31, ALU.bitwise_and)
            each = B("lstI", 0, nk)
            hk, hp, xk, wk, ns_, ks_ = "hid", "hid", "idx", "idw", "idn", "idk"
            if "k" in FL[h]:
                ts(H("k1b"), H("zb"), tau + 0.5, ALU.is_lt, 0.5, ALU.subtract)
                hk, xk, wk = "hi2", "ix2", "iw2"
            else:
                act(H("k1b"), H("zb"), AF.Sign, bias=tau + 0.5, scale=-1.0, by=each)
            if "p" in FL[h]:
                ts(H("kpb"), H("l5b"), tau + 0.5, ALU.is_gt, 0.5, ALU.subtract)
                hp = "hi2"
            else:
                act(H("kpb"), H("l5b"), AF.Sign, bias=-tau - 0.5, by=each)
            if "s" in FL[h]:
                ts(H("spb"), H("l5b"), tau + 1, ALU.subtract, 0.0, ALU.min)
                ns_, ks_ = "idp", "idn"
            else:
                act(H("spb"), H("l5b"), AF.Relu, bias=(tau + 1) * PEN, scale=-PEN, by=each)
            if "i" in FL[h]:
                ts(H("ibp"), H("l5b"), 15.5, ALU.is_lt, PEN, ALU.mult)
            else:
                act(H("ibp"), H("l5b"), AF.Relu, bias=31 * BIG, scale=-2 * BIG, by=each)
            if h in FAST:
                xb, Y, ta = [out(n, h) for n in ("xb", "Y", "ta")]
                sa, sb, wx, bo = B("dq%d" % h, 0, hi - lo), H("sp2"), H("a75"), H("bF")
                tt(H("d0"), bo, H("w1"), ALU.subtract)
                act(H("cb"), bo, AF.Sign, bias=-15.5)
                if last:
                    bo = H("fb")
                    decode(bo, H("bF"), sb, 512 + lo)
                total(w3, (hp, H("kpb")), (hk, H("k1b")))
                total(sa, ("idk", H("kpa")), ("idw", H("k1a")), ("idf", out("aP", h)), ("idn", H("ibp")))
                total(sb, ("idn", H("iap")), ("idf", bo), (wk, H("k1b")), (ks_, H("spb")))
                total(wx, ("hid", H("cb")), (hp, H("kpb")), (hk, H("k1b")))
                total(p2, ("idn", H("ca")), (ns_, H("spb")))
                tt(H("dp"), H("d0"), w3, ALU.add)
                ts(ns, H("dp"), C4096, ALU.add, C4096, ALU.is_equal)
                tt(H("bt"), bo, w3, ALU.add)
                act(wx, wx, AF.Relu, scale=2.0)
                tt(wx, H("fy" if last else "aw"), wx, ALU.subtract)
                tt(xb, H("bt"), wx, ALU.max)
                tt(ta, bo, p2, ALU.add)
                tt(H("X"), out("aP", h), sa, ALU.max)
                tt(sb, H("bt"), sb, ALU.max)
                tt(H("X"), H("X"), sb, ALU.max)
                tt(Y, H("X"), ns, ALU.mult)
            else:
                total(w3, (hp, H("kpb")), (hk, H("k1b")))
                xb, Y, ta = [out(n, h) for n in ("xb", "Y", "ta")]
                bo, wo = H("bF"), w3
                if last:
                    bo, wo = H("fb"), H("sp2")
                    decode(bo, H("bF"), wo, 512 + lo)
                    tt(wo, bo, w3, ALU.add)
                tt(w3, H("bF"), w3, ALU.add)
                total(p2, ("idn", H("ca")), (ns_, H("spb")))
                tt(ta, bo, p2, ALU.add)
                tt(H("dp"), w3, aP[h], ALU.subtract)
                if h in WXP:
                    act(H("cb"), H("bF"), AF.Sign, bias=-15.5)
                    total(wx, ("hid", H("cb")), (hp, H("kpb")), (hk, H("k1b")))
                    act(wx, wx, AF.Relu, scale=2.0)
                else:
                    act(wx, w3, AF.Relu, bias=-15.5 * 16384, scale=16384.0)
                X = H("X")
                if h in XP:
                    X, ns = H("w1"), H("d0")
                if h in SAMEV:
                    ts(ns, H("dp"), C4096, ALU.add, C4096, ALU.is_equal)
                else:
                    act(H("dp"), H("dp"), AF.Abs)
                    act(ns, H("dp"), AF.Relu, bias=-2047.5 * BIG, scale=BIG)
                dla, dlb = B("dl", 2 * lo, lo + hi), B("dl", lo + hi, 2 * hi)
                dqa, dqb = B("dq%d" % h, 0, hi - lo), B("dq%d" % h, hi - lo)
                total(dqa, ("idk", H("kpa")), ("idx", H("k1a")), ("idn", H("ibp")))
                total(dqb, ("idn", H("iap")), (ks_, H("spb")), (xk, H("k1b")))
                act(B("dl", 2 * lo, 2 * hi), dq, AF.Relu, bias=-10.0)
                tt(H("tb"), H("fy" if last else "aw"), wx, ALU.subtract)
                wa = H("w1")
                tt(wa, out("aP", h) if last else wa, dla, ALU.add)
                tt(H("bt"), wo, dlb, ALU.add)
                tt(X, wa, H("bt"), ALU.max)
                tt(xb, wo, H("tb"), ALU.max)
                tt(Y, X, ns, ALU.mult if h in SAMEV else ALU.subtract)
            if h:
                behind("met", AHEAD[1])
            mark("met")
            send("a%d%d" % (t, h), also="b%d%d" % (t, h))
            if h:
                behind("a%d0" % t, AHEAD[3])
            if not last:
                tt(B("erf", k0, k1), z, erf, ALU.max)
                cp(B("pos", k0, k1), B("erf", k0, k1))
                scatter(B(LB), B("pos", k0, k1), xb, Y)
                if h:
                    behind("scatter", AHEAD[3])
                mark("scatter")
        if not last:
            for h in (2, 0, 1):
                mm(B("cnt"), B("allf"), B("wacc", h, h + 1), h == 2, h == 1)
            ts(B("sc%d" % t, 0, 1), B("cnt"), -496.0, ALU.add)
            ts(B("sc%d" % t, 1, 2), B("cnt"), C4096 / 4, ALU.add, C4096 / 4, ALU.subtract)
            send("c%d" % t)

    expect("T%d" % NR)
    for c in range(4):
        decode(B("yo", 256 * c, 256 * c + 256), B("TB4", 256 * c, 256 * c + 256), B(("spare", "ctp")[c % 2]), 256 * c)
    complete(NR, "yo")
    put("dma", "y", lambda e: e.dma_start(T.yent[:], ap(B("yo", 0, 1024))), [B("yo")], [], 4.5, sem="st", inc=16)
    return ops


ORDER = {}


def plan(T):
    if "o" not in ORDER:
        ops = record(T)
        pre = links(ops)
        seq = arrange(ops, pre, WAKE)
        ORDER["o"] = (pre, seq, [m for i in seq if ops[i]["kind"] == "send" for m in ops[i]["msg"]])
    return ORDER["o"]


def rank_program(g, core, T, topo):
    rank = T.rank_of(core)
    if rank is None:
        hand_on(g, core, T, topo)
        return
    n = len(T.cores)
    ops = record(T)
    pre, seq, _ = plan(T)
    eng = {"v": g.vector, "s": g.scalar, "p": g.tensor, "g": g, "y": g.sync}
    cnt = {"v": 0, "s": 0, "p": 0, "g": 0}
    known, snaps, tok, sent = {q: {} for q in eng}, {}, {}, 0
    for i in seq:
        o = ops[i]
        q = o["q"]
        if o["kind"] == "land":
            m = o["msg"]
            src = T.cores[(rank - MSG[m][3]) % n]
            tok[i] = (m, sum(bits(share(topo, T, ((src,) + chain)[-1], core, m)) for chain, lo, hi in route(topo, T, src, core, m)))
            continue
        need = {}
        for j in pre[i]:
            if ops[j]["kind"] != "send" and not (q == "p" and ops[j]["q"] == "p"):
                need[tok[j][0]] = max(need.get(tok[j][0], 0), tok[j][1])
        for s in sorted(need):
            if known[q].get(s, 0) < need[s]:
                eng[q].wait_ge(T.sem[s], need[s])
                known[q][s] = need[s]
                for s2, v2 in snaps.get((s, need[s]), {}).items():
                    known[q][s2] = max(known[q].get(s2, 0), v2)
        if o["kind"] == "run":
            for fn in [o["fn"]] + o.get("more", []):
                cnt[q] += 1
                fn(eng[q]).then_inc(T.sem["q" + q], 1)
            tok[i] = ("q" + q, cnt[q])
        elif o["kind"] == "dma":
            tok[i] = (o["sem"], o["inc"])
            o["fn"](eng[q]).then_inc(T.sem[o["sem"]], 16)
        else:
            folds = []
            for m in o["msg"]:
                dst = T.cores[(rank + MSG[m][3]) % n]
                for chain, lo, hi in route(topo, T, core, dst, m):
                    to = (chain + (dst,))[0]
                    rid, pid = topo.addr(to, core)
                    mk = share(topo, T, core, to, m)
                    srcs = [view(T, s, lo, hi) for s in MSG[m][0]]
                    if len(srcs) == 1:
                        g.remote_dma(view(T, MSG[m][1], lo, hi), srcs[0], T.sem[m], T.sem.lsem, pid, rid, mk)
                    else:
                        folds.append(RemoteDMATransfer(dst_ids=[DstId(rid=rid, pnc=pid)], dma_engine_mask=mk, remote_sem=T.sem[m],
                                                       srcs=srcs, dsts=[view(T, MSG[m][1], lo, hi)], alu_op=2))
                    sent += bits(mk)
            if folds:
                g.remote_dma_fused(folds, local_sem=T.sem.lsem)
            continue
        snaps[tok[i]] = dict(known[q])
    g.wait_ge(T.sem.st, 16)
    g.wait_ge(T.sem.lsem, sent)
    for q in "vspg":
        g.wait_ge(T.sem["q" + q], cnt[q])
